import numpy as np
import ml_dtypes


def mxq(x, axis, fmt="e4m3"):
    dtype, down = {"e4m3": (ml_dtypes.float8_e4m3fn, 7), "e5m2": (ml_dtypes.float8_e5m2, 14)}[fmt]
    v = np.moveaxis(np.asarray(x, np.float32).astype(ml_dtypes.bfloat16).astype(np.float64), axis, -1)
    blocks = v.reshape(v.shape[:-1] + (-1, 32))
    amax = np.abs(blocks).max(-1, keepdims=True)
    byte = np.maximum(np.where(amax > 0, np.frexp(amax)[1] - 1 + 127, 0) - down, 1)
    scale = np.exp2(byte - 127.0)
    codes = (blocks / scale).astype(np.float32).astype(dtype).astype(np.float64)
    return np.moveaxis((codes * scale).reshape(v.shape), -1, axis)


WIDE = False


def mx_kscale(k):
    if not WIDE:
        return np.ones(k)
    levels = np.array([10, -10, 5, -5, 0])
    if k % 512:
        return np.exp2(np.random.permutation(np.resize(levels, k // 32))).repeat(32)
    a = np.empty((k // 512, 16))
    for p in range(k // 512):
        a[p, :8] = np.random.permutation(np.resize(levels, 8))
        for g in range(8):
            far = levels[np.abs(levels - a[p, g]) >= 10]
            a[p, g + 8] = far[np.random.randint(len(far))]
    return np.exp2(a.ravel()).repeat(32)


def f64(x):
    return np.asarray(x).astype(np.float64)


def striped(idx):
    return np.tile(idx.reshape(-1, 16).T, (8, 1)).astype(np.uint16)


def unstriped(offs):
    return offs[:16].T.reshape(-1).astype(np.int64)


E2M1 = np.array([0.0, 0.5, 1.0, 1.5, 2.0, 3.0, 4.0, 6.0, -0.0, -0.5, -1.0, -1.5, -2.0, -3.0, -4.0, -6.0])


def pack_weight(w, fmt):
    k, n = w.shape
    w = f64(np.asarray(w, np.float32).astype(ml_dtypes.bfloat16)).reshape(k // 32, 32, n)
    amax = np.abs(w).max(1)
    if fmt == "e4m3":
        byte = np.frexp(amax)[1] - 1 + 127 - 7
    else:
        mant, ex = np.frexp(amax / 6.0)
        byte = np.where(mant > 0.5, ex, ex - 1) + 127
    byte = np.clip(np.where(amax > 0, byte, 1), 1, 254)
    scaled = (w * np.exp2(127.0 - byte)[:, None, :]).reshape(k, n).astype(np.float32)
    by_word = np.ascontiguousarray(scaled.reshape(k // 512, 128, 4, n).transpose(0, 1, 3, 2))
    if fmt == "e4m3":
        words = by_word.astype(ml_dtypes.float8_e4m3fn).view(np.uint8)
    else:
        c = by_word.astype(ml_dtypes.float4_e2m1fn).view(np.uint8) & 0xF
        words = (c[..., 0::2] | (c[..., 1::2] << 4)).reshape(k // 512, 128, 2 * n)
    return np.ascontiguousarray(words), np.ascontiguousarray(byte.astype(np.uint8).reshape(k // 512, 16, n))


def unpack_weight(words, scales, fmt):
    g, _, n = scales.shape
    words = np.ascontiguousarray(words).reshape(g, 128, n, -1)
    if fmt == "e4m3":
        vals = words.view(ml_dtypes.float8_e4m3fn).astype(np.float64)
    else:
        nib = np.empty((g, 128, n, 4), np.uint8)
        nib[..., 0::2] = words & 0xF
        nib[..., 1::2] = words >> 4
        vals = E2M1[nib]
    vals = vals * np.repeat(np.exp2(scales.astype(np.float64) - 127.0), 8, axis=1)[..., None]
    return vals.transpose(0, 1, 3, 2).reshape(g * 512, n)


def gelu(v):
    return 0.5 * v * (1.0 + np.tanh(np.sqrt(2.0 / np.pi) * (v + 0.044715 * v**3)))


def striped8(idx):
    return np.concatenate([v.reshape(-1, 16).T for v in idx]).astype(np.uint16)


def unstriped8(offs):
    return np.stack([offs[16 * g:16 * g + 16].T.reshape(-1) for g in range(8)]).astype(np.int64)


def put_heads(h, wgs, idx8, t2):
    r = np.arange(h.shape[0])
    page = np.zeros((h.shape[0], t2))
    page[r[:, None], idx8[r % 512 // 64]] = wgs[r // 4 % 128] * h
    return page


K, T, S, H, T2, N = 1024, 2048, 512, 1024, 1024, 384

def setup_inputs():
    n = np.random.standard_normal
    s = mx_kscale(K)[:, None]
    u = mx_kscale(H)[:, None]
    tab_words, tab_scales = pack_weight(n((K, T)) * s, "e4m3")
    w2_words, w2_scales = pack_weight(n((K, H)) / np.sqrt(K) / s, "e2m1")
    w4_words, w4_scales = pack_weight(1.5 * n((H, N)) / np.sqrt(H) / u, "e4m3")
    return {
        "tab_words": tab_words, "tab_scales": tab_scales,
        "offs": striped(np.random.permutation(T)[:S]),
        "w1": (1.5 * n((K, H)) / np.sqrt(K) / s * u.T).astype(np.float32),
        "w2_words": w2_words, "w2_scales": w2_scales,
        "offs2": striped8(np.stack([np.random.permutation(T2)[:S] for _ in range(8)])),
        "wgs": np.repeat(np.random.uniform(0.5, 2.0, (8, S)), 16, axis=0).astype(np.float32),
        "clim": (0.7 * n((H, T2)) * u).astype(np.float32),
        "w3": (1.5 * n((H, N)) / np.sqrt(H) / u).astype(np.float32),
        "w4_words": w4_words, "w4_scales": w4_scales,
    }

def reference(tab_words, tab_scales, offs, w1, w2_words, w2_scales, offs2, wgs, clim, w3, w4_words, w4_scales):
    v = unpack_weight(tab_words, tab_scales, "e4m3")[:, unstriped(offs)]
    w2 = unpack_weight(w2_words, w2_scales, "e2m1")
    w4 = unpack_weight(w4_words, w4_scales, "e4m3")
    a = mxq(f64(w1), 0, "e4m3").T @ v
    b = w2.T @ v
    h = a / (1.0 + np.abs(b))
    page = put_heads(h, f64(wgs), unstriped8(offs2), T2)
    z = page + f64(clim)
    zq = mxq(z, 0, "e4m3")
    vol = mxq(f64(w3), 0, "e4m3").T @ zq
    gate = w4.T @ zq
    return vol / (1.0 + np.exp(-gate))

@@ -1,0 +1,323 @@
+from contextlib import ExitStack
+
+import concourse.mybir as mybir
+from concourse.masks import make_identity
+
+K, T, S, H, T2, N = 1024, 2048, 512, 1024, 1024, 384
+FLOPS = 2 * (2 * K * H * S + 2 * H * N * T2)
+
+F32 = mybir.dt.float32
+BF16 = mybir.dt.bfloat16
+I32 = mybir.dt.int32
+U32 = mybir.dt.uint32
+U16 = mybir.dt.uint16
+U8 = mybir.dt.uint8
+FP8X4 = mybir.dt.float8_e4m3fn_x4
+FP4X4 = mybir.dt.float4_e2m1fn_x4
+ACT = mybir.ActivationFunctionType
+MULT = mybir.AluOpType.mult
+
+P = 128
+PASSES = 2
+PLANES = 8
+PAGES = 4
+CHUNK = 256
+CHUNKS = T2 // CHUNK
+BANK = 512
+
+
+def tile_list_wind_bid_pages_kernel(tc, tab_words, tab_scales, offs, w1, w2_words, w2_scales, offs2, wgs,
+                                              clim, w3, w4_words, w4_scales, out):
+    nc = tc.nc
+    with ExitStack() as ctx:
+        keep = ctx.enter_context(tc.tile_pool(name="keep", bufs=1))
+        ring = ctx.enter_context(tc.tile_pool(name="ring", bufs=2))
+        psum = ctx.enter_context(tc.psum_pool(name="psum", bufs=1))
+
+        def held(name, shape, dtype):
+            return keep.tile(shape, dtype, name=name, align_bytes=64)
+
+        def bank(number):
+            return psum.tile([P, BANK], F32, name="bank%d" % number, tag="bank%d" % number)
+
+        def load_scales(tile, src, width):
+            view = tile[:].bitcast(I32).rearrange("p (a c) -> p a c", a=PASSES)
+            for q in range(4):
+                nc.sync.dma_start(out=view[32 * q:32 * q + 4],
+                                  in_=src[:, 4 * q:4 * q + 4, :].bitcast(I32).rearrange("a r c -> r a c"))
+
+        list1 = keep.tile([P, S // 16], U16, name="list1")
+        list2 = keep.tile([P, S // 16], U16, name="list2")
+        tab_s = held("tab_s", [P, PASSES * T], U8)
+        w2_s_raw = held("w2_s_raw", [P, PASSES * H], U8)
+        w4_s = held("w4_s", [P, PASSES * N], U8)
+        for tile in (tab_s, w2_s_raw, w4_s):
+            nc.vector.memset(tile[:].bitcast(I32), 0)
+        pages = [held("page%d" % n, [P, T2], F32) for n in range(PAGES)]
+        for tile in pages:
+            nc.vector.memset(tile[:].bitcast(I32), 0)
+        ident = held("ident", [P, P], F32)
+        make_identity(nc, ident[:])
+        warm = held("warm", [P, 16], F32)
+        nc.scalar.activation(out=warm[:, 0:1], in_=ident[:, 0:1], func=ACT.Abs_reciprocal_sqrt, bias=1.0)
+
+        tab_w = [held("tab_w%d" % a, [P, T], U32) for a in range(PASSES)]
+        w2_w_raw = held("w2_w_raw", [P, PASSES * 2 * H], U8)
+        w1_raw = {}
+        wgs_t = held("wgs_t", [P, S], F32)
+        clim_t = [held("clim%d" % b, [P, 4, T2], F32) for b in range(PASSES)]
+        w3_raw = [held("w3_raw%d" % b, [P, 4, N], F32) for b in range(PASSES)]
+        w4_w = held("w4_w", [P, PASSES * N], U32)
+
+        def load_tab(a):
+            nc.sync.dma_start(out=tab_w[a][:].bitcast(I32),
+                              in_=tab_words[a].rearrange("p t i -> p (t i)").bitcast(I32))
+
+        def load_w1(a, b):
+            w1_raw[a, b] = held("w1_raw%d%d" % (a, b), [P, 4, 512], F32)
+            nc.sync.dma_start(out=w1_raw[a, b][:],
+                              in_=w1[512 * a:512 * a + 512, 512 * b:512 * b + 512].rearrange("(p j) c -> p j c", j=4))
+
+        def load_rows(tile, src, b):
+            nc.sync.dma_start(out=tile[:], in_=src[512 * b:512 * b + 512, :].rearrange("(p j) c -> p j c", j=4))
+
+        nc.sync.dma_start(list1[:], offs)
+        load_tab(0)
+        load_scales(tab_s, tab_scales, T)
+        nc.sync.dma_start(out=w2_w_raw[:].bitcast(I32).rearrange("p (a c) -> p a c", a=PASSES),
+                          in_=w2_words.bitcast(I32).rearrange("a p c -> p a c"))
+        load_tab(1)
+        load_scales(w2_s_raw, w2_scales, H)
+        load_w1(0, 0)
+        load_w1(1, 0)
+        nc.sync.dma_start(out=wgs_t[:], in_=wgs)
+        nc.sync.dma_start(list2[:], offs2)
+        load_w1(0, 1)
+        load_w1(1, 1)
+        load_rows(clim_t[0], clim, 0)
+        load_rows(w3_raw[0], w3, 0)
+        load_rows(w3_raw[1], w3, 1)
+        nc.sync.dma_start(out=w4_w[:].bitcast(I32).rearrange("p (a c) -> p a c", a=PASSES),
+                          in_=w4_words.rearrange("a p c i -> p a (c i)").bitcast(I32))
+        load_scales(w4_s, w4_scales, N)
+        load_rows(clim_t[1], clim, 1)
+
+        v_w = [held("v_w%d" % a, [P, S], U32) for a in range(PASSES)]
+        v_s = [held("v_s%d" % a, [P, S], U8) for a in range(PASSES)]
+        w2_w = [held("w2_w%d" % b, [P, PASSES * 2 * 512], U8) for b in range(PASSES)]
+        w2_s = [held("w2_s%d" % b, [P, PASSES * 512], U8) for b in range(PASSES)]
+
+        def order_w2(b):
+            nc.vector.tensor_copy(
+                out=w2_w[b][:].bitcast(U16).rearrange("p (a t m) -> p a t m", a=PASSES, t=4),
+                in_=w2_w_raw[:].bitcast(U16).rearrange("p (a b m t) -> p b a t m", a=PASSES, b=PASSES, t=4)[:, b])
+            nc.vector.tensor_copy(
+                out=w2_s[b][:].rearrange("p (a t m) -> p a t m", a=PASSES, t=4),
+                in_=w2_s_raw[:].rearrange("p (a b m t) -> p b a t m", a=PASSES, b=PASSES, t=4)[:, b])
+
+        for a in range(PASSES):
+            nc.vector.tensor_copy(out=v_s[a][:], in_=tab_s[:, a * T:(a + 1) * T].indirect(list1[:]))
+        nc.vector.tensor_copy(out=v_w[0][:], in_=tab_w[0][:].indirect(list1[:]))
+        order_w2(0)
+        nc.vector.tensor_copy(out=v_w[1][:], in_=tab_w[1][:].indirect(list1[:]))
+
+        w1_w, w1_s, w1_bf = {}, {}, {}
+
+        def round_w1(a, b, copy):
+            w1_bf[a, b] = held("w1_bf%d" % a, [P, 2048], BF16)
+            copy(out=w1_bf[a, b][:].rearrange("p (t m j) -> p m j t", t=4, j=4),
+                 in_=w1_raw[a, b][:].rearrange("p j (m t) -> p m j t", t=4))
+
+        def quantize_w1(a, b):
+            w1_w[a, b] = held("w1_w%d%d" % (a, b), [P, 512], U32)
+            w1_s[a, b] = held("w1_s%d%d" % (a, b), [P, 512], U8)
+            nc.vector.quantize_mx(out=w1_w[a, b][:].bitcast(FP8X4), scales=w1_s[a, b][:], in_=w1_bf[a, b][:])
+
+        damp, weighted = {}, {}
+        behind = {3: "w1_bf1", 7: "z_bf3"}
+
+        def damping(n):
+            b, t = divmod(n, 4)
+            acc = bank(n % 2)
+            for a in range(PASSES):
+                c0 = a * 512 + t * P
+                nc.tensor.matmul_mx(out=acc[:], lhsT=w2_w[b][:, 2 * c0:2 * c0 + 2 * P].bitcast(FP4X4),
+                                    lhsT_scale=w2_s[b][:, c0:c0 + P], rhs=v_w[a][:].bitcast(FP8X4),
+                                    rhs_scale=v_s[a][:], start=(a == 0), stop=(a == PASSES - 1))
+            size = ring.tile([P, S], F32, name="size")
+            nc.scalar.activation(out=size[:], in_=acc[:], func=ACT.Abs)
+            root = ring.tile([P, S], F32, name="root")
+            nc.scalar.activation(out=root[:], in_=size[:], func=ACT.Abs_reciprocal_sqrt, bias=1.0)
+            damp[n] = held("damp%d" % n, [P, S], F32)
+            nc.scalar.activation(out=damp[n][:], in_=root[:], func=ACT.Square)
+
+        def weigh(n):
+            b, t = divmod(n, 4)
+            acc = bank(2 + n % 2)
+            for a in range(PASSES):
+                cols = slice(t * P, (t + 1) * P)
+                nc.tensor.matmul_mx(out=acc[:], lhsT=w1_w[a, b][:, cols].bitcast(FP8X4),
+                                    lhsT_scale=w1_s[a, b][:, cols], rhs=v_w[a][:].bitcast(FP8X4),
+                                    rhs_scale=v_s[a][:], start=(a == 0), stop=(a == PASSES - 1))
+            if n in behind:
+                weighted[n] = held(behind[n], [P, S], F32)
+            else:
+                weighted[n] = ring.tile([P, S], F32, name="weighted")
+            nc.vector.tensor_tensor(out=weighted[n][:], in0=acc[:], in1=wgs_t[:], op=MULT)
+
+        def scatter(n):
+            nc.vector.tensor_tensor(out=pages[n % PAGES][:].indirect(list2[:]), in0=weighted[n][:],
+                                    in1=damp[n][:], op=MULT)
+
+        sums, pairs = {}, {}
+
+        def add_t(b, u, c, e, src, first, last):
+            for g in range(2):
+                m0 = c * CHUNK + g * P
+                o0 = (2 * g + e) * P
+                nc.tensor.matmul(out=sums[b, u, c][:, o0:o0 + P], lhsT=src[:, m0:m0 + P], rhs=ident[:],
+                                 is_transpose=True, start=(first and g == 0), stop=(last and g == 1))
+
+        def open_sum(b, u, c, number):
+            sums[b, u, c] = bank(number)
+            add_t(b, u, c, 0, clim_t[b][:, 2 * u, :], True, False)
+            add_t(b, u, c, 1, clim_t[b][:, 2 * u + 1, :], False, False)
+            add_t(b, u, c, 0, pages[(4 * b + 2 * u) % PAGES], False, False)
+
+        def close_sum(b, u, c):
+            add_t(b, u, c, 1, pages[(4 * b + 2 * u + 1) % PAGES], False, True)
+
+        def round_sum(b, u, c, copy):
+            pairs[b, u, c] = held("pairs%d%d" % (u, c), [P, 512], BF16)
+            copy(out=pairs[b, u, c][:].rearrange("m (g p e) -> m g p e", g=2, e=2),
+                 in_=sums[b, u, c][:].rearrange("m (g e p) -> m g p e", g=2, e=2))
+
+        z_w = {(b, h): held("z_w%d%d" % (b, h), [P, 512], U32) for b in range(PASSES) for h in range(2)}
+        z_s = {(b, h): held("z_s%d%d" % (b, h), [P, 512], U8) for b in range(PASSES) for h in range(2)}
+        z_bf = {}
+
+        def turn_back(b, c, number, copy):
+            back = bank(number)
+            for g in range(2):
+                for u in range(2):
+                    o0 = (2 * g + u) * P
+                    nc.tensor.transpose(back[:, o0:o0 + P], pairs[b, u, c][:].bitcast(F32)[:, g * P:(g + 1) * P],
+                                        ident[:])
+            z_bf[b, c] = held("z_bf%d" % c, [P, 4 * CHUNK], BF16)
+            copy(out=z_bf[b, c][:].bitcast(F32).rearrange("p (g m u) -> p g m u", g=2, u=2),
+                 in_=back[:].rearrange("p (g u m) -> p g m u", g=2, u=2))
+
+        def quantize_z(b, c):
+            h, half = divmod(c, 2)
+            cols = slice(half * CHUNK, (half + 1) * CHUNK)
+            nc.vector.quantize_mx(out=z_w[b, h][:, cols].bitcast(FP8X4), scales=z_s[b, h][:, cols],
+                                  in_=z_bf[b, c][:])
+
+        def sum_pair(b, u):
+            for c in range(CHUNKS):
+                open_sum(b, u, c, 4 + c % 2)
+                close_sum(b, u, c)
+                round_sum(b, u, c, nc.scalar.copy)
+
+        w3_bf = held("w3_bf", [P, PASSES * 4 * N], BF16)
+        w3_w = held("w3_w", [P, PASSES * N], U32)
+        w3_s = held("w3_s", [P, PASSES * N], U8)
+
+        def round_w3(b):
+            nc.scalar.copy(out=w3_bf[:, b * 4 * N:(b + 1) * 4 * N].rearrange("p (c i j) -> p c j i", i=4, j=4),
+                           in_=w3_raw[b][:].rearrange("p j (c i) -> p c j i", i=4))
+
+        def quantize_w3():
+            for c0, c1 in ((0, 512), (512, 768)):
+                nc.vector.quantize_mx(out=w3_w[:, c0:c1].bitcast(FP8X4), scales=w3_s[:, c0:c1],
+                                      in_=w3_bf[:, 4 * c0:4 * c1])
+
+        def product(acc, words, scales, nt, h, b):
+            cols = slice(b * N + nt * P, b * N + (nt + 1) * P)
+            nc.tensor.matmul_mx(out=acc[:], lhsT=words[:, cols].bitcast(FP8X4), lhsT_scale=scales[:, cols],
+                                rhs=z_w[b, h][:].bitcast(FP8X4), rhs_scale=z_s[b, h][:],
+                                start=(b == 0), stop=(b == PASSES - 1))
+
+        round_w1(0, 0, nc.scalar.copy)
+        damping(0)
+        quantize_w1(0, 0)
+        round_w1(1, 0, nc.vector.tensor_copy)
+        quantize_w1(1, 0)
+        weigh(0)
+        scatter(0)
+        order_w2(1)
+        damping(1)
+        weigh(1)
+        scatter(1)
+        damping(2)
+        round_w1(0, 1, nc.scalar.copy)
+        round_w1(1, 1, nc.scalar.copy)
+        weigh(2)
+        quantize_w1(0, 1)
+        quantize_w1(1, 1)
+        scatter(2)
+        damping(3)
+        weigh(3)
+        scatter(3)
+        damping(4)
+        sum_pair(0, 0)
+        weigh(4)
+        damping(5)
+        damping(6)
+        round_w3(0)
+        round_w3(1)
+        sum_pair(0, 1)
+        scatter(4)
+        quantize_w3()
+        weigh(5)
+        scatter(5)
+        damping(7)
+        nc.scalar.activation(out=warm[:, 8:9], in_=damp[7][:, 0:1], func=ACT.Sigmoid)
+        for c in range(CHUNKS):
+            turn_back(0, c, 6 + c % 2, nc.scalar.copy)
+            quantize_z(0, c)
+        weigh(6)
+        sum_pair(1, 0)
+        scatter(6)
+        weigh(7)
+        scatter(7)
+
+        sum_banks = (0, 1, 4, 5)
+        for c in range(CHUNKS):
+            open_sum(1, 1, c, sum_banks[c])
+        tiles = [(h, nt) for h in range(2) for nt in range(N // P)]
+        out_banks = ((2, 3), (0, 1), (4, 5), (6, 7), (2, 3), (0, 1))
+        accs = {}
+
+        def first_pass(i):
+            h, nt = tiles[i]
+            accs[i] = (bank(out_banks[i][0]), bank(out_banks[i][1]))
+            product(accs[i][0], w4_w, w4_s, nt, h, 0)
+            product(accs[i][1], w3_w, w3_s, nt, h, 0)
+
+        def finish(i):
+            h, nt = tiles[i]
+            product(accs[i][0], w4_w, w4_s, nt, h, 1)
+            product(accs[i][1], w3_w, w3_s, nt, h, 1)
+            gate = ring.tile([P, 512], F32, name="gate")
+            nc.scalar.activation(out=gate[:], in_=accs[i][0][:], func=ACT.Sigmoid)
+            result = ring.tile([P, 512], F32, name="result", bufs=3)
+            nc.vector.tensor_tensor(out=result[:], in0=accs[i][1][:], in1=gate[:], op=MULT)
+            nc.sync.dma_start(out=out[nt * P:(nt + 1) * P, h * 512:(h + 1) * 512], in_=result[:])
+
+        first_pass(0)
+        for c in range(CHUNKS):
+            close_sum(1, 1, c)
+        for c in range(CHUNKS):
+            copy = nc.scalar.copy if c % 2 == 0 else nc.vector.tensor_copy
+            round_sum(1, 1, c, copy)
+        for c in range(CHUNKS):
+            copy = nc.scalar.copy if c % 2 == 0 else nc.vector.tensor_copy
+            turn_back(1, c, 6 + c % 2, copy)
+            quantize_z(1, c)
+        first_pass(1)
+        first_pass(2)
+        for i in range(len(tiles)):
+            if i >= 3:
+                first_pass(i)
+            finish(i)

@@ -53,16 +53,17 @@ def tile_list_wind_bid_pages_kernel(tc, tab_words, tab_scales, offs, w1, w2_word
         w4_s = held("w4_s", [P, PASSES * N], U8)
         for tile in (tab_s, w2_s_raw, w4_s):
             nc.vector.memset(tile[:].bitcast(I32), 0)
+        ident = held("ident", [P, P], F32)
+        nc.vector.memset(ident[:], 0.0)
+        make_identity(nc, ident[:], nomemset=True)
         pages = [held("page%d" % n, [P, T2], F32) for n in range(PAGES)]
         for tile in pages:
             nc.vector.memset(tile[:].bitcast(I32), 0)
-        ident = held("ident", [P, P], F32)
-        make_identity(nc, ident[:])
         warm = held("warm", [P, 16], F32)
         nc.scalar.activation(out=warm[:, 0:1], in_=ident[:, 0:1], func=ACT.Abs_reciprocal_sqrt, bias=1.0)
 
         tab_w = [held("tab_w%d" % a, [P, T], U32) for a in range(PASSES)]
-        w2_w_raw = held("w2_w_raw", [P, PASSES * 2 * H], U8)
+        w2_w = [held("w2_w%d" % b, [P, PASSES * 1024], U8) for b in range(PASSES)]
         w1_raw = {}
         wgs_t = held("wgs_t", [P, S], F32)
         clim_t = [held("clim%d" % b, [P, 4, T2], F32) for b in range(PASSES)]
@@ -73,10 +74,17 @@ def tile_list_wind_bid_pages_kernel(tc, tab_words, tab_scales, offs, w1, w2_word
             nc.sync.dma_start(out=tab_w[a][:].bitcast(I32),
                               in_=tab_words[a].rearrange("p t i -> p (t i)").bitcast(I32))
 
-        def load_w1(a, b):
-            w1_raw[a, b] = held("w1_raw%d%d" % (a, b), [P, 4, 512], F32)
-            nc.sync.dma_start(out=w1_raw[a, b][:],
-                              in_=w1[512 * a:512 * a + 512, 512 * b:512 * b + 512].rearrange("(p j) c -> p j c", j=4))
+        def load_w1(a, b, parts=1):
+            width = 512 // parts
+            w1_raw[a, b] = [held("w1_raw%d%d%d" % (a, b, part), [P, 4, width], F32) for part in range(parts)]
+            for part, raw in enumerate(w1_raw[a, b]):
+                c0 = 512 * b + part * width
+                nc.sync.dma_start(out=raw[:],
+                                  in_=w1[512 * a:512 * a + 512, c0:c0 + width].rearrange("(p j) c -> p j c", j=4))
+
+        def load_w2(b):
+            nc.sync.dma_start(out=w2_w[b][:].bitcast(I32).rearrange("p (a c) -> p a c", a=PASSES),
+                              in_=w2_words[:, :, 1024 * b:1024 * b + 1024].bitcast(I32).rearrange("a p c -> p a c"))
 
         def load_rows(tile, src, b):
             nc.sync.dma_start(out=tile[:], in_=src[512 * b:512 * b + 512, :].rearrange("(p j) c -> p j c", j=4))
@@ -84,16 +92,16 @@ def tile_list_wind_bid_pages_kernel(tc, tab_words, tab_scales, offs, w1, w2_word
         nc.sync.dma_start(list1[:], offs)
         load_tab(0)
         load_scales(tab_s, tab_scales, T)
-        nc.sync.dma_start(out=w2_w_raw[:].bitcast(I32).rearrange("p (a c) -> p a c", a=PASSES),
-                          in_=w2_words.bitcast(I32).rearrange("a p c -> p a c"))
+        load_w2(0)
         load_tab(1)
         load_scales(w2_s_raw, w2_scales, H)
         load_w1(0, 0)
-        load_w1(1, 0)
+        load_w1(1, 0, parts=2)
         nc.sync.dma_start(out=wgs_t[:], in_=wgs)
         nc.sync.dma_start(list2[:], offs2)
         load_w1(0, 1)
         load_w1(1, 1)
+        load_w2(1)
         load_rows(clim_t[0], clim, 0)
         load_rows(w3_raw[0], w3, 0)
         load_rows(w3_raw[1], w3, 1)
@@ -104,52 +112,58 @@ def tile_list_wind_bid_pages_kernel(tc, tab_words, tab_scales, offs, w1, w2_word
 
         v_w = [held("v_w%d" % a, [P, S], U32) for a in range(PASSES)]
         v_s = [held("v_s%d" % a, [P, S], U8) for a in range(PASSES)]
-        w2_w = [held("w2_w%d" % b, [P, PASSES * 2 * 512], U8) for b in range(PASSES)]
-        w2_s = [held("w2_s%d" % b, [P, PASSES * 512], U8) for b in range(PASSES)]
-
-        def order_w2(b):
-            nc.vector.tensor_copy(
-                out=w2_w[b][:].bitcast(U16).rearrange("p (a t m) -> p a t m", a=PASSES, t=4),
-                in_=w2_w_raw[:].bitcast(U16).rearrange("p (a b m t) -> p b a t m", a=PASSES, b=PASSES, t=4)[:, b])
-            nc.vector.tensor_copy(
-                out=w2_s[b][:].rearrange("p (a t m) -> p a t m", a=PASSES, t=4),
-                in_=w2_s_raw[:].rearrange("p (a b m t) -> p b a t m", a=PASSES, b=PASSES, t=4)[:, b])
 
         for a in range(PASSES):
             nc.vector.tensor_copy(out=v_s[a][:], in_=tab_s[:, a * T:(a + 1) * T].indirect(list1[:]))
         nc.vector.tensor_copy(out=v_w[0][:], in_=tab_w[0][:].indirect(list1[:]))
-        order_w2(0)
         nc.vector.tensor_copy(out=v_w[1][:], in_=tab_w[1][:].indirect(list1[:]))
 
         w1_w, w1_s, w1_bf = {}, {}, {}
 
         def round_w1(a, b, copy):
-            w1_bf[a, b] = held("w1_bf%d" % a, [P, 2048], BF16)
-            copy(out=w1_bf[a, b][:].rearrange("p (t m j) -> p m j t", t=4, j=4),
-                 in_=w1_raw[a, b][:].rearrange("p j (m t) -> p m j t", t=4))
+            w1_bf[a, b] = held("root2" if (a, b) == (0, 1) else "w1_bf%d" % a, [P, 2048], BF16)
+            rounded = w1_bf[a, b][:].rearrange("p (t m j) -> p m j t", t=4, j=4)
+            parts = len(w1_raw[a, b])
+            for part, raw in enumerate(w1_raw[a, b]):
+                copy(out=rounded[:, part * P // parts:(part + 1) * P // parts],
+                     in_=raw[:].rearrange("p j (m t) -> p m j t", t=4))
 
-        def quantize_w1(a, b):
+        def quantize_w1(a, b, cuts=(0, 512)):
             w1_w[a, b] = held("w1_w%d%d" % (a, b), [P, 512], U32)
             w1_s[a, b] = held("w1_s%d%d" % (a, b), [P, 512], U8)
-            nc.vector.quantize_mx(out=w1_w[a, b][:].bitcast(FP8X4), scales=w1_s[a, b][:], in_=w1_bf[a, b][:])
+            for c0, c1 in zip(cuts, cuts[1:]):
+                nc.vector.quantize_mx(out=w1_w[a, b][:, c0:c1].bitcast(FP8X4), scales=w1_s[a, b][:, c0:c1],
+                                      in_=w1_bf[a, b][:, 4 * c0:4 * c1])
 
         damp, weighted = {}, {}
-        behind = {3: "w1_bf1", 7: "z_bf3"}
+        behind = {3: "w1_bf1", 6: "w3_bf", 7: "z_bf3"}
+
+        size = {}
+
+        def spread(b):
+            accs = [bank(4 + jb) for jb in range(4)]
+            for a in range(PASSES):
+                c0 = a * H + b * 512
+                for jb in range(4):
+                    cols = slice(jb * P, (jb + 1) * P)
+                    nc.tensor.matmul_mx(out=accs[jb][:], lhsT=v_w[a][:, cols].bitcast(FP8X4),
+                                        lhsT_scale=v_s[a][:, cols],
+                                        rhs=w2_w[b][:, 1024 * a:1024 * a + 1024].bitcast(FP4X4),
+                                        rhs_scale=w2_s_raw[:, c0:c0 + 512], start=(a == 0), stop=(a == PASSES - 1))
+            size[b] = held("size", [P, 4, 4, P], F32)
+            for jb in range(4):
+                nc.scalar.activation(out=size[b][:, jb], in_=accs[jb][:].rearrange("j (p t) -> j t p", t=4),
+                                     func=ACT.Abs)
 
         def damping(n):
             b, t = divmod(n, 4)
-            acc = bank(n % 2)
-            for a in range(PASSES):
-                c0 = a * 512 + t * P
-                nc.tensor.matmul_mx(out=acc[:], lhsT=w2_w[b][:, 2 * c0:2 * c0 + 2 * P].bitcast(FP4X4),
-                                    lhsT_scale=w2_s[b][:, c0:c0 + P], rhs=v_w[a][:].bitcast(FP8X4),
-                                    rhs_scale=v_s[a][:], start=(a == 0), stop=(a == PASSES - 1))
-            size = ring.tile([P, S], F32, name="size")
-            nc.scalar.activation(out=size[:], in_=acc[:], func=ACT.Abs)
-            root = ring.tile([P, S], F32, name="root")
-            nc.scalar.activation(out=root[:], in_=size[:], func=ACT.Abs_reciprocal_sqrt, bias=1.0)
+            root = held("root%d" % (2, 1, 1, 0, 1, 0, 1, 0)[n], [P, 4, P], F32)
+            nc.scalar.activation(out=root[:], in_=size[b][:, :, t, :], func=ACT.Abs_reciprocal_sqrt, bias=1.0)
+            acc = bank(2 if n == 1 else n % 2)
+            for jb in range(4):
+                nc.tensor.transpose(acc[:, jb * P:(jb + 1) * P], root[:, jb, :], ident[:])
             damp[n] = held("damp%d" % n, [P, S], F32)
-            nc.scalar.activation(out=damp[n][:], in_=root[:], func=ACT.Square)
+            nc.scalar.activation(out=damp[n][:], in_=acc[:], func=ACT.Square)
 
         def weigh(n):
             b, t = divmod(n, 4)
@@ -232,20 +246,14 @@ def tile_list_wind_bid_pages_kernel(tc, tab_words, tab_scales, offs, w1, w2_word
                 nc.vector.quantize_mx(out=w3_w[:, c0:c1].bitcast(FP8X4), scales=w3_s[:, c0:c1],
                                       in_=w3_bf[:, 4 * c0:4 * c1])
 
-        def product(acc, words, scales, nt, h, b):
-            cols = slice(b * N + nt * P, b * N + (nt + 1) * P)
-            nc.tensor.matmul_mx(out=acc[:], lhsT=words[:, cols].bitcast(FP8X4), lhsT_scale=scales[:, cols],
-                                rhs=z_w[b, h][:].bitcast(FP8X4), rhs_scale=z_s[b, h][:],
-                                start=(b == 0), stop=(b == PASSES - 1))
-
-        round_w1(0, 0, nc.scalar.copy)
+        spread(0)
         damping(0)
+        round_w1(0, 0, nc.vector.tensor_copy)
         quantize_w1(0, 0)
         round_w1(1, 0, nc.vector.tensor_copy)
-        quantize_w1(1, 0)
+        quantize_w1(1, 0, cuts=(0, 128, 256, 512))
         weigh(0)
         scatter(0)
-        order_w2(1)
         damping(1)
         weigh(1)
         scatter(1)
@@ -259,6 +267,7 @@ def tile_list_wind_bid_pages_kernel(tc, tab_words, tab_scales, offs, w1, w2_word
         damping(3)
         weigh(3)
         scatter(3)
+        spread(1)
         damping(4)
         sum_pair(0, 0)
         weigh(4)
@@ -282,28 +291,42 @@ def tile_list_wind_bid_pages_kernel(tc, tab_words, tab_scales, offs, w1, w2_word
         weigh(7)
         scatter(7)
 
-        sum_banks = (0, 1, 4, 5)
+        sum_banks = (0, 1, 6, 7)
         for c in range(CHUNKS):
             open_sum(1, 1, c, sum_banks[c])
-        tiles = [(h, nt) for h in range(2) for nt in range(N // P)]
-        out_banks = ((2, 3), (0, 1), (4, 5), (6, 7), (2, 3), (0, 1))
+        pieces = [(nt, 0, 512) for nt in range(3)] + [(0, 512, 512), (1, 512, 512), (2, 512, 256), (2, 768, 256)]
+        out_banks = ((2, 3), (0, 1), (6, 7), (4, 5), (2, 3), (0, 1), (6, 7))
         accs = {}
 
+        def product(i, which, b):
+            nt, m0, width = pieces[i]
+            words, scales = ((w4_w, w4_s), (w3_w, w3_s))[which]
+            cols = slice(b * N + nt * P, b * N + (nt + 1) * P)
+            h, c0 = divmod(m0, 512)
+            nc.tensor.matmul_mx(out=accs[i][which][:, 0:width], lhsT=words[:, cols].bitcast(FP8X4),
+                                lhsT_scale=scales[:, cols], rhs=z_w[b, h][:, c0:c0 + width].bitcast(FP8X4),
+                                rhs_scale=z_s[b, h][:, c0:c0 + width], start=(b == 0), stop=(b == PASSES - 1))
+
         def first_pass(i):
-            h, nt = tiles[i]
             accs[i] = (bank(out_banks[i][0]), bank(out_banks[i][1]))
-            product(accs[i][0], w4_w, w4_s, nt, h, 0)
-            product(accs[i][1], w3_w, w3_s, nt, h, 0)
+            product(i, 0, 0)
+            product(i, 1, 0)
 
         def finish(i):
-            h, nt = tiles[i]
-            product(accs[i][0], w4_w, w4_s, nt, h, 1)
-            product(accs[i][1], w3_w, w3_s, nt, h, 1)
-            gate = ring.tile([P, 512], F32, name="gate")
-            nc.scalar.activation(out=gate[:], in_=accs[i][0][:], func=ACT.Sigmoid)
-            result = ring.tile([P, 512], F32, name="result", bufs=3)
-            nc.vector.tensor_tensor(out=result[:], in0=accs[i][1][:], in1=gate[:], op=MULT)
-            nc.sync.dma_start(out=out[nt * P:(nt + 1) * P, h * 512:(h + 1) * 512], in_=result[:])
+            nt, m0, width = pieces[i]
+            if i not in accs:
+                accs[i] = (bank(out_banks[i][0]), bank(out_banks[i][1]))
+                product(i, 0, 0)
+                product(i, 0, 1)
+                product(i, 1, 0)
+            else:
+                product(i, 0, 1)
+            product(i, 1, 1)
+            gate = held("root%d" % (i % 3), [P, width], F32)
+            nc.scalar.activation(out=gate[:], in_=accs[i][0][:, 0:width], func=ACT.Sigmoid)
+            result = held("damp%d" % i, [P, width], F32)
+            nc.vector.tensor_tensor(out=result[:], in0=accs[i][1][:, 0:width], in1=gate[:], op=MULT)
+            nc.sync.dma_start(out=out[nt * P:(nt + 1) * P, m0:m0 + width], in_=result[:])
 
         first_pass(0)
         for c in range(CHUNKS):
@@ -313,11 +336,9 @@ def tile_list_wind_bid_pages_kernel(tc, tab_words, tab_scales, offs, w1, w2_word
             round_sum(1, 1, c, copy)
         for c in range(CHUNKS):
             copy = nc.scalar.copy if c % 2 == 0 else nc.vector.tensor_copy
-            turn_back(1, c, 6 + c % 2, copy)
+            turn_back(1, c, 4 + c % 2, copy)
             quantize_z(1, c)
         first_pass(1)
         first_pass(2)
-        for i in range(len(tiles)):
-            if i >= 3:
-                first_pass(i)
+        for i in range(len(pieces)):
             finish(i)

@@ -16,6 +16,7 @@ FP8X4 = mybir.dt.float8_e4m3fn_x4
 FP4X4 = mybir.dt.float4_e2m1fn_x4
 ACT = mybir.ActivationFunctionType
 MULT = mybir.AluOpType.mult
+ADD = mybir.AluOpType.add
 
 P = 128
 PASSES = 2
@@ -24,6 +25,7 @@ PAGES = 4
 CHUNK = 256
 CHUNKS = T2 // CHUNK
 BANK = 512
+FOLDED = 8
 
 
 def tile_list_wind_bid_pages_kernel(tc, tab_words, tab_scales, offs, w1, w2_words, w2_scales, offs2, wgs,
@@ -31,7 +33,6 @@ def tile_list_wind_bid_pages_kernel(tc, tab_words, tab_scales, offs, w1, w2_word
     nc = tc.nc
     with ExitStack() as ctx:
         keep = ctx.enter_context(tc.tile_pool(name="keep", bufs=1))
-        ring = ctx.enter_context(tc.tile_pool(name="ring", bufs=2))
         psum = ctx.enter_context(tc.psum_pool(name="psum", bufs=1))
 
         def held(name, shape, dtype):
@@ -66,7 +67,7 @@ def tile_list_wind_bid_pages_kernel(tc, tab_words, tab_scales, offs, w1, w2_word
         w2_w = [held("w2_w%d" % b, [P, PASSES * 1024], U8) for b in range(PASSES)]
         w1_raw = {}
         wgs_t = held("wgs_t", [P, S], F32)
-        clim_t = [held("clim%d" % b, [P, 4, T2], F32) for b in range(PASSES)]
+        clim_t = {(b, u): held("clim%d%d" % (b, u), [P, 2, T2], F32) for b in range(PASSES) for u in range(2)}
         w3_raw = [held("w3_raw%d" % b, [P, 4, N], F32) for b in range(PASSES)]
         w4_w = held("w4_w", [P, PASSES * N], U32)
 
@@ -86,6 +87,11 @@ def tile_list_wind_bid_pages_kernel(tc, tab_words, tab_scales, offs, w1, w2_word
             nc.sync.dma_start(out=w2_w[b][:].bitcast(I32).rearrange("p (a c) -> p a c", a=PASSES),
                               in_=w2_words[:, :, 1024 * b:1024 * b + 1024].bitcast(I32).rearrange("a p c -> p a c"))
 
+        def load_clim(b):
+            rows = clim[512 * b:512 * b + 512, :].rearrange("(p j) c -> p j c", j=4)
+            for u in range(2):
+                nc.sync.dma_start(out=clim_t[b, u][:], in_=rows[:, 2 * u:2 * u + 2, :])
+
         def load_rows(tile, src, b):
             nc.sync.dma_start(out=tile[:], in_=src[512 * b:512 * b + 512, :].rearrange("(p j) c -> p j c", j=4))
 
@@ -99,29 +105,28 @@ def tile_list_wind_bid_pages_kernel(tc, tab_words, tab_scales, offs, w1, w2_word
         load_w1(1, 0, parts=2)
         nc.sync.dma_start(out=wgs_t[:], in_=wgs)
         nc.sync.dma_start(list2[:], offs2)
+        load_w2(1)
         load_w1(0, 1)
         load_w1(1, 1)
-        load_w2(1)
-        load_rows(clim_t[0], clim, 0)
+        load_clim(0)
         load_rows(w3_raw[0], w3, 0)
         load_rows(w3_raw[1], w3, 1)
         nc.sync.dma_start(out=w4_w[:].bitcast(I32).rearrange("p (a c) -> p a c", a=PASSES),
                           in_=w4_words.rearrange("a p c i -> p a (c i)").bitcast(I32))
         load_scales(w4_s, w4_scales, N)
-        load_rows(clim_t[1], clim, 1)
+        load_clim(1)
 
         v_w = [held("v_w%d" % a, [P, S], U32) for a in range(PASSES)]
         v_s = [held("v_s%d" % a, [P, S], U8) for a in range(PASSES)]
 
         for a in range(PASSES):
             nc.vector.tensor_copy(out=v_s[a][:], in_=tab_s[:, a * T:(a + 1) * T].indirect(list1[:]))
-        nc.vector.tensor_copy(out=v_w[0][:], in_=tab_w[0][:].indirect(list1[:]))
-        nc.vector.tensor_copy(out=v_w[1][:], in_=tab_w[1][:].indirect(list1[:]))
+            nc.vector.tensor_copy(out=v_w[a][:], in_=tab_w[a][:].indirect(list1[:]))
 
         w1_w, w1_s, w1_bf = {}, {}, {}
 
         def round_w1(a, b, copy):
-            w1_bf[a, b] = held("root2" if (a, b) == (0, 1) else "w1_bf%d" % a, [P, 2048], BF16)
+            w1_bf[a, b] = held("root3" if (a, b) == (0, 1) else "w1_bf%d" % a, [P, 2048], BF16)
             rounded = w1_bf[a, b][:].rearrange("p (t m j) -> p m j t", t=4, j=4)
             parts = len(w1_raw[a, b])
             for part, raw in enumerate(w1_raw[a, b]):
@@ -136,9 +141,8 @@ def tile_list_wind_bid_pages_kernel(tc, tab_words, tab_scales, offs, w1, w2_word
                                       in_=w1_bf[a, b][:, 4 * c0:4 * c1])
 
         damp, weighted = {}, {}
-        behind = {3: "w1_bf1", 6: "w3_bf", 7: "z_bf3"}
 
-        size = {}
+        size, spreads = {}, {}
 
         def spread(b):
             accs = [bank(4 + jb) for jb in range(4)]
@@ -150,34 +154,70 @@ def tile_list_wind_bid_pages_kernel(tc, tab_words, tab_scales, offs, w1, w2_word
                                         lhsT_scale=v_s[a][:, cols],
                                         rhs=w2_w[b][:, 1024 * a:1024 * a + 1024].bitcast(FP4X4),
                                         rhs_scale=w2_s_raw[:, c0:c0 + 512], start=(a == 0), stop=(a == PASSES - 1))
-            size[b] = held("size", [P, 4, 4, P], F32)
-            for jb in range(4):
-                nc.scalar.activation(out=size[b][:, jb], in_=accs[jb][:].rearrange("j (p t) -> j t p", t=4),
-                                     func=ACT.Abs)
+            spreads[b] = accs
 
-        def damping(n):
-            b, t = divmod(n, 4)
-            root = held("root%d" % (2, 1, 1, 0, 1, 0, 1, 0)[n], [P, 4, P], F32)
-            nc.scalar.activation(out=root[:], in_=size[b][:, :, t, :], func=ACT.Abs_reciprocal_sqrt, bias=1.0)
-            acc = bank(2 if n == 1 else n % 2)
+        def absolute(b, t0, t1, slot):
+            tile = held(slot, [P, 4, t1 - t0, P], F32)
+            for t in range(t0, t1):
+                size[t] = tile[:, :, t - t0, :]
             for jb in range(4):
-                nc.tensor.transpose(acc[:, jb * P:(jb + 1) * P], root[:, jb, :], ident[:])
+                nc.scalar.activation(out=tile[:, jb],
+                                     in_=spreads[b][jb][:].rearrange("j (p t) -> j t p", t=4)[:, t0:t1], func=ACT.Abs)
+
+
+        roots = {}
+
+        def plain_root(n, slot):
+            roots[n] = held(slot, [P, 4, P], F32)[:]
+            nc.scalar.activation(out=roots[n], in_=size[n], func=ACT.Abs_reciprocal_sqrt, bias=1.0)
+
+        def damping(n, number):
+            acc = bank(number)
+            for jb in range(4):
+                nc.tensor.transpose(acc[:, jb * P:(jb + 1) * P], roots[n][:, jb, :], ident[:])
             damp[n] = held("damp%d" % n, [P, S], F32)
             nc.scalar.activation(out=damp[n][:], in_=acc[:], func=ACT.Square)
 
-        def weigh(n):
+        ordered = {}
+
+        def order_w2():
+            w2_cols = held("w1_raw101", [P, PASSES * 1024], U8)
+            w2_s = held("w1_raw100", [P, PASSES * 512], U8)
+            ordered["words"], ordered["scales"] = w2_cols, w2_s
+            nc.vector.tensor_copy(
+                out=w2_cols[:].bitcast(U16).rearrange("p (a t m) -> p a t m", a=PASSES, t=4),
+                in_=w2_w[1][:].bitcast(U16).rearrange("p (a m t) -> p a t m", a=PASSES, t=4))
+            nc.vector.tensor_copy(
+                out=w2_s[:].rearrange("p (a t m) -> p a t m", a=PASSES, t=4),
+                in_=w2_s_raw[:].rearrange("p (a b m t) -> p b a t m", a=PASSES, b=PASSES, t=4)[:, 1])
+
+        def direct_damping(n, number, slot):
+            acc = bank(number)
+            for a in range(PASSES):
+                c0 = a * 512 + (n % 4) * P
+                nc.tensor.matmul_mx(out=acc[:], lhsT=ordered["words"][:, 2 * c0:2 * c0 + 2 * P].bitcast(FP4X4),
+                                    lhsT_scale=ordered["scales"][:, c0:c0 + P], rhs=v_w[a][:].bitcast(FP8X4),
+                                    rhs_scale=v_s[a][:], start=(a == 0), stop=(a == PASSES - 1))
+            magnitude = held(("w1_raw110", "w1_raw010")[n % 2], [P, S], F32)
+            nc.scalar.activation(out=magnitude[:], in_=acc[:], func=ACT.Abs)
+            root = held("root%d" % (n % 2), [P, S], F32)
+            nc.scalar.activation(out=root[:], in_=magnitude[:], func=ACT.Abs_reciprocal_sqrt, bias=1.0)
+            damp[n] = held(slot, [P, S], F32)
+            nc.scalar.activation(out=damp[n][:], in_=root[:], func=ACT.Square)
+
+        def weigh(n, number, slot):
             b, t = divmod(n, 4)
-            acc = bank(2 + n % 2)
+            acc = bank(number)
             for a in range(PASSES):
                 cols = slice(t * P, (t + 1) * P)
                 nc.tensor.matmul_mx(out=acc[:], lhsT=w1_w[a, b][:, cols].bitcast(FP8X4),
                                     lhsT_scale=w1_s[a, b][:, cols], rhs=v_w[a][:].bitcast(FP8X4),
                                     rhs_scale=v_s[a][:], start=(a == 0), stop=(a == PASSES - 1))
-            if n in behind:
-                weighted[n] = held(behind[n], [P, S], F32)
+            weighted[n] = held(slot, [P, S], F32)
+            if n < FOLDED:
+                nc.vector.tensor_tensor(out=weighted[n][:], in0=acc[:], in1=wgs_t[:], op=MULT)
             else:
-                weighted[n] = ring.tile([P, S], F32, name="weighted")
-            nc.vector.tensor_tensor(out=weighted[n][:], in0=acc[:], in1=wgs_t[:], op=MULT)
+                nc.scalar.copy(out=weighted[n][:], in_=acc[:])
 
         def scatter(n):
             nc.vector.tensor_tensor(out=pages[n % PAGES][:].indirect(list2[:]), in0=weighted[n][:],
@@ -194,8 +234,8 @@ def tile_list_wind_bid_pages_kernel(tc, tab_words, tab_scales, offs, w1, w2_word
 
         def open_sum(b, u, c, number):
             sums[b, u, c] = bank(number)
-            add_t(b, u, c, 0, clim_t[b][:, 2 * u, :], True, False)
-            add_t(b, u, c, 1, clim_t[b][:, 2 * u + 1, :], False, False)
+            add_t(b, u, c, 0, clim_t[b, u][:, 0, :], True, False)
+            add_t(b, u, c, 1, clim_t[b, u][:, 1, :], False, False)
             add_t(b, u, c, 0, pages[(4 * b + 2 * u) % PAGES], False, False)
 
         def close_sum(b, u, c):
@@ -212,8 +252,8 @@ def tile_list_wind_bid_pages_kernel(tc, tab_words, tab_scales, offs, w1, w2_word
 
         def turn_back(b, c, number, copy):
             back = bank(number)
-            for g in range(2):
-                for u in range(2):
+            for u in (1, 0):
+                for g in range(2):
                     o0 = (2 * g + u) * P
                     nc.tensor.transpose(back[:, o0:o0 + P], pairs[b, u, c][:].bitcast(F32)[:, g * P:(g + 1) * P],
                                         ident[:])
@@ -227,11 +267,35 @@ def tile_list_wind_bid_pages_kernel(tc, tab_words, tab_scales, offs, w1, w2_word
             nc.vector.quantize_mx(out=z_w[b, h][:, cols].bitcast(FP8X4), scales=z_s[b, h][:, cols],
                                   in_=z_bf[b, c][:])
 
-        def sum_pair(b, u):
+        def sum_pair(b, u, numbers):
             for c in range(CHUNKS):
-                open_sum(b, u, c, 4 + c % 2)
+                open_sum(b, u, c, numbers[c % len(numbers)])
                 close_sum(b, u, c)
                 round_sum(b, u, c, nc.scalar.copy)
+
+
+        planes = [held("tab_w%d" % h, [P, 4, 512], BF16) for h in range(2)]
+
+        def part_pair(h, number):
+            back = bank(number)
+            for c in range(2):
+                for g in range(2):
+                    o0 = (2 * c + g) * P
+                    nc.tensor.transpose(back[:, o0:o0 + P],
+                                        pairs[1, 0, 2 * h + c][:].bitcast(F32)[:, g * P:(g + 1) * P], ident[:])
+            nc.scalar.copy(out=planes[h][:, 0:2, :], in_=back[:].bitcast(BF16).rearrange("p (m e) -> p e m", e=2))
+
+        def add_plane(t):
+            for h in range(2):
+                cols = slice(h * 512, (h + 1) * 512)
+                nc.vector.tensor_tensor(out=planes[h][:, t, :], in0=pages[t][:, cols],
+                                        in1=clim_t[1, t // 2][:, t % 2, cols], op=ADD)
+
+        def weave(c, copy):
+            h, half = divmod(c, 2)
+            z_bf[1, c] = held("z_bf%d" % (0, 1, 2, 1)[c], [P, 4 * CHUNK], BF16)
+            copy(out=z_bf[1, c][:].rearrange("p (m i t) -> p m t i", i=4, t=4),
+                 in_=planes[h][:, :, half * CHUNK:(half + 1) * CHUNK].rearrange("p t (m i) -> p m t i", i=4))
 
         w3_bf = held("w3_bf", [P, PASSES * 4 * N], BF16)
         w3_w = held("w3_w", [P, PASSES * N], U32)
@@ -246,56 +310,8 @@ def tile_list_wind_bid_pages_kernel(tc, tab_words, tab_scales, offs, w1, w2_word
                 nc.vector.quantize_mx(out=w3_w[:, c0:c1].bitcast(FP8X4), scales=w3_s[:, c0:c1],
                                       in_=w3_bf[:, 4 * c0:4 * c1])
 
-        spread(0)
-        damping(0)
-        round_w1(0, 0, nc.vector.tensor_copy)
-        quantize_w1(0, 0)
-        round_w1(1, 0, nc.vector.tensor_copy)
-        quantize_w1(1, 0, cuts=(0, 128, 256, 512))
-        weigh(0)
-        scatter(0)
-        damping(1)
-        weigh(1)
-        scatter(1)
-        damping(2)
-        round_w1(0, 1, nc.scalar.copy)
-        round_w1(1, 1, nc.scalar.copy)
-        weigh(2)
-        quantize_w1(0, 1)
-        quantize_w1(1, 1)
-        scatter(2)
-        damping(3)
-        weigh(3)
-        scatter(3)
-        spread(1)
-        damping(4)
-        sum_pair(0, 0)
-        weigh(4)
-        damping(5)
-        damping(6)
-        round_w3(0)
-        round_w3(1)
-        sum_pair(0, 1)
-        scatter(4)
-        quantize_w3()
-        weigh(5)
-        scatter(5)
-        damping(7)
-        nc.scalar.activation(out=warm[:, 8:9], in_=damp[7][:, 0:1], func=ACT.Sigmoid)
-        for c in range(CHUNKS):
-            turn_back(0, c, 6 + c % 2, nc.scalar.copy)
-            quantize_z(0, c)
-        weigh(6)
-        sum_pair(1, 0)
-        scatter(6)
-        weigh(7)
-        scatter(7)
-
-        sum_banks = (0, 1, 6, 7)
-        for c in range(CHUNKS):
-            open_sum(1, 1, c, sum_banks[c])
-        pieces = [(nt, 0, 512) for nt in range(3)] + [(0, 512, 512), (1, 512, 512), (2, 512, 256), (2, 768, 256)]
-        out_banks = ((2, 3), (0, 1), (6, 7), (4, 5), (2, 3), (0, 1), (6, 7))
+        pieces = [(0, 0, 512), (1, 0, 512), (0, 512, 512), (1, 512, 512), (2, 0, 512), (2, 512, 256), (2, 768, 256)]
+        out_banks = ((6, 7), (4, 5), (0, 1), (2, 3), (6, 7), (4, 5), (0, 1))
         accs = {}
 
         def product(i, which, b):
@@ -328,17 +344,67 @@ def tile_list_wind_bid_pages_kernel(tc, tab_words, tab_scales, offs, w1, w2_word
             nc.vector.tensor_tensor(out=result[:], in0=accs[i][1][:, 0:width], in1=gate[:], op=MULT)
             nc.sync.dma_start(out=out[nt * P:(nt + 1) * P, m0:m0 + width], in_=result[:])
 
-        first_pass(0)
+        spread(0)
+        absolute(0, 0, 1, "size_first")
+        plain_root(0, "root2")
+        damping(0, 0)
+        round_w1(0, 0, nc.vector.tensor_copy)
+        quantize_w1(0, 0)
+        round_w1(1, 0, nc.vector.tensor_copy)
+        quantize_w1(1, 0, cuts=(0, 128, 256, 512))
+        weigh(0, 2, "weighted0")
+        scatter(0)
+        order_w2()
+        absolute(0, 1, 4, "root2")
+        plain_root(1, "root1")
+        plain_root(2, "root0")
+        plain_root(3, "root3")
+        damping(1, 1)
+        damping(2, 6)
+        damping(3, 7)
+        weigh(1, 3, "weighted1")
+        scatter(1)
+        weigh(2, 2, "weighted2")
+        scatter(2)
+        round_w1(0, 1, nc.scalar.copy)
+        round_w1(1, 1, nc.scalar.copy)
+        quantize_w1(0, 1)
+        quantize_w1(1, 1)
+        weigh(3, 3, "w1_bf1")
+        scatter(3)
+        direct_damping(4, 0, "damp4")
+        sum_pair(0, 0, (6, 7))
+        weigh(4, 2, "weighted0")
+        scatter(4)
+        direct_damping(5, 1, "damp5")
+        weigh(5, 3, "weighted1")
+        scatter(5)
+        sum_pair(0, 1, (6, 7))
+        direct_damping(6, 0, "damp6")
         for c in range(CHUNKS):
-            close_sum(1, 1, c)
+            turn_back(0, c, 4 + c % 2, nc.scalar.copy)
+            quantize_z(0, c)
+        direct_damping(7, 1, "damp7")
+        weigh(6, 2, "weighted0")
+        scatter(6)
+        add_plane(2)
+        round_w3(0)
+        round_w3(1)
+        quantize_w3()
+        weigh(7, 3, "w3_bf")
+        sum_pair(1, 0, (6, 7))
+        part_pair(0, 4)
+        part_pair(1, 5)
+        nc.scalar.activation(out=warm[:, 8:9], in_=damp[7][:, 0:1], func=ACT.Sigmoid)
+        scatter(7)
+        late = held("damp7", [P, 512], U8)
+        nc.vector.tensor_copy(out=late[:].bitcast(I32), in_=z_s[0, 1][:].bitcast(I32))
+        z_s[0, 1] = late
+        for i in range(4):
+            first_pass(i)
+        add_plane(3)
         for c in range(CHUNKS):
-            copy = nc.scalar.copy if c % 2 == 0 else nc.vector.tensor_copy
-            round_sum(1, 1, c, copy)
-        for c in range(CHUNKS):
-            copy = nc.scalar.copy if c % 2 == 0 else nc.vector.tensor_copy
-            turn_back(1, c, 4 + c % 2, copy)
+            weave(c, nc.scalar.copy if c % 2 == 0 else nc.vector.tensor_copy)
             quantize_z(1, c)
-        first_pass(1)
-        first_pass(2)
         for i in range(len(pieces)):
             finish(i)

@@ -43,9 +43,9 @@ def tile_list_wind_bid_pages_kernel(tc, tab_words, tab_scales, offs, w1, w2_word
 
         def load_scales(tile, src, width):
             view = tile[:].bitcast(I32).rearrange("p (a c) -> p a c", a=PASSES)
-            for q in range(4):
-                nc.sync.dma_start(out=view[32 * q:32 * q + 4],
-                                  in_=src[:, 4 * q:4 * q + 4, :].bitcast(I32).rearrange("a r c -> r a c"))
+            rows = src.bitcast(I32).rearrange("a (q r) c -> r q a c", r=4)
+            for r in range(4):
+                nc.sync.dma_start(out=view[r:P:32], in_=rows[r])
 
         list1 = keep.tile([P, S // 16], U16, name="list1")
         list2 = keep.tile([P, S // 16], U16, name="list2")
@@ -127,11 +127,11 @@ def tile_list_wind_bid_pages_kernel(tc, tab_words, tab_scales, offs, w1, w2_word
 
         def round_w1(a, b, copy):
             w1_bf[a, b] = held("root3" if (a, b) == (0, 1) else "w1_bf%d" % a, [P, 2048], BF16)
-            rounded = w1_bf[a, b][:].rearrange("p (t m j) -> p m j t", t=4, j=4)
+            rounded = w1_bf[a, b][:].rearrange("p (t m j) -> p m t j", t=4, j=4)
             parts = len(w1_raw[a, b])
             for part, raw in enumerate(w1_raw[a, b]):
                 copy(out=rounded[:, part * P // parts:(part + 1) * P // parts],
-                     in_=raw[:].rearrange("p j (m t) -> p m j t", t=4))
+                     in_=raw[:].rearrange("p j (m t) -> p m t j", t=4))
 
         def quantize_w1(a, b, cuts=(0, 512)):
             w1_w[a, b] = held("w1_w%d%d" % (a, b), [P, 512], U32)
@@ -161,8 +161,9 @@ def tile_list_wind_bid_pages_kernel(tc, tab_words, tab_scales, offs, w1, w2_word
             for t in range(t0, t1):
                 size[t] = tile[:, :, t - t0, :]
             for jb in range(4):
-                nc.scalar.activation(out=tile[:, jb],
-                                     in_=spreads[b][jb][:].rearrange("j (p t) -> j t p", t=4)[:, t0:t1], func=ACT.Abs)
+                nc.scalar.activation(out=tile[:, jb].rearrange("j t p -> j p t"),
+                                     in_=spreads[b][jb][:].rearrange("j (p t) -> j p t", t=4)[:, :, t0:t1],
+                                     func=ACT.Abs)
 
 
         roots = {}
@@ -293,7 +294,7 @@ def tile_list_wind_bid_pages_kernel(tc, tab_words, tab_scales, offs, w1, w2_word
 
         def weave(c, copy):
             h, half = divmod(c, 2)
-            z_bf[1, c] = held("z_bf%d" % (0, 1, 2, 1)[c], [P, 4 * CHUNK], BF16)
+            z_bf[1, c] = held("z_bf%d" % c, [P, 4 * CHUNK], BF16)
             copy(out=z_bf[1, c][:].rearrange("p (m i t) -> p m t i", i=4, t=4),
                  in_=planes[h][:, :, half * CHUNK:(half + 1) * CHUNK].rearrange("p t (m i) -> p m t i", i=4))
 
@@ -404,7 +405,7 @@ def tile_list_wind_bid_pages_kernel(tc, tab_words, tab_scales, offs, w1, w2_word
             first_pass(i)
         add_plane(3)
         for c in range(CHUNKS):
-            weave(c, nc.scalar.copy if c % 2 == 0 else nc.vector.tensor_copy)
+            weave(c, nc.vector.tensor_copy if c < 2 else nc.scalar.copy)
             quantize_z(1, c)
         for i in range(len(pieces)):
             finish(i)

@@ -19,13 +19,14 @@ MULT = mybir.AluOpType.mult
 ADD = mybir.AluOpType.add
 
 P = 128
+PACK = 4
+SPAN = P * PACK
 PASSES = 2
-PLANES = 8
+BANK = 512
 PAGES = 4
 CHUNK = 256
 CHUNKS = T2 // CHUNK
-BANK = 512
-FOLDED = 8
+HALF = T2 // 2
 
 
 def tile_list_wind_bid_pages_kernel(tc, tab_words, tab_scales, offs, w1, w2_words, w2_scales, offs2, wgs,
@@ -35,24 +36,18 @@ def tile_list_wind_bid_pages_kernel(tc, tab_words, tab_scales, offs, w1, w2_word
         keep = ctx.enter_context(tc.tile_pool(name="keep", bufs=1))
         psum = ctx.enter_context(tc.psum_pool(name="psum", bufs=1))
 
-        def held(name, shape, dtype):
-            return keep.tile(shape, dtype, name=name, align_bytes=64)
+        def held(slot, shape, dtype):
+            return keep.tile(shape, dtype, name=slot, align_bytes=64)
 
         def bank(number):
             return psum.tile([P, BANK], F32, name="bank%d" % number, tag="bank%d" % number)
 
-        def load_scales(tile, src, width):
-            view = tile[:].bitcast(I32).rearrange("p (a c) -> p a c", a=PASSES)
-            rows = src.bitcast(I32).rearrange("a (q r) c -> r q a c", r=4)
-            for r in range(4):
-                nc.sync.dma_start(out=view[r:P:32], in_=rows[r])
-
         list1 = keep.tile([P, S // 16], U16, name="list1")
         list2 = keep.tile([P, S // 16], U16, name="list2")
         tab_s = held("tab_s", [P, PASSES * T], U8)
-        w2_s_raw = held("w2_s_raw", [P, PASSES * H], U8)
+        w2_s = held("w2_s", [P, PASSES * H], U8)
         w4_s = held("w4_s", [P, PASSES * N], U8)
-        for tile in (tab_s, w2_s_raw, w4_s):
+        for tile in (tab_s, w2_s, w4_s):
             nc.vector.memset(tile[:].bitcast(I32), 0)
         ident = held("ident", [P, P], F32)
         nc.vector.memset(ident[:], 0.0)
@@ -60,47 +55,55 @@ def tile_list_wind_bid_pages_kernel(tc, tab_words, tab_scales, offs, w1, w2_word
         pages = [held("page%d" % n, [P, T2], F32) for n in range(PAGES)]
         for tile in pages:
             nc.vector.memset(tile[:].bitcast(I32), 0)
+
         warm = held("warm", [P, 16], F32)
         nc.scalar.activation(out=warm[:, 0:1], in_=ident[:, 0:1], func=ACT.Abs_reciprocal_sqrt, bias=1.0)
 
         tab_w = [held("tab_w%d" % a, [P, T], U32) for a in range(PASSES)]
-        w2_w = [held("w2_w%d" % b, [P, PASSES * 1024], U8) for b in range(PASSES)]
+        w2_w = [held("w2_w%d" % b, [P, PASSES * 2 * SPAN], U8) for b in range(PASSES)]
         w1_raw = {}
         wgs_t = held("wgs_t", [P, S], F32)
         clim_t = {(b, u): held("clim%d%d" % (b, u), [P, 2, T2], F32) for b in range(PASSES) for u in range(2)}
-        w3_raw = [held("w3_raw%d" % b, [P, 4, N], F32) for b in range(PASSES)]
+        w3_raw = [held("w3_raw%d" % b, [P, PACK, N], F32) for b in range(PASSES)]
         w4_w = held("w4_w", [P, PASSES * N], U32)
+
+        def load_scales(tile, src):
+            view = tile[:].bitcast(I32).rearrange("p (a c) -> p a c", a=PASSES)
+            rows = src.bitcast(I32).rearrange("a (q r) c -> r q a c", r=4)
+            for r in range(4):
+                nc.sync.dma_start(out=view[r:P:32], in_=rows[r])
 
         def load_tab(a):
             nc.sync.dma_start(out=tab_w[a][:].bitcast(I32),
                               in_=tab_words[a].rearrange("p t i -> p (t i)").bitcast(I32))
 
         def load_w1(a, b, parts=1):
-            width = 512 // parts
-            w1_raw[a, b] = [held("w1_raw%d%d%d" % (a, b, part), [P, 4, width], F32) for part in range(parts)]
+            width = SPAN // parts
+            w1_raw[a, b] = [held("w1_raw%d%d%d" % (a, b, part), [P, PACK, width], F32) for part in range(parts)]
             for part, raw in enumerate(w1_raw[a, b]):
-                c0 = 512 * b + part * width
-                nc.sync.dma_start(out=raw[:],
-                                  in_=w1[512 * a:512 * a + 512, c0:c0 + width].rearrange("(p j) c -> p j c", j=4))
+                c0 = SPAN * b + part * width
+                rows = w1[SPAN * a:SPAN * (a + 1), c0:c0 + width]
+                nc.sync.dma_start(out=raw[:], in_=rows.rearrange("(p j) c -> p j c", j=PACK))
 
         def load_w2(b):
+            words = w2_words[:, :, 2 * SPAN * b:2 * SPAN * (b + 1)]
             nc.sync.dma_start(out=w2_w[b][:].bitcast(I32).rearrange("p (a c) -> p a c", a=PASSES),
-                              in_=w2_words[:, :, 1024 * b:1024 * b + 1024].bitcast(I32).rearrange("a p c -> p a c"))
+                              in_=words.bitcast(I32).rearrange("a p c -> p a c"))
 
         def load_clim(b):
-            rows = clim[512 * b:512 * b + 512, :].rearrange("(p j) c -> p j c", j=4)
+            rows = clim[SPAN * b:SPAN * (b + 1), :].rearrange("(p j) c -> p j c", j=PACK)
             for u in range(2):
                 nc.sync.dma_start(out=clim_t[b, u][:], in_=rows[:, 2 * u:2 * u + 2, :])
 
-        def load_rows(tile, src, b):
-            nc.sync.dma_start(out=tile[:], in_=src[512 * b:512 * b + 512, :].rearrange("(p j) c -> p j c", j=4))
+        def load_w3(b):
+            nc.sync.dma_start(out=w3_raw[b][:], in_=w3[SPAN * b:SPAN * (b + 1), :].rearrange("(p j) c -> p j c", j=PACK))
 
         nc.sync.dma_start(list1[:], offs)
         load_tab(0)
-        load_scales(tab_s, tab_scales, T)
+        load_scales(tab_s, tab_scales)
         load_w2(0)
         load_tab(1)
-        load_scales(w2_s_raw, w2_scales, H)
+        load_scales(w2_s, w2_scales)
         load_w1(0, 0)
         load_w1(1, 0, parts=2)
         nc.sync.dma_start(out=wgs_t[:], in_=wgs)
@@ -109,158 +112,139 @@ def tile_list_wind_bid_pages_kernel(tc, tab_words, tab_scales, offs, w1, w2_word
         load_w1(0, 1)
         load_w1(1, 1)
         load_clim(0)
-        load_rows(w3_raw[0], w3, 0)
-        load_rows(w3_raw[1], w3, 1)
+        load_w3(0)
+        load_w3(1)
         nc.sync.dma_start(out=w4_w[:].bitcast(I32).rearrange("p (a c) -> p a c", a=PASSES),
                           in_=w4_words.rearrange("a p c i -> p a (c i)").bitcast(I32))
-        load_scales(w4_s, w4_scales, N)
+        load_scales(w4_s, w4_scales)
         load_clim(1)
 
         v_w = [held("v_w%d" % a, [P, S], U32) for a in range(PASSES)]
         v_s = [held("v_s%d" % a, [P, S], U8) for a in range(PASSES)]
-
+        nc.vector.tensor_copy(out=v_w[0][:], in_=tab_w[0][:].indirect(list1[:]))
         for a in range(PASSES):
             nc.vector.tensor_copy(out=v_s[a][:], in_=tab_s[:, a * T:(a + 1) * T].indirect(list1[:]))
-            nc.vector.tensor_copy(out=v_w[a][:], in_=tab_w[a][:].indirect(list1[:]))
+        nc.vector.tensor_copy(out=v_w[1][:], in_=tab_w[1][:].indirect(list1[:]))
 
         w1_w, w1_s, w1_bf = {}, {}, {}
+        magnitudes, roots, damp, weighted = {}, {}, {}, {}
 
-        def round_w1(a, b, copy):
-            w1_bf[a, b] = held("root3" if (a, b) == (0, 1) else "w1_bf%d" % a, [P, 2048], BF16)
-            rounded = w1_bf[a, b][:].rearrange("p (t m j) -> p m t j", t=4, j=4)
+        def round_w1(a, b, slot, copy):
+            w1_bf[a, b] = held(slot, [P, PACK * SPAN], BF16)
+            rounded = w1_bf[a, b][:].rearrange("p (t m j) -> p m t j", t=PACK, j=PACK)
             parts = len(w1_raw[a, b])
             for part, raw in enumerate(w1_raw[a, b]):
                 copy(out=rounded[:, part * P // parts:(part + 1) * P // parts],
-                     in_=raw[:].rearrange("p j (m t) -> p m t j", t=4))
+                     in_=raw[:].rearrange("p j (m t) -> p m t j", t=PACK))
 
-        def quantize_w1(a, b, cuts=(0, 512)):
-            w1_w[a, b] = held("w1_w%d%d" % (a, b), [P, 512], U32)
-            w1_s[a, b] = held("w1_s%d%d" % (a, b), [P, 512], U8)
+        def quantize_w1(a, b, cuts=(0, SPAN)):
+            w1_w[a, b] = held("w1_w%d%d" % (a, b), [P, SPAN], U32)
+            w1_s[a, b] = held("w1_s%d%d" % (a, b), [P, SPAN], U8)
             for c0, c1 in zip(cuts, cuts[1:]):
                 nc.vector.quantize_mx(out=w1_w[a, b][:, c0:c1].bitcast(FP8X4), scales=w1_s[a, b][:, c0:c1],
-                                      in_=w1_bf[a, b][:, 4 * c0:4 * c1])
+                                      in_=w1_bf[a, b][:, PACK * c0:PACK * c1])
 
-        damp, weighted = {}, {}
-
-        size, spreads = {}, {}
-
-        def spread(b):
+        def turned_spread():
             accs = [bank(4 + jb) for jb in range(4)]
             for a in range(PASSES):
-                c0 = a * H + b * 512
                 for jb in range(4):
                     cols = slice(jb * P, (jb + 1) * P)
                     nc.tensor.matmul_mx(out=accs[jb][:], lhsT=v_w[a][:, cols].bitcast(FP8X4),
                                         lhsT_scale=v_s[a][:, cols],
-                                        rhs=w2_w[b][:, 1024 * a:1024 * a + 1024].bitcast(FP4X4),
-                                        rhs_scale=w2_s_raw[:, c0:c0 + 512], start=(a == 0), stop=(a == PASSES - 1))
-            spreads[b] = accs
+                                        rhs=w2_w[0][:, 2 * SPAN * a:2 * SPAN * (a + 1)].bitcast(FP4X4),
+                                        rhs_scale=w2_s[:, a * H:a * H + SPAN], start=(a == 0), stop=(a == PASSES - 1))
+            return accs
 
-        def absolute(b, t0, t1, slot):
+        def turned_magnitude(accs, t0, t1, slot):
             tile = held(slot, [P, 4, t1 - t0, P], F32)
             for t in range(t0, t1):
-                size[t] = tile[:, :, t - t0, :]
+                magnitudes[t] = tile[:, :, t - t0, :]
             for jb in range(4):
                 nc.scalar.activation(out=tile[:, jb].rearrange("j t p -> j p t"),
-                                     in_=spreads[b][jb][:].rearrange("j (p t) -> j p t", t=4)[:, :, t0:t1],
-                                     func=ACT.Abs)
+                                     in_=accs[jb][:].rearrange("j (p t) -> j p t", t=PACK)[:, :, t0:t1], func=ACT.Abs)
 
-
-        roots = {}
-
-        def plain_root(n, slot):
+        def turned_root(n, slot):
             roots[n] = held(slot, [P, 4, P], F32)[:]
-            nc.scalar.activation(out=roots[n], in_=size[n], func=ACT.Abs_reciprocal_sqrt, bias=1.0)
+            nc.scalar.activation(out=roots[n], in_=magnitudes[n], func=ACT.Abs_reciprocal_sqrt, bias=1.0)
 
-        def damping(n, number):
+        def turned_damping(n, number):
             acc = bank(number)
             for jb in range(4):
                 nc.tensor.transpose(acc[:, jb * P:(jb + 1) * P], roots[n][:, jb, :], ident[:])
             damp[n] = held("damp%d" % n, [P, S], F32)
             nc.scalar.activation(out=damp[n][:], in_=acc[:], func=ACT.Square)
 
-        ordered = {}
-
         def order_w2():
-            w2_cols = held("w1_raw101", [P, PASSES * 1024], U8)
-            w2_s = held("w1_raw100", [P, PASSES * 512], U8)
-            ordered["words"], ordered["scales"] = w2_cols, w2_s
+            words = held("w1_raw101", [P, PASSES * 2 * SPAN], U8)
+            scales = held("w2_s_late", [P, PASSES * SPAN], U8)
             nc.vector.tensor_copy(
-                out=w2_cols[:].bitcast(U16).rearrange("p (a t m) -> p a t m", a=PASSES, t=4),
-                in_=w2_w[1][:].bitcast(U16).rearrange("p (a m t) -> p a t m", a=PASSES, t=4))
+                out=words[:].bitcast(U16).rearrange("p (a t m) -> p a t m", a=PASSES, t=PACK),
+                in_=w2_w[1][:].bitcast(U16).rearrange("p (a m t) -> p a t m", a=PASSES, t=PACK))
             nc.vector.tensor_copy(
-                out=w2_s[:].rearrange("p (a t m) -> p a t m", a=PASSES, t=4),
-                in_=w2_s_raw[:].rearrange("p (a b m t) -> p b a t m", a=PASSES, b=PASSES, t=4)[:, 1])
+                out=scales[:].rearrange("p (a t m) -> p a t m", a=PASSES, t=PACK),
+                in_=w2_s[:].rearrange("p (a b m t) -> p b a t m", a=PASSES, b=PASSES, t=PACK)[:, 1])
+            return words, scales
 
-        def direct_damping(n, number, slot):
-            acc = bank(number)
+        def direct_damping(n, words, scales):
+            acc = bank(n % 2)
             for a in range(PASSES):
-                c0 = a * 512 + (n % 4) * P
-                nc.tensor.matmul_mx(out=acc[:], lhsT=ordered["words"][:, 2 * c0:2 * c0 + 2 * P].bitcast(FP4X4),
-                                    lhsT_scale=ordered["scales"][:, c0:c0 + P], rhs=v_w[a][:].bitcast(FP8X4),
+                c0 = a * SPAN + (n % PACK) * P
+                nc.tensor.matmul_mx(out=acc[:], lhsT=words[:, 2 * c0:2 * c0 + 2 * P].bitcast(FP4X4),
+                                    lhsT_scale=scales[:, c0:c0 + P], rhs=v_w[a][:].bitcast(FP8X4),
                                     rhs_scale=v_s[a][:], start=(a == 0), stop=(a == PASSES - 1))
             magnitude = held(("w1_raw110", "w1_raw010")[n % 2], [P, S], F32)
             nc.scalar.activation(out=magnitude[:], in_=acc[:], func=ACT.Abs)
             root = held("root%d" % (n % 2), [P, S], F32)
             nc.scalar.activation(out=root[:], in_=magnitude[:], func=ACT.Abs_reciprocal_sqrt, bias=1.0)
-            damp[n] = held(slot, [P, S], F32)
+            damp[n] = held("damp%d" % n, [P, S], F32)
             nc.scalar.activation(out=damp[n][:], in_=root[:], func=ACT.Square)
 
-        def weigh(n, number, slot):
-            b, t = divmod(n, 4)
-            acc = bank(number)
+        def weigh(n, slot):
+            b, t = divmod(n, PACK)
+            acc = bank(2 + n % 2)
             for a in range(PASSES):
                 cols = slice(t * P, (t + 1) * P)
                 nc.tensor.matmul_mx(out=acc[:], lhsT=w1_w[a, b][:, cols].bitcast(FP8X4),
                                     lhsT_scale=w1_s[a, b][:, cols], rhs=v_w[a][:].bitcast(FP8X4),
                                     rhs_scale=v_s[a][:], start=(a == 0), stop=(a == PASSES - 1))
             weighted[n] = held(slot, [P, S], F32)
-            if n < FOLDED:
-                nc.vector.tensor_tensor(out=weighted[n][:], in0=acc[:], in1=wgs_t[:], op=MULT)
-            else:
-                nc.scalar.copy(out=weighted[n][:], in_=acc[:])
+            nc.vector.tensor_tensor(out=weighted[n][:], in0=acc[:], in1=wgs_t[:], op=MULT)
 
         def scatter(n):
             nc.vector.tensor_tensor(out=pages[n % PAGES][:].indirect(list2[:]), in0=weighted[n][:],
                                     in1=damp[n][:], op=MULT)
 
-        sums, pairs = {}, {}
+        pairs, z_bf = {}, {}
+        z_w = {(b, h): held("z_w%d%d" % (b, h), [P, HALF], U32) for b in range(PASSES) for h in range(2)}
+        z_s = {(b, h): held("z_s%d%d" % (b, h), [P, HALF], U8) for b in range(PASSES) for h in range(2)}
 
-        def add_t(b, u, c, e, src, first, last):
-            for g in range(2):
-                m0 = c * CHUNK + g * P
-                o0 = (2 * g + e) * P
-                nc.tensor.matmul(out=sums[b, u, c][:, o0:o0 + P], lhsT=src[:, m0:m0 + P], rhs=ident[:],
-                                 is_transpose=True, start=(first and g == 0), stop=(last and g == 1))
+        def sum_pair(b, u):
+            first = PACK * b + 2 * u
+            sources = [(0, clim_t[b, u][:, 0, :]), (1, clim_t[b, u][:, 1, :]),
+                       (0, pages[first % PAGES]), (1, pages[(first + 1) % PAGES])]
+            for c in range(CHUNKS):
+                acc = bank(6 + c % 2)
+                for step, (e, src) in enumerate(sources):
+                    for g in range(2):
+                        m0 = c * CHUNK + g * P
+                        o0 = (2 * g + e) * P
+                        nc.tensor.matmul(out=acc[:, o0:o0 + P], lhsT=src[:, m0:m0 + P], rhs=ident[:],
+                                         is_transpose=True, start=(step == 0 and g == 0),
+                                         stop=(step == len(sources) - 1 and g == 1))
+                pairs[b, u, c] = held("pairs%d%d" % (u, c), [P, BANK], BF16)
+                nc.scalar.copy(out=pairs[b, u, c][:].rearrange("m (g p e) -> m g p e", g=2, e=2),
+                               in_=acc[:].rearrange("m (g e p) -> m g p e", g=2, e=2))
 
-        def open_sum(b, u, c, number):
-            sums[b, u, c] = bank(number)
-            add_t(b, u, c, 0, clim_t[b, u][:, 0, :], True, False)
-            add_t(b, u, c, 1, clim_t[b, u][:, 1, :], False, False)
-            add_t(b, u, c, 0, pages[(4 * b + 2 * u) % PAGES], False, False)
-
-        def close_sum(b, u, c):
-            add_t(b, u, c, 1, pages[(4 * b + 2 * u + 1) % PAGES], False, True)
-
-        def round_sum(b, u, c, copy):
-            pairs[b, u, c] = held("pairs%d%d" % (u, c), [P, 512], BF16)
-            copy(out=pairs[b, u, c][:].rearrange("m (g p e) -> m g p e", g=2, e=2),
-                 in_=sums[b, u, c][:].rearrange("m (g e p) -> m g p e", g=2, e=2))
-
-        z_w = {(b, h): held("z_w%d%d" % (b, h), [P, 512], U32) for b in range(PASSES) for h in range(2)}
-        z_s = {(b, h): held("z_s%d%d" % (b, h), [P, 512], U8) for b in range(PASSES) for h in range(2)}
-        z_bf = {}
-
-        def turn_back(b, c, number, copy):
-            back = bank(number)
+        def turn_back(c):
+            back = bank(4 + c % 2)
             for u in (1, 0):
                 for g in range(2):
                     o0 = (2 * g + u) * P
-                    nc.tensor.transpose(back[:, o0:o0 + P], pairs[b, u, c][:].bitcast(F32)[:, g * P:(g + 1) * P],
+                    nc.tensor.transpose(back[:, o0:o0 + P], pairs[0, u, c][:].bitcast(F32)[:, g * P:(g + 1) * P],
                                         ident[:])
-            z_bf[b, c] = held("z_bf%d" % c, [P, 4 * CHUNK], BF16)
-            copy(out=z_bf[b, c][:].bitcast(F32).rearrange("p (g m u) -> p g m u", g=2, u=2),
-                 in_=back[:].rearrange("p (g u m) -> p g m u", g=2, u=2))
+            z_bf[0, c] = held("z_bf%d" % c, [P, PACK * CHUNK], BF16)
+            nc.scalar.copy(out=z_bf[0, c][:].bitcast(F32).rearrange("p (g m u) -> p g m u", g=2, u=2),
+                           in_=back[:].rearrange("p (g u m) -> p g m u", g=2, u=2))
 
         def quantize_z(b, c):
             h, half = divmod(c, 2)
@@ -268,17 +252,10 @@ def tile_list_wind_bid_pages_kernel(tc, tab_words, tab_scales, offs, w1, w2_word
             nc.vector.quantize_mx(out=z_w[b, h][:, cols].bitcast(FP8X4), scales=z_s[b, h][:, cols],
                                   in_=z_bf[b, c][:])
 
-        def sum_pair(b, u, numbers):
-            for c in range(CHUNKS):
-                open_sum(b, u, c, numbers[c % len(numbers)])
-                close_sum(b, u, c)
-                round_sum(b, u, c, nc.scalar.copy)
+        planes = [held("tab_w%d" % h, [P, PACK, HALF], BF16) for h in range(2)]
 
-
-        planes = [held("tab_w%d" % h, [P, 4, 512], BF16) for h in range(2)]
-
-        def part_pair(h, number):
-            back = bank(number)
+        def part_pair(h):
+            back = bank(4 + h)
             for c in range(2):
                 for g in range(2):
                     o0 = (2 * c + g) * P
@@ -286,126 +263,135 @@ def tile_list_wind_bid_pages_kernel(tc, tab_words, tab_scales, offs, w1, w2_word
                                         pairs[1, 0, 2 * h + c][:].bitcast(F32)[:, g * P:(g + 1) * P], ident[:])
             nc.scalar.copy(out=planes[h][:, 0:2, :], in_=back[:].bitcast(BF16).rearrange("p (m e) -> p e m", e=2))
 
-        def add_plane(t):
+        def add_plane(n):
+            t = n % PACK
             for h in range(2):
-                cols = slice(h * 512, (h + 1) * 512)
-                nc.vector.tensor_tensor(out=planes[h][:, t, :], in0=pages[t][:, cols],
+                cols = slice(h * HALF, (h + 1) * HALF)
+                nc.vector.tensor_tensor(out=planes[h][:, t, :], in0=pages[n % PAGES][:, cols],
                                         in1=clim_t[1, t // 2][:, t % 2, cols], op=ADD)
 
         def weave(c, copy):
             h, half = divmod(c, 2)
-            z_bf[1, c] = held("z_bf%d" % c, [P, 4 * CHUNK], BF16)
-            copy(out=z_bf[1, c][:].rearrange("p (m i t) -> p m t i", i=4, t=4),
+            z_bf[1, c] = held("z_bf%d" % c, [P, PACK * CHUNK], BF16)
+            copy(out=z_bf[1, c][:].rearrange("p (m i t) -> p m t i", i=4, t=PACK),
                  in_=planes[h][:, :, half * CHUNK:(half + 1) * CHUNK].rearrange("p t (m i) -> p m t i", i=4))
 
-        w3_bf = held("w3_bf", [P, PASSES * 4 * N], BF16)
+        w3_bf = held("w3_bf", [P, PASSES * PACK * N], BF16)
         w3_w = held("w3_w", [P, PASSES * N], U32)
         w3_s = held("w3_s", [P, PASSES * N], U8)
 
         def round_w3(b):
-            nc.scalar.copy(out=w3_bf[:, b * 4 * N:(b + 1) * 4 * N].rearrange("p (c i j) -> p c j i", i=4, j=4),
+            nc.scalar.copy(out=w3_bf[:, b * PACK * N:(b + 1) * PACK * N].rearrange("p (c i j) -> p c j i", i=4, j=PACK),
                            in_=w3_raw[b][:].rearrange("p j (c i) -> p c j i", i=4))
 
         def quantize_w3():
-            for c0, c1 in ((0, 512), (512, 768)):
+            for c0, c1 in ((0, 512), (512, PASSES * N)):
                 nc.vector.quantize_mx(out=w3_w[:, c0:c1].bitcast(FP8X4), scales=w3_s[:, c0:c1],
-                                      in_=w3_bf[:, 4 * c0:4 * c1])
+                                      in_=w3_bf[:, PACK * c0:PACK * c1])
 
-        pieces = [(0, 0, 512), (1, 0, 512), (0, 512, 512), (1, 512, 512), (2, 0, 512), (2, 512, 256), (2, 768, 256)]
-        out_banks = ((6, 7), (4, 5), (0, 1), (2, 3), (6, 7), (4, 5), (0, 1))
+        pieces = [(0, 0, HALF), (1, 0, HALF), (0, HALF, HALF), (1, HALF, HALF), (2, 0, HALF),
+                  (2, HALF, CHUNK), (2, HALF + CHUNK, CHUNK)]
+        piece_banks = ((6, 7), (4, 5), (0, 1), (2, 3))
+        ahead = len(piece_banks)
+        gate_side, vol_side = 0, 1
         accs = {}
 
-        def product(i, which, b):
+        def open_piece(i):
+            accs[i] = [bank(number) for number in piece_banks[i % ahead]]
+
+        def product(i, side, b):
             nt, m0, width = pieces[i]
-            words, scales = ((w4_w, w4_s), (w3_w, w3_s))[which]
+            words, scales = ((w4_w, w4_s), (w3_w, w3_s))[side]
             cols = slice(b * N + nt * P, b * N + (nt + 1) * P)
-            h, c0 = divmod(m0, 512)
-            nc.tensor.matmul_mx(out=accs[i][which][:, 0:width], lhsT=words[:, cols].bitcast(FP8X4),
+            h, c0 = divmod(m0, HALF)
+            nc.tensor.matmul_mx(out=accs[i][side][:, 0:width], lhsT=words[:, cols].bitcast(FP8X4),
                                 lhsT_scale=scales[:, cols], rhs=z_w[b, h][:, c0:c0 + width].bitcast(FP8X4),
                                 rhs_scale=z_s[b, h][:, c0:c0 + width], start=(b == 0), stop=(b == PASSES - 1))
 
-        def first_pass(i):
-            accs[i] = (bank(out_banks[i][0]), bank(out_banks[i][1]))
-            product(i, 0, 0)
-            product(i, 1, 0)
-
         def finish(i):
             nt, m0, width = pieces[i]
-            if i not in accs:
-                accs[i] = (bank(out_banks[i][0]), bank(out_banks[i][1]))
-                product(i, 0, 0)
-                product(i, 0, 1)
-                product(i, 1, 0)
+            if i < ahead:
+                product(i, gate_side, 1)
             else:
-                product(i, 0, 1)
-            product(i, 1, 1)
+                open_piece(i)
+                product(i, gate_side, 0)
+                product(i, gate_side, 1)
+                product(i, vol_side, 0)
+            product(i, vol_side, 1)
             gate = held("root%d" % (i % 3), [P, width], F32)
-            nc.scalar.activation(out=gate[:], in_=accs[i][0][:, 0:width], func=ACT.Sigmoid)
+            nc.scalar.activation(out=gate[:], in_=accs[i][gate_side][:, 0:width], func=ACT.Sigmoid)
             result = held("damp%d" % i, [P, width], F32)
-            nc.vector.tensor_tensor(out=result[:], in0=accs[i][1][:, 0:width], in1=gate[:], op=MULT)
+            nc.vector.tensor_tensor(out=result[:], in0=accs[i][vol_side][:, 0:width], in1=gate[:], op=MULT)
             nc.sync.dma_start(out=out[nt * P:(nt + 1) * P, m0:m0 + width], in_=result[:])
 
-        spread(0)
-        absolute(0, 0, 1, "size_first")
-        plain_root(0, "root2")
-        damping(0, 0)
-        round_w1(0, 0, nc.vector.tensor_copy)
+        spread = turned_spread()
+        turned_magnitude(spread, 0, 1, "magnitude0")
+        turned_root(0, "root2")
+        turned_damping(0, 0)
+        round_w1(0, 0, "w1_bf0", nc.vector.tensor_copy)
         quantize_w1(0, 0)
-        round_w1(1, 0, nc.vector.tensor_copy)
-        quantize_w1(1, 0, cuts=(0, 128, 256, 512))
-        weigh(0, 2, "weighted0")
+        round_w1(1, 0, "w1_bf1", nc.vector.tensor_copy)
+        quantize_w1(1, 0, cuts=(0, P, 2 * P, SPAN))
+        weigh(0, "weighted0")
         scatter(0)
-        order_w2()
-        absolute(0, 1, 4, "root2")
-        plain_root(1, "root1")
-        plain_root(2, "root0")
-        plain_root(3, "root3")
-        damping(1, 1)
-        damping(2, 6)
-        damping(3, 7)
-        weigh(1, 3, "weighted1")
+        w2_late = order_w2()
+
+        turned_magnitude(spread, 1, PACK, "root2")
+        turned_root(1, "root1")
+        turned_root(2, "root0")
+        turned_root(3, "root3")
+        turned_damping(1, 1)
+        turned_damping(2, 6)
+        turned_damping(3, 7)
+        weigh(1, "weighted1")
         scatter(1)
-        weigh(2, 2, "weighted2")
+        weigh(2, "weighted2")
         scatter(2)
-        round_w1(0, 1, nc.scalar.copy)
-        round_w1(1, 1, nc.scalar.copy)
+        round_w1(0, 1, "root3", nc.scalar.copy)
+        round_w1(1, 1, "w1_bf1", nc.scalar.copy)
         quantize_w1(0, 1)
         quantize_w1(1, 1)
-        weigh(3, 3, "w1_bf1")
+        weigh(3, "w1_bf1")
         scatter(3)
-        direct_damping(4, 0, "damp4")
-        sum_pair(0, 0, (6, 7))
-        weigh(4, 2, "weighted0")
+
+        direct_damping(4, *w2_late)
+        sum_pair(0, 0)
+        weigh(4, "weighted0")
         scatter(4)
-        direct_damping(5, 1, "damp5")
-        weigh(5, 3, "weighted1")
+        direct_damping(5, *w2_late)
+        weigh(5, "weighted1")
         scatter(5)
-        sum_pair(0, 1, (6, 7))
-        direct_damping(6, 0, "damp6")
+        sum_pair(0, 1)
+        direct_damping(6, *w2_late)
         for c in range(CHUNKS):
-            turn_back(0, c, 4 + c % 2, nc.scalar.copy)
+            turn_back(c)
             quantize_z(0, c)
-        direct_damping(7, 1, "damp7")
-        weigh(6, 2, "weighted0")
+        direct_damping(7, *w2_late)
+        weigh(6, "weighted0")
         scatter(6)
-        add_plane(2)
+        add_plane(6)
         round_w3(0)
         round_w3(1)
         quantize_w3()
-        weigh(7, 3, "w3_bf")
-        sum_pair(1, 0, (6, 7))
-        part_pair(0, 4)
-        part_pair(1, 5)
+
+        weigh(7, "w3_bf")
+        sum_pair(1, 0)
+        part_pair(0)
+        part_pair(1)
         nc.scalar.activation(out=warm[:, 8:9], in_=damp[7][:, 0:1], func=ACT.Sigmoid)
         scatter(7)
-        late = held("damp7", [P, 512], U8)
-        nc.vector.tensor_copy(out=late[:].bitcast(I32), in_=z_s[0, 1][:].bitcast(I32))
-        z_s[0, 1] = late
-        for i in range(4):
-            first_pass(i)
-        add_plane(3)
+
+        late_scales = held("damp7", [P, HALF], U8)
+        nc.vector.tensor_copy(out=late_scales[:].bitcast(I32), in_=z_s[0, 1][:].bitcast(I32))
+        z_s[0, 1] = late_scales
+        for i in range(ahead):
+            open_piece(i)
+            product(i, gate_side, 0)
+            product(i, vol_side, 0)
+
+        add_plane(7)
         for c in range(CHUNKS):
-            weave(c, nc.vector.tensor_copy if c < 2 else nc.scalar.copy)
+            weave(c, nc.vector.tensor_copy if c < CHUNKS // 2 else nc.scalar.copy)
             quantize_z(1, c)
         for i in range(len(pieces)):
             finish(i)

@@ -23,9 +23,10 @@ PACK = 4
 SPAN = P * PACK
 PASSES = 2
 BANK = 512
-PAGES = 4
+PAGES = 6
 CHUNK = 256
 CHUNKS = T2 // CHUNK
+LISTS = 8
 HALF = T2 // 2
 
 
@@ -45,14 +46,14 @@ def tile_list_wind_bid_pages_kernel(tc, tab_words, tab_scales, offs, w1, w2_word
         list1 = keep.tile([P, S // 16], U16, name="list1")
         list2 = keep.tile([P, S // 16], U16, name="list2")
         tab_s = held("tab_s", [P, PASSES * T], U8)
-        w2_s = held("w2_s", [P, PASSES * H], U8)
+        w2_s = [held("w2_s%d" % b, [P, PASSES * SPAN], U8) for b in range(PASSES)]
         w4_s = held("w4_s", [P, PASSES * N], U8)
-        for tile in (tab_s, w2_s, w4_s):
+        for tile in (tab_s, w2_s[0], w2_s[1], w4_s):
             nc.vector.memset(tile[:].bitcast(I32), 0)
         ident = held("ident", [P, P], F32)
         nc.vector.memset(ident[:], 0.0)
         make_identity(nc, ident[:], nomemset=True)
-        pages = [held("page%d" % n, [P, T2], F32) for n in range(PAGES)]
+        pages = [held("page%d" % n, [P, T2], F32) for n in range(PAGES - 1)]
         for tile in pages:
             nc.vector.memset(tile[:].bitcast(I32), 0)
 
@@ -103,13 +104,14 @@ def tile_list_wind_bid_pages_kernel(tc, tab_words, tab_scales, offs, w1, w2_word
         load_scales(tab_s, tab_scales)
         load_w2(0)
         load_tab(1)
-        load_scales(w2_s, w2_scales)
+        load_scales(w2_s[0], w2_scales[:, :, 0:SPAN])
         load_w1(0, 0)
         load_w1(1, 0, parts=2)
         nc.sync.dma_start(out=wgs_t[:], in_=wgs)
         nc.sync.dma_start(list2[:], offs2)
-        load_w2(1)
         load_w1(0, 1)
+        load_w2(1)
+        load_scales(w2_s[1], w2_scales[:, :, SPAN:H])
         load_w1(1, 1)
         load_clim(0)
         load_w3(0)
@@ -125,12 +127,17 @@ def tile_list_wind_bid_pages_kernel(tc, tab_words, tab_scales, offs, w1, w2_word
         for a in range(PASSES):
             nc.vector.tensor_copy(out=v_s[a][:], in_=tab_s[:, a * T:(a + 1) * T].indirect(list1[:]))
         nc.vector.tensor_copy(out=v_w[1][:], in_=tab_w[1][:].indirect(list1[:]))
+        def late_page(slot):
+            pages.append(held(slot, [P, T2], F32))
+            nc.vector.memset(pages[-1][:].bitcast(I32), 0)
+
+        late_page("tab_w1")
 
         w1_w, w1_s, w1_bf = {}, {}, {}
-        magnitudes, roots, damp, weighted = {}, {}, {}, {}
+        magnitudes, roots, turned, damp, expected, weighted = {}, {}, {}, {}, {}, {}
 
-        def round_w1(a, b, slot, copy):
-            w1_bf[a, b] = held(slot, [P, PACK * SPAN], BF16)
+        def round_w1(a, b, tile, copy):
+            w1_bf[a, b] = tile
             rounded = w1_bf[a, b][:].rearrange("p (t m j) -> p m t j", t=PACK, j=PACK)
             parts = len(w1_raw[a, b])
             for part, raw in enumerate(w1_raw[a, b]):
@@ -152,7 +159,7 @@ def tile_list_wind_bid_pages_kernel(tc, tab_words, tab_scales, offs, w1, w2_word
                     nc.tensor.matmul_mx(out=accs[jb][:], lhsT=v_w[a][:, cols].bitcast(FP8X4),
                                         lhsT_scale=v_s[a][:, cols],
                                         rhs=w2_w[0][:, 2 * SPAN * a:2 * SPAN * (a + 1)].bitcast(FP4X4),
-                                        rhs_scale=w2_s[:, a * H:a * H + SPAN], start=(a == 0), stop=(a == PASSES - 1))
+                                        rhs_scale=w2_s[0][:, a * SPAN:(a + 1) * SPAN], start=(a == 0), stop=(a == PASSES - 1))
             return accs
 
         def turned_magnitude(accs, t0, t1, slot):
@@ -163,67 +170,86 @@ def tile_list_wind_bid_pages_kernel(tc, tab_words, tab_scales, offs, w1, w2_word
                 nc.scalar.activation(out=tile[:, jb].rearrange("j t p -> j p t"),
                                      in_=accs[jb][:].rearrange("j (p t) -> j p t", t=PACK)[:, :, t0:t1], func=ACT.Abs)
 
-        def turned_root(n, slot):
-            roots[n] = held(slot, [P, 4, P], F32)[:]
+        def turned_root(n, tile):
+            roots[n] = tile
             nc.scalar.activation(out=roots[n], in_=magnitudes[n], func=ACT.Abs_reciprocal_sqrt, bias=1.0)
 
-        def turned_damping(n, number):
-            acc = bank(number)
+        def turn_root(n, number):
+            acc = turned[n] = bank(number)
             for jb in range(4):
                 nc.tensor.transpose(acc[:, jb * P:(jb + 1) * P], roots[n][:, jb, :], ident[:])
-            damp[n] = held("damp%d" % n, [P, S], F32)
-            nc.scalar.activation(out=damp[n][:], in_=acc[:], func=ACT.Square)
 
-        def order_w2():
-            words = held("w1_raw101", [P, PASSES * 2 * SPAN], U8)
-            scales = held("w2_s_late", [P, PASSES * SPAN], U8)
-            nc.vector.tensor_copy(
-                out=words[:].bitcast(U16).rearrange("p (a t m) -> p a t m", a=PASSES, t=PACK),
-                in_=w2_w[1][:].bitcast(U16).rearrange("p (a m t) -> p a t m", a=PASSES, t=PACK))
-            nc.vector.tensor_copy(
-                out=scales[:].rearrange("p (a t m) -> p a t m", a=PASSES, t=PACK),
-                in_=w2_s[:].rearrange("p (a b m t) -> p b a t m", a=PASSES, b=PASSES, t=PACK)[:, 1])
-            return words, scales
+        def square(n, tile=None):
+            damp[n] = held("damp%d" % n, [P, S], F32) if tile is None else tile
+            nc.scalar.activation(out=damp[n][:], in_=turned[n][:], func=ACT.Square)
 
-        def direct_damping(n, words, scales):
-            acc = bank(n % 2)
-            for a in range(PASSES):
-                c0 = a * SPAN + (n % PACK) * P
-                nc.tensor.matmul_mx(out=acc[:], lhsT=words[:, 2 * c0:2 * c0 + 2 * P].bitcast(FP4X4),
-                                    lhsT_scale=scales[:, c0:c0 + P], rhs=v_w[a][:].bitcast(FP8X4),
-                                    rhs_scale=v_s[a][:], start=(a == 0), stop=(a == PASSES - 1))
-            magnitude = held(("w1_raw110", "w1_raw010")[n % 2], [P, S], F32)
-            nc.scalar.activation(out=magnitude[:], in_=acc[:], func=ACT.Abs)
-            root = held("root%d" % (n % 2), [P, S], F32)
-            nc.scalar.activation(out=root[:], in_=magnitude[:], func=ACT.Abs_reciprocal_sqrt, bias=1.0)
-            damp[n] = held("damp%d" % n, [P, S], F32)
-            nc.scalar.activation(out=damp[n][:], in_=root[:], func=ACT.Square)
+        def turned_weights():
+            acc = bank(0)
+            for jb in range(4):
+                nc.tensor.transpose(acc[:, jb * P:(jb + 1) * P], wgs_t[:, jb * P:(jb + 1) * P], ident[:])
+            inverse = held("inverse", [P, 4 * LISTS], F32)
+            picked = held("picked", [P, 4 * LISTS], F32)
+            nc.scalar.activation(out=picked[:], in_=acc[:, 0:BANK:P // LISTS], func=ACT.Abs_reciprocal_sqrt)
+            nc.scalar.activation(out=inverse[:], in_=picked[:], func=ACT.Square)
+            return inverse
 
-        def weigh(n, slot):
+        def late_magnitude(slot):
+            tile = held(slot, [P, 4, PACK, P], F32)
+            for jb in range(4):
+                acc = bank((0, 5, 6, 7)[jb])
+                cols = slice(jb * P, (jb + 1) * P)
+                for a in range(PASSES):
+                    nc.tensor.matmul_mx(out=acc[:], lhsT=v_w[a][:, cols].bitcast(FP8X4),
+                                        lhsT_scale=v_s[a][:, cols],
+                                        rhs=w2_w[1][:, 2 * SPAN * a:2 * SPAN * (a + 1)].bitcast(FP4X4),
+                                        rhs_scale=w2_s[1][:, a * SPAN:(a + 1) * SPAN], start=(a == 0),
+                                        stop=(a == PASSES - 1))
+                nc.scalar.activation(out=tile[:, jb].rearrange("j t p -> j p t"),
+                                     in_=acc[:].rearrange("j (p t) -> j p t", t=PACK), func=ACT.Abs)
+            return tile
+
+        def late_roots(magnitude, inverse, slot):
+            tile = held(slot, [P, 4, PACK, P], F32)
+            width = P // LISTS
+            for jb in range(4):
+                for g in range(LISTS):
+                    factor = inverse[:, LISTS * jb + g:LISTS * jb + g + 1]
+                    nc.scalar.activation(out=tile[:, jb, :, g * width:(g + 1) * width],
+                                         in_=magnitude[:, jb, :, g * width:(g + 1) * width],
+                                         func=ACT.Abs_reciprocal_sqrt, bias=factor, scale=factor)
+            for t in range(PACK):
+                roots[PACK + t] = tile[:, :, t, :]
+
+        def expect(n, number):
             b, t = divmod(n, PACK)
-            acc = bank(2 + n % 2)
+            acc = expected[n] = bank(number)
             for a in range(PASSES):
                 cols = slice(t * P, (t + 1) * P)
                 nc.tensor.matmul_mx(out=acc[:], lhsT=w1_w[a, b][:, cols].bitcast(FP8X4),
                                     lhsT_scale=w1_s[a, b][:, cols], rhs=v_w[a][:].bitcast(FP8X4),
                                     rhs_scale=v_s[a][:], start=(a == 0), stop=(a == PASSES - 1))
-            weighted[n] = held(slot, [P, S], F32)
-            nc.vector.tensor_tensor(out=weighted[n][:], in0=acc[:], in1=wgs_t[:], op=MULT)
+
+        def weigh(n, slot=None):
+            weighted[n] = held(slot or "weighted%d" % n, [P, S], F32)
+            if n < PACK:
+                nc.vector.tensor_tensor(out=weighted[n][:], in0=expected[n][:], in1=wgs_t[:], op=MULT)
+            else:
+                nc.scalar.copy(out=weighted[n][:], in_=expected[n][:])
 
         def scatter(n):
             nc.vector.tensor_tensor(out=pages[n % PAGES][:].indirect(list2[:]), in0=weighted[n][:],
                                     in1=damp[n][:], op=MULT)
 
-        pairs, z_bf = {}, {}
+        sums, pairs, z_bf = {}, {}, {}
         z_w = {(b, h): held("z_w%d%d" % (b, h), [P, HALF], U32) for b in range(PASSES) for h in range(2)}
         z_s = {(b, h): held("z_s%d%d" % (b, h), [P, HALF], U8) for b in range(PASSES) for h in range(2)}
 
-        def sum_pair(b, u):
+        def sum_pair(b, u, banks, chunks=range(CHUNKS)):
             first = PACK * b + 2 * u
             sources = [(0, clim_t[b, u][:, 0, :]), (1, clim_t[b, u][:, 1, :]),
                        (0, pages[first % PAGES]), (1, pages[(first + 1) % PAGES])]
-            for c in range(CHUNKS):
-                acc = bank(6 + c % 2)
+            for c, number in zip(chunks, banks):
+                acc = sums[c] = bank(number)
                 for step, (e, src) in enumerate(sources):
                     for g in range(2):
                         m0 = c * CHUNK + g * P
@@ -231,12 +257,15 @@ def tile_list_wind_bid_pages_kernel(tc, tab_words, tab_scales, offs, w1, w2_word
                         nc.tensor.matmul(out=acc[:, o0:o0 + P], lhsT=src[:, m0:m0 + P], rhs=ident[:],
                                          is_transpose=True, start=(step == 0 and g == 0),
                                          stop=(step == len(sources) - 1 and g == 1))
+
+        def round_pair(b, u):
+            for c in range(CHUNKS):
                 pairs[b, u, c] = held("pairs%d%d" % (u, c), [P, BANK], BF16)
                 nc.scalar.copy(out=pairs[b, u, c][:].rearrange("m (g p e) -> m g p e", g=2, e=2),
-                               in_=acc[:].rearrange("m (g e p) -> m g p e", g=2, e=2))
+                               in_=sums[c][:].rearrange("m (g e p) -> m g p e", g=2, e=2))
 
         def turn_back(c):
-            back = bank(4 + c % 2)
+            back = bank((1, 3, 4, 6)[c])
             for u in (1, 0):
                 for g in range(2):
                     o0 = (2 * g + u) * P
@@ -252,10 +281,10 @@ def tile_list_wind_bid_pages_kernel(tc, tab_words, tab_scales, offs, w1, w2_word
             nc.vector.quantize_mx(out=z_w[b, h][:, cols].bitcast(FP8X4), scales=z_s[b, h][:, cols],
                                   in_=z_bf[b, c][:])
 
-        planes = [held("tab_w%d" % h, [P, PACK, HALF], BF16) for h in range(2)]
+        planes = []
 
         def part_pair(h):
-            back = bank(4 + h)
+            back = bank(3 + h)
             for c in range(2):
                 for g in range(2):
                     o0 = (2 * c + g) * P
@@ -276,22 +305,21 @@ def tile_list_wind_bid_pages_kernel(tc, tab_words, tab_scales, offs, w1, w2_word
             copy(out=z_bf[1, c][:].rearrange("p (m i t) -> p m t i", i=4, t=PACK),
                  in_=planes[h][:, :, half * CHUNK:(half + 1) * CHUNK].rearrange("p t (m i) -> p m t i", i=4))
 
-        w3_bf = held("w3_bf", [P, PASSES * PACK * N], BF16)
         w3_w = held("w3_w", [P, PASSES * N], U32)
         w3_s = held("w3_s", [P, PASSES * N], U8)
 
-        def round_w3(b):
+        def round_w3(w3_bf, b):
             nc.scalar.copy(out=w3_bf[:, b * PACK * N:(b + 1) * PACK * N].rearrange("p (c i j) -> p c j i", i=4, j=PACK),
                            in_=w3_raw[b][:].rearrange("p j (c i) -> p c j i", i=4))
 
-        def quantize_w3():
+        def quantize_w3(w3_bf):
             for c0, c1 in ((0, 512), (512, PASSES * N)):
                 nc.vector.quantize_mx(out=w3_w[:, c0:c1].bitcast(FP8X4), scales=w3_s[:, c0:c1],
                                       in_=w3_bf[:, PACK * c0:PACK * c1])
 
         pieces = [(0, 0, HALF), (1, 0, HALF), (0, HALF, HALF), (1, HALF, HALF), (2, 0, HALF),
                   (2, HALF, CHUNK), (2, HALF + CHUNK, CHUNK)]
-        piece_banks = ((6, 7), (4, 5), (0, 1), (2, 3))
+        piece_banks = ((6, 2), (7, 0), (5, 1), (3, 4))
         ahead = len(piece_banks)
         gate_side, vol_side = 0, 1
         accs = {}
@@ -326,64 +354,86 @@ def tile_list_wind_bid_pages_kernel(tc, tab_words, tab_scales, offs, w1, w2_word
 
         spread = turned_spread()
         turned_magnitude(spread, 0, 1, "magnitude0")
-        turned_root(0, "root2")
-        turned_damping(0, 0)
-        round_w1(0, 0, "w1_bf0", nc.vector.tensor_copy)
+        turned_root(0, held("root0", [P, 4, P], F32)[:])
+        turn_root(0, 0)
+        square(0)
+        round_w1(0, 0, held("w1_bf0", [P, PACK * SPAN], BF16), nc.vector.tensor_copy)
         quantize_w1(0, 0)
-        round_w1(1, 0, "w1_bf1", nc.vector.tensor_copy)
+        round_w1(1, 0, held("w1_bf1", [P, PACK * SPAN], BF16), nc.vector.tensor_copy)
         quantize_w1(1, 0, cuts=(0, P, 2 * P, SPAN))
-        weigh(0, "weighted0")
+        expect(0, 1)
+        weigh(0)
         scatter(0)
-        w2_late = order_w2()
 
-        turned_magnitude(spread, 1, PACK, "root2")
-        turned_root(1, "root1")
-        turned_root(2, "root0")
-        turned_root(3, "root3")
-        turned_damping(1, 1)
-        turned_damping(2, 6)
-        turned_damping(3, 7)
-        weigh(1, "weighted1")
+        turned_magnitude(spread, 1, PACK, "magnitude0")
+        early_roots = held("w1_bf1", [P, PACK - 1, 4, P], F32)
+        for n in range(1, PACK):
+            turned_root(n, early_roots[:, n - 1])
+        turn_root(1, 0)
+        square(1)
+        inverse = turned_weights()
+        expect(1, 2)
+        weigh(1)
         scatter(1)
-        weigh(2, "weighted2")
-        scatter(2)
-        round_w1(0, 1, "root3", nc.scalar.copy)
-        round_w1(1, 1, "w1_bf1", nc.scalar.copy)
+        expect(2, 3)
+        weigh(2)
+        expect(3, 4)
+        weigh(3)
+        late_bf = held("magnitude0", [P, PASSES, PACK * SPAN], BF16)
+        round_w1(0, 1, late_bf[:, 0], nc.scalar.copy)
+        round_w1(1, 1, late_bf[:, 1], nc.scalar.copy)
         quantize_w1(0, 1)
         quantize_w1(1, 1)
-        weigh(3, "w1_bf1")
+        turn_root(2, 1)
+        held_back = held("w1_raw110", [P, 2, S], F32)
+        square(2, held_back[:, 0])
+        scatter(2)
+        turn_root(3, 2)
+        square(3, held_back[:, 1])
         scatter(3)
 
-        direct_damping(4, *w2_late)
-        sum_pair(0, 0)
-        weigh(4, "weighted0")
+        late = late_magnitude("w1_raw010")
+        sum_pair(0, 0, (6, 7), (0, 1))
+        late_roots(late, inverse, "w1_raw000")
+        nc.scalar.activation(out=warm[:, 8:9], in_=roots[7][:, 3, P - 1:P], func=ACT.Sigmoid)
+        for n, number in ((4, 1), (5, 2), (6, 3), (7, 4)):
+            turn_root(n, number)
+        square(4)
+        expect(4, 0)
+        weigh(4)
         scatter(4)
-        direct_damping(5, *w2_late)
-        weigh(5, "weighted1")
+        expect(5, 5)
+        weigh(5)
+        sum_pair(0, 0, (0, 5), (2, 3))
+        square(5)
         scatter(5)
-        sum_pair(0, 1)
-        direct_damping(6, *w2_late)
+        expect(6, 1)
+        expect(7, 2)
+        round_pair(0, 0)
+        sum_pair(0, 1, (6, 7, 0, 5))
+        square(6)
+        weigh(6)
+        scatter(6)
+        square(7)
+        round_pair(0, 1)
+        w3_bf = held("w1_raw000", [P, PASSES * PACK * N], BF16)
+        round_w3(w3_bf, 0)
+        round_w3(w3_bf, 1)
+        quantize_w3(w3_bf)
+        both = held("w1_raw000", [P, 2, PACK, HALF], BF16)
+        planes.extend(both[:, h] for h in range(2))
+        add_plane(6)
         for c in range(CHUNKS):
             turn_back(c)
             quantize_z(0, c)
-        direct_damping(7, *w2_late)
-        weigh(6, "weighted0")
-        scatter(6)
-        add_plane(6)
-        round_w3(0)
-        round_w3(1)
-        quantize_w3()
 
-        weigh(7, "w3_bf")
-        sum_pair(1, 0)
+        weigh(7, "pairs13")
+        sum_pair(1, 0, (7, 0, 5, 1))
+        round_pair(1, 0)
         part_pair(0)
         part_pair(1)
-        nc.scalar.activation(out=warm[:, 8:9], in_=damp[7][:, 0:1], func=ACT.Sigmoid)
         scatter(7)
 
-        late_scales = held("damp7", [P, HALF], U8)
-        nc.vector.tensor_copy(out=late_scales[:].bitcast(I32), in_=z_s[0, 1][:].bitcast(I32))
-        z_s[0, 1] = late_scales
         for i in range(ahead):
             open_piece(i)
             product(i, gate_side, 0)

@@ -68,11 +68,11 @@ def tile_list_wind_bid_pages_kernel(tc, tab_words, tab_scales, offs, w1, w2_word
         w3_raw = [held("w3_raw%d" % b, [P, PACK, N], F32) for b in range(PASSES)]
         w4_w = held("w4_w", [P, PASSES * N], U32)
 
-        def load_scales(tile, src):
+        def load_scales(tile, src, queue=nc.sync):
             view = tile[:].bitcast(I32).rearrange("p (a c) -> p a c", a=PASSES)
             rows = src.bitcast(I32).rearrange("a (q r) c -> r q a c", r=4)
             for r in range(4):
-                nc.sync.dma_start(out=view[r:P:32], in_=rows[r])
+                queue.dma_start(out=view[r:P:32], in_=rows[r])
 
         def load_tab(a):
             nc.sync.dma_start(out=tab_w[a][:].bitcast(I32),
@@ -229,8 +229,8 @@ def tile_list_wind_bid_pages_kernel(tc, tab_words, tab_scales, offs, w1, w2_word
                                     lhsT_scale=w1_s[a, b][:, cols], rhs=v_w[a][:].bitcast(FP8X4),
                                     rhs_scale=v_s[a][:], start=(a == 0), stop=(a == PASSES - 1))
 
-        def weigh(n, slot=None):
-            weighted[n] = held(slot or "weighted%d" % n, [P, S], F32)
+        def weigh(n, tile=None):
+            weighted[n] = held("weighted%d" % n, [P, S], F32) if tile is None else tile
             if n < PACK:
                 nc.vector.tensor_tensor(out=weighted[n][:], in0=expected[n][:], in1=wgs_t[:], op=MULT)
             else:
@@ -258,14 +258,14 @@ def tile_list_wind_bid_pages_kernel(tc, tab_words, tab_scales, offs, w1, w2_word
                                          is_transpose=True, start=(step == 0 and g == 0),
                                          stop=(step == len(sources) - 1 and g == 1))
 
-        def round_pair(b, u):
-            for c in range(CHUNKS):
+        def round_pair(b, u, chunks=range(CHUNKS)):
+            for c in chunks:
                 pairs[b, u, c] = held("pairs%d%d" % (u, c), [P, BANK], BF16)
                 nc.scalar.copy(out=pairs[b, u, c][:].rearrange("m (g p e) -> m g p e", g=2, e=2),
                                in_=sums[c][:].rearrange("m (g e p) -> m g p e", g=2, e=2))
 
         def turn_back(c):
-            back = bank((1, 3, 4, 6)[c])
+            back = bank((1, 3, 4, 0)[c])
             for u in (1, 0):
                 for g in range(2):
                     o0 = (2 * g + u) * P
@@ -283,21 +283,20 @@ def tile_list_wind_bid_pages_kernel(tc, tab_words, tab_scales, offs, w1, w2_word
 
         planes = []
 
-        def part_pair(h):
-            back = bank(3 + h)
-            for c in range(2):
-                for g in range(2):
-                    o0 = (2 * c + g) * P
-                    nc.tensor.transpose(back[:, o0:o0 + P],
-                                        pairs[1, 0, 2 * h + c][:].bitcast(F32)[:, g * P:(g + 1) * P], ident[:])
-            nc.scalar.copy(out=planes[h][:, 0:2, :], in_=back[:].bitcast(BF16).rearrange("p (m e) -> p e m", e=2))
+        def part_pair(c):
+            h, half = divmod(c, 2)
+            back = bank((3, 4, 0, 2)[c])
+            for g in range(2):
+                nc.tensor.transpose(back[:, g * P:(g + 1) * P], pairs[1, 0, c][:].bitcast(F32)[:, g * P:(g + 1) * P],
+                                    ident[:])
+            nc.scalar.copy(out=planes[h][:, 0:2, half * CHUNK:(half + 1) * CHUNK],
+                           in_=back[:, 0:CHUNK].bitcast(BF16).rearrange("p (m e) -> p e m", e=2))
 
-        def add_plane(n):
+        def add_plane(n, m0, width):
             t = n % PACK
-            for h in range(2):
-                cols = slice(h * HALF, (h + 1) * HALF)
-                nc.vector.tensor_tensor(out=planes[h][:, t, :], in0=pages[n % PAGES][:, cols],
-                                        in1=clim_t[1, t // 2][:, t % 2, cols], op=ADD)
+            h, c0 = divmod(m0, HALF)
+            nc.vector.tensor_tensor(out=planes[h][:, t, c0:c0 + width], in0=pages[n % PAGES][:, m0:m0 + width],
+                                    in1=clim_t[1, t // 2][:, t % 2, m0:m0 + width], op=ADD)
 
         def weave(c, copy):
             h, half = divmod(c, 2)
@@ -308,9 +307,9 @@ def tile_list_wind_bid_pages_kernel(tc, tab_words, tab_scales, offs, w1, w2_word
         w3_w = held("w3_w", [P, PASSES * N], U32)
         w3_s = held("w3_s", [P, PASSES * N], U8)
 
-        def round_w3(w3_bf, b):
-            nc.scalar.copy(out=w3_bf[:, b * PACK * N:(b + 1) * PACK * N].rearrange("p (c i j) -> p c j i", i=4, j=PACK),
-                           in_=w3_raw[b][:].rearrange("p j (c i) -> p c j i", i=4))
+        def round_w3(w3_bf, b, copy):
+            copy(out=w3_bf[:, b * PACK * N:(b + 1) * PACK * N].rearrange("p (c i j) -> p c j i", i=4, j=PACK),
+                 in_=w3_raw[b][:].rearrange("p j (c i) -> p c j i", i=4))
 
         def quantize_w3(w3_bf):
             for c0, c1 in ((0, 512), (512, PASSES * N)):
@@ -319,7 +318,7 @@ def tile_list_wind_bid_pages_kernel(tc, tab_words, tab_scales, offs, w1, w2_word
 
         pieces = [(0, 0, HALF), (1, 0, HALF), (0, HALF, HALF), (1, HALF, HALF), (2, 0, HALF),
                   (2, HALF, CHUNK), (2, HALF + CHUNK, CHUNK)]
-        piece_banks = ((6, 2), (7, 0), (5, 1), (3, 4))
+        piece_banks = ((5, 7), (6, 1), (3, 4), (0, 2))
         ahead = len(piece_banks)
         gate_side, vol_side = 0, 1
         accs = {}
@@ -327,25 +326,31 @@ def tile_list_wind_bid_pages_kernel(tc, tab_words, tab_scales, offs, w1, w2_word
         def open_piece(i):
             accs[i] = [bank(number) for number in piece_banks[i % ahead]]
 
-        def product(i, side, b):
+        def product(i, side, b, part=None):
             nt, m0, width = pieces[i]
+            o0, stop = 0, b == PASSES - 1
+            if part is not None:
+                width = width // 2
+                o0, stop = part * width, part == 1
+                m0 = m0 + o0
             words, scales = ((w4_w, w4_s), (w3_w, w3_s))[side]
             cols = slice(b * N + nt * P, b * N + (nt + 1) * P)
             h, c0 = divmod(m0, HALF)
-            nc.tensor.matmul_mx(out=accs[i][side][:, 0:width], lhsT=words[:, cols].bitcast(FP8X4),
+            nc.tensor.matmul_mx(out=accs[i][side][:, o0:o0 + width], lhsT=words[:, cols].bitcast(FP8X4),
                                 lhsT_scale=scales[:, cols], rhs=z_w[b, h][:, c0:c0 + width].bitcast(FP8X4),
-                                rhs_scale=z_s[b, h][:, c0:c0 + width], start=(b == 0), stop=(b == PASSES - 1))
+                                rhs_scale=z_s[b, h][:, c0:c0 + width], start=(b == 0), stop=stop)
 
         def finish(i):
             nt, m0, width = pieces[i]
             if i < ahead:
-                product(i, gate_side, 1)
+                product(i, gate_side, 1, 1)
+                product(i, vol_side, 1, 1)
             else:
                 open_piece(i)
                 product(i, gate_side, 0)
                 product(i, gate_side, 1)
                 product(i, vol_side, 0)
-            product(i, vol_side, 1)
+                product(i, vol_side, 1)
             gate = held("root%d" % (i % 3), [P, width], F32)
             nc.scalar.activation(out=gate[:], in_=accs[i][gate_side][:, 0:width], func=ACT.Sigmoid)
             result = held("damp%d" % i, [P, width], F32)
@@ -376,62 +381,61 @@ def tile_list_wind_bid_pages_kernel(tc, tab_words, tab_scales, offs, w1, w2_word
         weigh(1)
         scatter(1)
         expect(2, 3)
-        weigh(2)
         expect(3, 4)
-        weigh(3)
         late_bf = held("magnitude0", [P, PASSES, PACK * SPAN], BF16)
         round_w1(0, 1, late_bf[:, 0], nc.scalar.copy)
         round_w1(1, 1, late_bf[:, 1], nc.scalar.copy)
         quantize_w1(0, 1)
         quantize_w1(1, 1)
-        turn_root(2, 1)
-        held_back = held("w1_raw110", [P, 2, S], F32)
-        square(2, held_back[:, 0])
+        held_back = held("magnitude0", [P, 2, S], F32)
+        for n in (2, 3):
+            turn_root(n, n - 1)
+            square(n)
+            weigh(n, held_back[:, n - 2])
         scatter(2)
-        turn_root(3, 2)
-        square(3, held_back[:, 1])
         scatter(3)
 
-        late = late_magnitude("w1_raw010")
-        sum_pair(0, 0, (6, 7), (0, 1))
+        late = late_magnitude("w1_raw110")
+        sum_pair(0, 0, (0, 5), (0, 1))
         late_roots(late, inverse, "w1_raw000")
-        nc.scalar.activation(out=warm[:, 8:9], in_=roots[7][:, 3, P - 1:P], func=ACT.Sigmoid)
         for n, number in ((4, 1), (5, 2), (6, 3), (7, 4)):
             turn_root(n, number)
         square(4)
-        expect(4, 0)
+        expect(4, 7)
         weigh(4)
         scatter(4)
-        expect(5, 5)
+        expect(5, 6)
         weigh(5)
-        sum_pair(0, 0, (0, 5), (2, 3))
+        sum_pair(0, 0, (7, 6), (2, 3))
         square(5)
         scatter(5)
         expect(6, 1)
         expect(7, 2)
+        nc.scalar.activation(out=warm[:, 8:9], in_=damp[5][:, 0:1], func=ACT.Sigmoid)
         round_pair(0, 0)
-        sum_pair(0, 1, (6, 7, 0, 5))
+        sum_pair(0, 1, (0, 5, 7, 6))
         square(6)
         weigh(6)
         scatter(6)
         square(7)
         round_pair(0, 1)
         w3_bf = held("w1_raw000", [P, PASSES * PACK * N], BF16)
-        round_w3(w3_bf, 0)
-        round_w3(w3_bf, 1)
+        round_w3(w3_bf, 0, nc.scalar.copy)
+        round_w3(w3_bf, 1, nc.vector.tensor_copy)
         quantize_w3(w3_bf)
         both = held("w1_raw000", [P, 2, PACK, HALF], BF16)
         planes.extend(both[:, h] for h in range(2))
-        add_plane(6)
+        for h in range(2):
+            add_plane(6, h * HALF, HALF)
         for c in range(CHUNKS):
             turn_back(c)
             quantize_z(0, c)
 
-        weigh(7, "pairs13")
-        sum_pair(1, 0, (7, 0, 5, 1))
+        weigh(7, held("pairs13", [P, S], F32))
+        sum_pair(1, 0, (5, 7, 6, 1))
         round_pair(1, 0)
-        part_pair(0)
-        part_pair(1)
+        for c in range(CHUNKS):
+            part_pair(c)
         scatter(7)
 
         for i in range(ahead):
@@ -439,9 +443,16 @@ def tile_list_wind_bid_pages_kernel(tc, tab_words, tab_scales, offs, w1, w2_word
             product(i, gate_side, 0)
             product(i, vol_side, 0)
 
-        add_plane(7)
+        for c in (0, 1, 2, 3):
+            add_plane(7, c * CHUNK, CHUNK)
         for c in range(CHUNKS):
-            weave(c, nc.vector.tensor_copy if c < CHUNKS // 2 else nc.scalar.copy)
+            weave(c, (nc.vector.tensor_copy, nc.vector.tensor_copy, nc.scalar.copy, nc.scalar.copy)[c])
             quantize_z(1, c)
-        for i in range(len(pieces)):
+            for i in (2 * (c // 2), 2 * (c // 2) + 1):
+                if c % 2 == 0:
+                    product(i, gate_side, 1, 0)
+                    product(i, vol_side, 1, 0)
+                else:
+                    finish(i)
+        for i in range(ahead, len(pieces)):
             finish(i)

@@ -138,11 +138,11 @@ def tile_list_wind_bid_pages_kernel(tc, tab_words, tab_scales, offs, w1, w2_word
 
         def round_w1(a, b, tile, copy):
             w1_bf[a, b] = tile
-            rounded = w1_bf[a, b][:].rearrange("p (t m j) -> p m t j", t=PACK, j=PACK)
+            rounded = w1_bf[a, b][:].rearrange("p (t m u e) -> p m u t e", t=PACK, u=2, e=2)
             parts = len(w1_raw[a, b])
             for part, raw in enumerate(w1_raw[a, b]):
                 copy(out=rounded[:, part * P // parts:(part + 1) * P // parts],
-                     in_=raw[:].rearrange("p j (m t) -> p m t j", t=PACK))
+                     in_=raw[:].rearrange("p (u e) (m t) -> p m u t e", t=PACK, e=2))
 
         def quantize_w1(a, b, cuts=(0, SPAN)):
             w1_w[a, b] = held("w1_w%d%d" % (a, b), [P, SPAN], U32)
@@ -167,8 +167,8 @@ def tile_list_wind_bid_pages_kernel(tc, tab_words, tab_scales, offs, w1, w2_word
             for t in range(t0, t1):
                 magnitudes[t] = tile[:, :, t - t0, :]
             for jb in range(4):
-                nc.scalar.activation(out=tile[:, jb].rearrange("j t p -> j p t"),
-                                     in_=accs[jb][:].rearrange("j (p t) -> j p t", t=PACK)[:, :, t0:t1], func=ACT.Abs)
+                nc.scalar.activation(out=tile[:, jb], func=ACT.Abs,
+                                     in_=accs[jb][:].rearrange("j (p t) -> j t p", t=PACK)[:, t0:t1])
 
         def turned_root(n, tile):
             roots[n] = tile
@@ -204,8 +204,7 @@ def tile_list_wind_bid_pages_kernel(tc, tab_words, tab_scales, offs, w1, w2_word
                                         rhs=w2_w[1][:, 2 * SPAN * a:2 * SPAN * (a + 1)].bitcast(FP4X4),
                                         rhs_scale=w2_s[1][:, a * SPAN:(a + 1) * SPAN], start=(a == 0),
                                         stop=(a == PASSES - 1))
-                nc.scalar.activation(out=tile[:, jb].rearrange("j t p -> j p t"),
-                                     in_=acc[:].rearrange("j (p t) -> j p t", t=PACK), func=ACT.Abs)
+                nc.scalar.activation(out=tile[:, jb], in_=acc[:].rearrange("j (p t) -> j t p", t=PACK), func=ACT.Abs)
             return tile
 
         def late_roots(magnitude, inverse, slot):

@@ -240,7 +240,7 @@ def tile_list_wind_bid_pages_kernel(tc, tab_words, tab_scales, offs, w1, w2_word
                                     in1=damp[n][:], op=MULT)
 
         sums, pairs, z_bf = {}, {}, {}
-        z_w = {(b, h): held("z_w%d%d" % (b, h), [P, HALF], U32) for b in range(PASSES) for h in range(2)}
+        z_w = {(b, h): held("z_w%d%d" % (b, h), [P, HALF], U32) for b, h in ((0, 0), (1, 0), (1, 1))}
         z_s = {(b, h): held("z_s%d%d" % (b, h), [P, HALF], U8) for b in range(PASSES) for h in range(2)}
 
         def sum_pair(b, u, banks, chunks=range(CHUNKS)):
@@ -420,22 +420,26 @@ def tile_list_wind_bid_pages_kernel(tc, tab_words, tab_scales, offs, w1, w2_word
         round_pair(0, 1)
         w3_bf = held("w1_raw000", [P, PASSES * PACK * N], BF16)
         round_w3(w3_bf, 0, nc.scalar.copy)
-        round_w3(w3_bf, 1, nc.vector.tensor_copy)
+        round_w3(w3_bf, 1, nc.scalar.copy)
         quantize_w3(w3_bf)
         both = held("w1_raw000", [P, 2, PACK, HALF], BF16)
         planes.extend(both[:, h] for h in range(2))
         for h in range(2):
             add_plane(6, h * HALF, HALF)
-        for c in range(CHUNKS):
+        for c in (0, 1):
             turn_back(c)
             quantize_z(0, c)
-
-        weigh(7, held("pairs13", [P, S], F32))
+        weigh(7, held("pairs11", [P, S], F32))
+        for c in (2, 3):
+            turn_back(c)
         sum_pair(1, 0, (5, 7, 6, 1))
         round_pair(1, 0)
         for c in range(CHUNKS):
             part_pair(c)
         scatter(7)
+        z_w[0, 1] = held("damp7", [P, HALF], U32)
+        quantize_z(0, 2)
+        quantize_z(0, 3)
 
         for i in range(ahead):
             open_piece(i)

@@ -23,15 +23,17 @@ PACK = 4
 SPAN = P * PACK
 PASSES = 2
 BANK = 512
+BLOCKS = S // P
+LISTS = 8
+GROUP = P // LISTS
 PAGES = 6
 CHUNK = 256
 CHUNKS = T2 // CHUNK
-LISTS = 8
 HALF = T2 // 2
 
 
 def tile_list_wind_bid_pages_kernel(tc, tab_words, tab_scales, offs, w1, w2_words, w2_scales, offs2, wgs,
-                                              clim, w3, w4_words, w4_scales, out):
+                                                 clim, w3, w4_words, w4_scales, out):
     nc = tc.nc
     with ExitStack() as ctx:
         keep = ctx.enter_context(tc.tile_pool(name="keep", bufs=1))
@@ -40,11 +42,15 @@ def tile_list_wind_bid_pages_kernel(tc, tab_words, tab_scales, offs, w1, w2_word
         def held(slot, shape, dtype):
             return keep.tile(shape, dtype, name=slot, align_bytes=64)
 
-        def bank(number):
-            return psum.tile([P, BANK], F32, name="bank%d" % number, tag="bank%d" % number)
+        banks = {("free", i): i for i in range(8)}
 
-        list1 = keep.tile([P, S // 16], U16, name="list1")
-        list2 = keep.tile([P, S // 16], U16, name="list2")
+        def bank(step, after):
+            banks[step] = banks[after]
+            name = "bank%d" % banks[step]
+            return psum.tile([P, BANK], F32, name=name, tag=name)
+
+        list1 = keep.tile([P, S // GROUP], U16, name="list1")
+        list2 = keep.tile([P, S // GROUP], U16, name="list2")
         tab_s = held("tab_s", [P, PASSES * T], U8)
         w2_s = [held("w2_s%d" % b, [P, PASSES * SPAN], U8) for b in range(PASSES)]
         w4_s = held("w4_s", [P, PASSES * N], U8)
@@ -53,9 +59,13 @@ def tile_list_wind_bid_pages_kernel(tc, tab_words, tab_scales, offs, w1, w2_word
         ident = held("ident", [P, P], F32)
         nc.vector.memset(ident[:], 0.0)
         make_identity(nc, ident[:], nomemset=True)
-        pages = [held("page%d" % n, [P, T2], F32) for n in range(PAGES - 1)]
+        pages = [held("page%d" % n, [P, T2], F32) for n in range(2)]
         for tile in pages:
             nc.vector.memset(tile[:].bitcast(I32), 0)
+
+        def add_page(slot):
+            pages.append(held(slot, [P, T2], F32))
+            nc.gpsimd.memset(pages[-1][:].bitcast(I32), 0)
 
         warm = held("warm", [P, 16], F32)
         nc.scalar.activation(out=warm[:, 0:1], in_=ident[:, 0:1], func=ACT.Abs_reciprocal_sqrt, bias=1.0)
@@ -68,11 +78,11 @@ def tile_list_wind_bid_pages_kernel(tc, tab_words, tab_scales, offs, w1, w2_word
         w3_raw = [held("w3_raw%d" % b, [P, PACK, N], F32) for b in range(PASSES)]
         w4_w = held("w4_w", [P, PASSES * N], U32)
 
-        def load_scales(tile, src, queue=nc.sync):
+        def load_scales(tile, src):
             view = tile[:].bitcast(I32).rearrange("p (a c) -> p a c", a=PASSES)
             rows = src.bitcast(I32).rearrange("a (q r) c -> r q a c", r=4)
             for r in range(4):
-                queue.dma_start(out=view[r:P:32], in_=rows[r])
+                nc.sync.dma_start(out=view[r:P:32], in_=rows[r])
 
         def load_tab(a):
             nc.sync.dma_start(out=tab_w[a][:].bitcast(I32),
@@ -86,10 +96,13 @@ def tile_list_wind_bid_pages_kernel(tc, tab_words, tab_scales, offs, w1, w2_word
                 rows = w1[SPAN * a:SPAN * (a + 1), c0:c0 + width]
                 nc.sync.dma_start(out=raw[:], in_=rows.rearrange("(p j) c -> p j c", j=PACK))
 
-        def load_w2(b):
+        def load_w2_words(b):
             words = w2_words[:, :, 2 * SPAN * b:2 * SPAN * (b + 1)]
             nc.sync.dma_start(out=w2_w[b][:].bitcast(I32).rearrange("p (a c) -> p a c", a=PASSES),
                               in_=words.bitcast(I32).rearrange("a p c -> p a c"))
+
+        def load_w2_scales(b):
+            load_scales(w2_s[b], w2_scales[:, :, SPAN * b:SPAN * (b + 1)])
 
         def load_clim(b):
             rows = clim[SPAN * b:SPAN * (b + 1), :].rearrange("(p j) c -> p j c", j=PACK)
@@ -97,21 +110,22 @@ def tile_list_wind_bid_pages_kernel(tc, tab_words, tab_scales, offs, w1, w2_word
                 nc.sync.dma_start(out=clim_t[b, u][:], in_=rows[:, 2 * u:2 * u + 2, :])
 
         def load_w3(b):
-            nc.sync.dma_start(out=w3_raw[b][:], in_=w3[SPAN * b:SPAN * (b + 1), :].rearrange("(p j) c -> p j c", j=PACK))
+            rows = w3[SPAN * b:SPAN * (b + 1), :]
+            nc.sync.dma_start(out=w3_raw[b][:], in_=rows.rearrange("(p j) c -> p j c", j=PACK))
 
         nc.sync.dma_start(list1[:], offs)
         load_tab(0)
         load_scales(tab_s, tab_scales)
-        load_w2(0)
+        load_w2_words(0)
         load_tab(1)
-        load_scales(w2_s[0], w2_scales[:, :, 0:SPAN])
+        load_w2_scales(0)
         load_w1(0, 0)
         load_w1(1, 0, parts=2)
         nc.sync.dma_start(out=wgs_t[:], in_=wgs)
         nc.sync.dma_start(list2[:], offs2)
         load_w1(0, 1)
-        load_w2(1)
-        load_scales(w2_s[1], w2_scales[:, :, SPAN:H])
+        load_w2_words(1)
+        load_w2_scales(1)
         load_w1(1, 1)
         load_clim(0)
         load_w3(0)
@@ -127,113 +141,102 @@ def tile_list_wind_bid_pages_kernel(tc, tab_words, tab_scales, offs, w1, w2_word
         for a in range(PASSES):
             nc.vector.tensor_copy(out=v_s[a][:], in_=tab_s[:, a * T:(a + 1) * T].indirect(list1[:]))
         nc.vector.tensor_copy(out=v_w[1][:], in_=tab_w[1][:].indirect(list1[:]))
-        def late_page(slot):
-            pages.append(held(slot, [P, T2], F32))
-            nc.vector.memset(pages[-1][:].bitcast(I32), 0)
-
-        late_page("tab_w1")
 
         w1_w, w1_s, w1_bf = {}, {}, {}
         magnitudes, roots, turned, damp, expected, weighted = {}, {}, {}, {}, {}, {}
 
         def round_w1(a, b, tile, copy):
             w1_bf[a, b] = tile
-            rounded = w1_bf[a, b][:].rearrange("p (t m u e) -> p m u t e", t=PACK, u=2, e=2)
+            rounded = tile[:].rearrange("p (t m u e) -> p m u t e", t=PACK, u=2, e=2)
             parts = len(w1_raw[a, b])
             for part, raw in enumerate(w1_raw[a, b]):
                 copy(out=rounded[:, part * P // parts:(part + 1) * P // parts],
                      in_=raw[:].rearrange("p (u e) (m t) -> p m u t e", t=PACK, e=2))
 
-        def quantize_w1(a, b, cuts=(0, SPAN)):
-            w1_w[a, b] = held("w1_w%d%d" % (a, b), [P, SPAN], U32)
-            w1_s[a, b] = held("w1_s%d%d" % (a, b), [P, SPAN], U8)
-            for c0, c1 in zip(cuts, cuts[1:]):
-                nc.vector.quantize_mx(out=w1_w[a, b][:, c0:c1].bitcast(FP8X4), scales=w1_s[a, b][:, c0:c1],
-                                      in_=w1_bf[a, b][:, PACK * c0:PACK * c1])
+        def quantize_w1(a, b, t0, t1, slot=None):
+            name = "%d%d%d" % (a, b, t0)
+            words = held(slot or "w1_w" + name, [P, (t1 - t0) * P], U32)
+            scales = held("w1_s" + name, [P, (t1 - t0) * P], U8)
+            nc.vector.quantize_mx(out=words[:].bitcast(FP8X4), scales=scales[:],
+                                  in_=w1_bf[a, b][:, SPAN * t0:SPAN * t1])
+            for t in range(t0, t1):
+                cols = slice((t - t0) * P, (t - t0 + 1) * P)
+                w1_w[a, b, t], w1_s[a, b, t] = words[:, cols], scales[:, cols]
 
-        def turned_spread():
-            accs = [bank(4 + jb) for jb in range(4)]
-            for a in range(PASSES):
-                for jb in range(4):
-                    cols = slice(jb * P, (jb + 1) * P)
-                    nc.tensor.matmul_mx(out=accs[jb][:], lhsT=v_w[a][:, cols].bitcast(FP8X4),
-                                        lhsT_scale=v_s[a][:, cols],
-                                        rhs=w2_w[0][:, 2 * SPAN * a:2 * SPAN * (a + 1)].bitcast(FP4X4),
-                                        rhs_scale=w2_s[0][:, a * SPAN:(a + 1) * SPAN], start=(a == 0), stop=(a == PASSES - 1))
-            return accs
+        def spread_pass(acc, a, b, jb):
+            cols = slice(jb * P, (jb + 1) * P)
+            nc.tensor.matmul_mx(out=acc[:], lhsT=v_w[a][:, cols].bitcast(FP8X4), lhsT_scale=v_s[a][:, cols],
+                                rhs=w2_w[b][:, 2 * SPAN * a:2 * SPAN * (a + 1)].bitcast(FP4X4),
+                                rhs_scale=w2_s[b][:, a * SPAN:(a + 1) * SPAN], start=(a == 0), stop=(a == PASSES - 1))
 
-        def turned_magnitude(accs, t0, t1, slot):
-            tile = held(slot, [P, 4, t1 - t0, P], F32)
+        def take_magnitude(tile, acc, t0, t1):
+            nc.scalar.activation(out=tile, in_=acc[:].rearrange("j (p t) -> j t p", t=PACK)[:, t0:t1], func=ACT.Abs)
+
+        def early_magnitudes(accs, t0, t1):
+            tile = held("magnitude", [P, BLOCKS, t1 - t0, P], F32)
             for t in range(t0, t1):
                 magnitudes[t] = tile[:, :, t - t0, :]
-            for jb in range(4):
-                nc.scalar.activation(out=tile[:, jb], func=ACT.Abs,
-                                     in_=accs[jb][:].rearrange("j (p t) -> j t p", t=PACK)[:, t0:t1])
+            for jb in range(BLOCKS):
+                take_magnitude(tile[:, jb], accs[jb], t0, t1)
 
-        def turned_root(n, tile):
+        def early_root(n, tile):
             roots[n] = tile
-            nc.scalar.activation(out=roots[n], in_=magnitudes[n], func=ACT.Abs_reciprocal_sqrt, bias=1.0)
+            nc.scalar.activation(out=tile, in_=magnitudes[n], func=ACT.Abs_reciprocal_sqrt, bias=1.0)
 
-        def turn_root(n, number):
-            acc = turned[n] = bank(number)
-            for jb in range(4):
-                nc.tensor.transpose(acc[:, jb * P:(jb + 1) * P], roots[n][:, jb, :], ident[:])
-
-        def square(n, tile=None):
-            damp[n] = held("damp%d" % n, [P, S], F32) if tile is None else tile
-            nc.scalar.activation(out=damp[n][:], in_=turned[n][:], func=ACT.Square)
-
-        def turned_weights():
-            acc = bank(0)
-            for jb in range(4):
+        def inverse_weights(after):
+            acc = bank("wgs", after)
+            for jb in range(BLOCKS):
                 nc.tensor.transpose(acc[:, jb * P:(jb + 1) * P], wgs_t[:, jb * P:(jb + 1) * P], ident[:])
-            inverse = held("inverse", [P, 4 * LISTS], F32)
-            picked = held("picked", [P, 4 * LISTS], F32)
-            nc.scalar.activation(out=picked[:], in_=acc[:, 0:BANK:P // LISTS], func=ACT.Abs_reciprocal_sqrt)
+            inverse = held("inverse", [P, BLOCKS * LISTS], F32)
+            picked = held("picked", [P, BLOCKS * LISTS], F32)
+            nc.scalar.activation(out=picked[:], in_=acc[:, 0:BANK:GROUP], func=ACT.Abs_reciprocal_sqrt)
             nc.scalar.activation(out=inverse[:], in_=picked[:], func=ACT.Square)
             return inverse
 
-        def late_magnitude(slot):
-            tile = held(slot, [P, 4, PACK, P], F32)
-            for jb in range(4):
-                acc = bank((0, 5, 6, 7)[jb])
-                cols = slice(jb * P, (jb + 1) * P)
+        def late_magnitudes(afters, slot):
+            tile = held(slot, [P, BLOCKS, PACK, P], F32)
+            for jb in range(BLOCKS):
+                acc = bank(("late", jb), afters[jb])
                 for a in range(PASSES):
-                    nc.tensor.matmul_mx(out=acc[:], lhsT=v_w[a][:, cols].bitcast(FP8X4),
-                                        lhsT_scale=v_s[a][:, cols],
-                                        rhs=w2_w[1][:, 2 * SPAN * a:2 * SPAN * (a + 1)].bitcast(FP4X4),
-                                        rhs_scale=w2_s[1][:, a * SPAN:(a + 1) * SPAN], start=(a == 0),
-                                        stop=(a == PASSES - 1))
-                nc.scalar.activation(out=tile[:, jb], in_=acc[:].rearrange("j (p t) -> j t p", t=PACK), func=ACT.Abs)
+                    spread_pass(acc, a, 1, jb)
+                take_magnitude(tile[:, jb], acc, 0, PACK)
             return tile
 
         def late_roots(magnitude, inverse, slot):
-            tile = held(slot, [P, 4, PACK, P], F32)
-            width = P // LISTS
-            for jb in range(4):
+            tile = held(slot, [P, BLOCKS, PACK, P], F32)
+            for jb in range(BLOCKS):
                 for g in range(LISTS):
                     factor = inverse[:, LISTS * jb + g:LISTS * jb + g + 1]
-                    nc.scalar.activation(out=tile[:, jb, :, g * width:(g + 1) * width],
-                                         in_=magnitude[:, jb, :, g * width:(g + 1) * width],
+                    places = slice(g * GROUP, (g + 1) * GROUP)
+                    nc.scalar.activation(out=tile[:, jb, :, places], in_=magnitude[:, jb, :, places],
                                          func=ACT.Abs_reciprocal_sqrt, bias=factor, scale=factor)
             for t in range(PACK):
                 roots[PACK + t] = tile[:, :, t, :]
 
-        def expect(n, number):
-            b, t = divmod(n, PACK)
-            acc = expected[n] = bank(number)
-            for a in range(PASSES):
-                cols = slice(t * P, (t + 1) * P)
-                nc.tensor.matmul_mx(out=acc[:], lhsT=w1_w[a, b][:, cols].bitcast(FP8X4),
-                                    lhsT_scale=w1_s[a, b][:, cols], rhs=v_w[a][:].bitcast(FP8X4),
-                                    rhs_scale=v_s[a][:], start=(a == 0), stop=(a == PASSES - 1))
+        def turn_root(n, after):
+            acc = turned[n] = bank(("root", n), after)
+            for jb in range(BLOCKS):
+                nc.tensor.transpose(acc[:, jb * P:(jb + 1) * P], roots[n][:, jb, :], ident[:])
 
-        def weigh(n, tile=None):
-            weighted[n] = held("weighted%d" % n, [P, S], F32) if tile is None else tile
-            if n < PACK:
-                nc.vector.tensor_tensor(out=weighted[n][:], in0=expected[n][:], in1=wgs_t[:], op=MULT)
-            else:
-                nc.scalar.copy(out=weighted[n][:], in_=expected[n][:])
+        def square(n):
+            damp[n] = held("damp%d" % n, [P, S], F32)
+            nc.scalar.activation(out=damp[n][:], in_=turned[n][:], func=ACT.Square)
+
+        def expect(n, after):
+            b, t = divmod(n, PACK)
+            acc = expected[n] = bank(("a", n), after)
+            for a in range(PASSES):
+                nc.tensor.matmul_mx(out=acc[:], lhsT=w1_w[a, b, t].bitcast(FP8X4), lhsT_scale=w1_s[a, b, t],
+                                    rhs=v_w[a][:].bitcast(FP8X4), rhs_scale=v_s[a][:],
+                                    start=(a == 0), stop=(a == PASSES - 1))
+
+        def weigh(n, tile):
+            weighted[n] = tile
+            nc.vector.tensor_tensor(out=tile[:], in0=expected[n][:], in1=wgs_t[:], op=MULT)
+
+        def copy_out(n, slot):
+            weighted[n] = held(slot, [P, S], F32)
+            nc.scalar.copy(out=weighted[n][:], in_=expected[n][:])
 
         def scatter(n):
             nc.vector.tensor_tensor(out=pages[n % PAGES][:].indirect(list2[:]), in0=weighted[n][:],
@@ -243,28 +246,27 @@ def tile_list_wind_bid_pages_kernel(tc, tab_words, tab_scales, offs, w1, w2_word
         z_w = {(b, h): held("z_w%d%d" % (b, h), [P, HALF], U32) for b, h in ((0, 0), (1, 0), (1, 1))}
         z_s = {(b, h): held("z_s%d%d" % (b, h), [P, HALF], U8) for b in range(PASSES) for h in range(2)}
 
-        def sum_pair(b, u, banks, chunks=range(CHUNKS)):
+        def sum_pair(b, u, c, after):
             first = PACK * b + 2 * u
             sources = [(0, clim_t[b, u][:, 0, :]), (1, clim_t[b, u][:, 1, :]),
                        (0, pages[first % PAGES]), (1, pages[(first + 1) % PAGES])]
-            for c, number in zip(chunks, banks):
-                acc = sums[c] = bank(number)
-                for step, (e, src) in enumerate(sources):
-                    for g in range(2):
-                        m0 = c * CHUNK + g * P
-                        o0 = (2 * g + e) * P
-                        nc.tensor.matmul(out=acc[:, o0:o0 + P], lhsT=src[:, m0:m0 + P], rhs=ident[:],
-                                         is_transpose=True, start=(step == 0 and g == 0),
-                                         stop=(step == len(sources) - 1 and g == 1))
+            acc = sums[c] = bank(("sum", b, u, c), after)
+            for step, (e, src) in enumerate(sources):
+                for g in range(2):
+                    m0 = c * CHUNK + g * P
+                    o0 = (2 * g + e) * P
+                    nc.tensor.matmul(out=acc[:, o0:o0 + P], lhsT=src[:, m0:m0 + P], rhs=ident[:],
+                                     is_transpose=True, start=(step == 0 and g == 0),
+                                     stop=(step == len(sources) - 1 and g == 1))
 
-        def round_pair(b, u, chunks=range(CHUNKS)):
-            for c in chunks:
+        def round_pair(b, u):
+            for c in range(CHUNKS):
                 pairs[b, u, c] = held("pairs%d%d" % (u, c), [P, BANK], BF16)
                 nc.scalar.copy(out=pairs[b, u, c][:].rearrange("m (g p e) -> m g p e", g=2, e=2),
                                in_=sums[c][:].rearrange("m (g e p) -> m g p e", g=2, e=2))
 
-        def turn_back(c):
-            back = bank((1, 3, 4, 0)[c])
+        def turn_back(c, after):
+            back = bank(("back", c), after)
             for u in (1, 0):
                 for g in range(2):
                     o0 = (2 * g + u) * P
@@ -275,187 +277,187 @@ def tile_list_wind_bid_pages_kernel(tc, tab_words, tab_scales, offs, w1, w2_word
                            in_=back[:].rearrange("p (g u m) -> p g m u", g=2, u=2))
 
         def quantize_z(b, c):
-            h, half = divmod(c, 2)
-            cols = slice(half * CHUNK, (half + 1) * CHUNK)
+            h, side = divmod(c, 2)
+            cols = slice(side * CHUNK, (side + 1) * CHUNK)
             nc.vector.quantize_mx(out=z_w[b, h][:, cols].bitcast(FP8X4), scales=z_s[b, h][:, cols],
                                   in_=z_bf[b, c][:])
 
-        planes = []
-
-        def part_pair(c):
-            h, half = divmod(c, 2)
-            back = bank((3, 4, 0, 2)[c])
+        def part_pair(planes, c, after):
+            h, side = divmod(c, 2)
+            back = bank(("part", c), after)
             for g in range(2):
                 nc.tensor.transpose(back[:, g * P:(g + 1) * P], pairs[1, 0, c][:].bitcast(F32)[:, g * P:(g + 1) * P],
                                     ident[:])
-            nc.scalar.copy(out=planes[h][:, 0:2, half * CHUNK:(half + 1) * CHUNK],
+            nc.scalar.copy(out=planes[:, h, 0:2, side * CHUNK:(side + 1) * CHUNK],
                            in_=back[:, 0:CHUNK].bitcast(BF16).rearrange("p (m e) -> p e m", e=2))
 
-        def add_plane(n, m0, width):
+        def add_plane(planes, n, m0, width):
             t = n % PACK
             h, c0 = divmod(m0, HALF)
-            nc.vector.tensor_tensor(out=planes[h][:, t, c0:c0 + width], in0=pages[n % PAGES][:, m0:m0 + width],
+            nc.vector.tensor_tensor(out=planes[:, h, t, c0:c0 + width], in0=pages[n % PAGES][:, m0:m0 + width],
                                     in1=clim_t[1, t // 2][:, t % 2, m0:m0 + width], op=ADD)
 
-        def weave(c, copy):
-            h, half = divmod(c, 2)
+        def weave(planes, c, copy):
+            h, side = divmod(c, 2)
             z_bf[1, c] = held("z_bf%d" % c, [P, PACK * CHUNK], BF16)
             copy(out=z_bf[1, c][:].rearrange("p (m i t) -> p m t i", i=4, t=PACK),
-                 in_=planes[h][:, :, half * CHUNK:(half + 1) * CHUNK].rearrange("p t (m i) -> p m t i", i=4))
+                 in_=planes[:, h, :, side * CHUNK:(side + 1) * CHUNK].rearrange("p t (m i) -> p m t i", i=4))
 
         w3_w = held("w3_w", [P, PASSES * N], U32)
         w3_s = held("w3_s", [P, PASSES * N], U8)
 
-        def round_w3(w3_bf, b, copy):
-            copy(out=w3_bf[:, b * PACK * N:(b + 1) * PACK * N].rearrange("p (c i j) -> p c j i", i=4, j=PACK),
-                 in_=w3_raw[b][:].rearrange("p j (c i) -> p c j i", i=4))
-
-        def quantize_w3(w3_bf):
+        def prepare_w3(slot):
+            w3_bf = held(slot, [P, PASSES * PACK * N], BF16)
+            for b in range(PASSES):
+                rounded = w3_bf[:, b * PACK * N:(b + 1) * PACK * N]
+                nc.scalar.copy(out=rounded.rearrange("p (c i j) -> p c j i", i=4, j=PACK),
+                               in_=w3_raw[b][:].rearrange("p j (c i) -> p c j i", i=4))
             for c0, c1 in ((0, 512), (512, PASSES * N)):
                 nc.vector.quantize_mx(out=w3_w[:, c0:c1].bitcast(FP8X4), scales=w3_s[:, c0:c1],
                                       in_=w3_bf[:, PACK * c0:PACK * c1])
 
         pieces = [(0, 0, HALF), (1, 0, HALF), (0, HALF, HALF), (1, HALF, HALF), (2, 0, HALF),
                   (2, HALF, CHUNK), (2, HALF + CHUNK, CHUNK)]
-        piece_banks = ((5, 7), (6, 1), (3, 4), (0, 2))
-        ahead = len(piece_banks)
+        ahead = 4
         gate_side, vol_side = 0, 1
         accs = {}
 
-        def open_piece(i):
-            accs[i] = [bank(number) for number in piece_banks[i % ahead]]
+        def open_piece(i, afters):
+            accs[i] = [bank(("piece", i, side), afters[side]) for side in (gate_side, vol_side)]
 
-        def product(i, side, b, part=None):
-            nt, m0, width = pieces[i]
-            o0, stop = 0, b == PASSES - 1
-            if part is not None:
-                width = width // 2
-                o0, stop = part * width, part == 1
-                m0 = m0 + o0
+        def product(i, side, b, o0, width, stop):
+            nt, m0 = pieces[i][0:2]
             words, scales = ((w4_w, w4_s), (w3_w, w3_s))[side]
             cols = slice(b * N + nt * P, b * N + (nt + 1) * P)
-            h, c0 = divmod(m0, HALF)
+            h, c0 = divmod(m0 + o0, HALF)
             nc.tensor.matmul_mx(out=accs[i][side][:, o0:o0 + width], lhsT=words[:, cols].bitcast(FP8X4),
                                 lhsT_scale=scales[:, cols], rhs=z_w[b, h][:, c0:c0 + width].bitcast(FP8X4),
                                 rhs_scale=z_s[b, h][:, c0:c0 + width], start=(b == 0), stop=stop)
 
         def finish(i):
             nt, m0, width = pieces[i]
-            if i < ahead:
-                product(i, gate_side, 1, 1)
-                product(i, vol_side, 1, 1)
-            else:
-                open_piece(i)
-                product(i, gate_side, 0)
-                product(i, gate_side, 1)
-                product(i, vol_side, 0)
-                product(i, vol_side, 1)
             gate = held("root%d" % (i % 3), [P, width], F32)
             nc.scalar.activation(out=gate[:], in_=accs[i][gate_side][:, 0:width], func=ACT.Sigmoid)
             result = held("damp%d" % i, [P, width], F32)
             nc.vector.tensor_tensor(out=result[:], in0=accs[i][vol_side][:, 0:width], in1=gate[:], op=MULT)
             nc.sync.dma_start(out=out[nt * P:(nt + 1) * P, m0:m0 + width], in_=result[:])
 
-        spread = turned_spread()
-        turned_magnitude(spread, 0, 1, "magnitude0")
-        turned_root(0, held("root0", [P, 4, P], F32)[:])
-        turn_root(0, 0)
+        spread = [bank(("early", jb), ("free", 4 + jb)) for jb in range(BLOCKS)]
+        for a in range(PASSES):
+            for jb in range(BLOCKS):
+                spread_pass(spread[jb], a, 0, jb)
+        early_magnitudes(spread, 0, 1)
+        early_root(0, held("root0", [P, BLOCKS, P], F32)[:])
+        turn_root(0, ("free", 0))
         square(0)
-        round_w1(0, 0, held("w1_bf0", [P, PACK * SPAN], BF16), nc.vector.tensor_copy)
-        quantize_w1(0, 0)
-        round_w1(1, 0, held("w1_bf1", [P, PACK * SPAN], BF16), nc.vector.tensor_copy)
-        quantize_w1(1, 0, cuts=(0, P, 2 * P, SPAN))
-        expect(0, 1)
-        weigh(0)
+        for a in range(PASSES):
+            round_w1(a, 0, held("w1_bf%d" % a, [P, PACK * SPAN], BF16), nc.vector.tensor_copy)
+            quantize_w1(a, 0, 0, 1)
+            quantize_w1(a, 0, 1, 2)
+        quantize_w1(0, 0, 2, PACK, slot="w1_raw101")
+        quantize_w1(1, 0, 2, PACK)
+        expect(0, ("free", 1))
+        weigh(0, held("weighted0", [P, S], F32))
         scatter(0)
+        add_page("damp0")
+        add_page("weighted0")
 
-        turned_magnitude(spread, 1, PACK, "magnitude0")
-        early_roots = held("w1_bf1", [P, PACK - 1, 4, P], F32)
+        early_magnitudes(spread, 1, PACK)
+        early_roots = held("w1_bf1", [P, PACK - 1, BLOCKS, P], F32)
         for n in range(1, PACK):
-            turned_root(n, early_roots[:, n - 1])
-        turn_root(1, 0)
+            early_root(n, early_roots[:, n - 1])
+        turn_root(1, ("root", 0))
         square(1)
-        inverse = turned_weights()
-        expect(1, 2)
-        weigh(1)
+        inverse = inverse_weights(("root", 1))
+        expect(1, ("free", 2))
+        weigh(1, held("weighted1", [P, S], F32))
         scatter(1)
-        expect(2, 3)
-        expect(3, 4)
-        late_bf = held("magnitude0", [P, PASSES, PACK * SPAN], BF16)
-        round_w1(0, 1, late_bf[:, 0], nc.scalar.copy)
-        round_w1(1, 1, late_bf[:, 1], nc.scalar.copy)
-        quantize_w1(0, 1)
-        quantize_w1(1, 1)
-        held_back = held("magnitude0", [P, 2, S], F32)
+        expect(2, ("free", 3))
+        expect(3, ("early", 0))
+        late_bf = held("magnitude", [P, PASSES, PACK * SPAN], BF16)
+        for a in range(PASSES):
+            round_w1(a, 1, late_bf[:, a], nc.scalar.copy)
+        for a in range(PASSES):
+            quantize_w1(a, 1, 0, PACK)
+        held_back = held("magnitude", [P, 2, S], F32)
         for n in (2, 3):
-            turn_root(n, n - 1)
+            turn_root(n, ("a", n - 2))
             square(n)
             weigh(n, held_back[:, n - 2])
         scatter(2)
+        add_page("damp2")
         scatter(3)
+        add_page("damp3")
 
-        late = late_magnitude("w1_raw110")
-        sum_pair(0, 0, (0, 5), (0, 1))
-        late_roots(late, inverse, "w1_raw000")
-        for n, number in ((4, 1), (5, 2), (6, 3), (7, 4)):
-            turn_root(n, number)
+        magnitude = late_magnitudes(["wgs", ("early", 1), ("early", 2), ("early", 3)], "w1_raw110")
+        for c in (0, 1):
+            sum_pair(0, 0, c, ("late", c))
+        late_roots(magnitude, inverse, "w1_raw000")
+        for n, after in ((4, ("root", 2)), (5, ("root", 3)), (6, ("a", 2)), (7, ("a", 3))):
+            turn_root(n, after)
         square(4)
-        expect(4, 7)
-        weigh(4)
+        expect(4, ("late", 3))
+        copy_out(4, "weighted4")
         scatter(4)
-        expect(5, 6)
-        weigh(5)
-        sum_pair(0, 0, (7, 6), (2, 3))
+        expect(5, ("late", 2))
+        copy_out(5, "weighted5")
+        for c in (2, 3):
+            sum_pair(0, 0, c, ("a", c + 2))
         square(5)
         scatter(5)
-        expect(6, 1)
-        expect(7, 2)
+        expect(6, ("root", 4))
+        expect(7, ("root", 5))
         nc.scalar.activation(out=warm[:, 8:9], in_=damp[5][:, 0:1], func=ACT.Sigmoid)
         round_pair(0, 0)
-        sum_pair(0, 1, (0, 5, 7, 6))
+        for c in range(CHUNKS):
+            sum_pair(0, 1, c, ("sum", 0, 0, c))
         square(6)
-        weigh(6)
+        copy_out(6, "weighted6")
         scatter(6)
         square(7)
         round_pair(0, 1)
-        w3_bf = held("w1_raw000", [P, PASSES * PACK * N], BF16)
-        round_w3(w3_bf, 0, nc.scalar.copy)
-        round_w3(w3_bf, 1, nc.scalar.copy)
-        quantize_w3(w3_bf)
-        both = held("w1_raw000", [P, 2, PACK, HALF], BF16)
-        planes.extend(both[:, h] for h in range(2))
+
+        prepare_w3("w1_raw000")
+        planes = held("w1_raw000", [P, 2, PACK, HALF], BF16)
         for h in range(2):
-            add_plane(6, h * HALF, HALF)
+            add_plane(planes, 6, h * HALF, HALF)
+        back_afters = [("a", 6), ("root", 6), ("root", 7), ("sum", 0, 1, 0)]
         for c in (0, 1):
-            turn_back(c)
+            turn_back(c, back_afters[c])
             quantize_z(0, c)
-        weigh(7, held("pairs11", [P, S], F32))
+        copy_out(7, "pairs11")
         for c in (2, 3):
-            turn_back(c)
-        sum_pair(1, 0, (5, 7, 6, 1))
+            turn_back(c, back_afters[c])
+        for c, after in enumerate([("sum", 0, 1, 1), ("sum", 0, 1, 2), ("sum", 0, 1, 3), ("back", 0)]):
+            sum_pair(1, 0, c, after)
         round_pair(1, 0)
-        for c in range(CHUNKS):
-            part_pair(c)
+        for c, after in enumerate([("back", 1), ("back", 2), ("back", 3), ("a", 7)]):
+            part_pair(planes, c, after)
         scatter(7)
+
         z_w[0, 1] = held("damp7", [P, HALF], U32)
-        quantize_z(0, 2)
-        quantize_z(0, 3)
-
+        for c in (2, 3):
+            quantize_z(0, c)
+        freed = [("sum", 1, 0, c) for c in range(CHUNKS)] + [("part", c) for c in range(CHUNKS)]
         for i in range(ahead):
-            open_piece(i)
-            product(i, gate_side, 0)
-            product(i, vol_side, 0)
+            open_piece(i, freed[2 * i:2 * i + 2])
+            for side in (gate_side, vol_side):
+                product(i, side, 0, 0, HALF, stop=False)
 
-        for c in (0, 1, 2, 3):
-            add_plane(7, c * CHUNK, CHUNK)
         for c in range(CHUNKS):
-            weave(c, (nc.vector.tensor_copy, nc.vector.tensor_copy, nc.scalar.copy, nc.scalar.copy)[c])
+            add_plane(planes, 7, c * CHUNK, CHUNK)
+        for c in range(CHUNKS):
+            h, last = divmod(c, 2)
+            weave(planes, c, (nc.vector.tensor_copy, nc.scalar.copy)[h])
             quantize_z(1, c)
-            for i in (2 * (c // 2), 2 * (c // 2) + 1):
-                if c % 2 == 0:
-                    product(i, gate_side, 1, 0)
-                    product(i, vol_side, 1, 0)
-                else:
+            for i in (2 * h, 2 * h + 1):
+                for side in (gate_side, vol_side):
+                    product(i, side, 1, last * CHUNK, CHUNK, stop=(last == 1))
+                if last == 1:
                     finish(i)
         for i in range(ahead, len(pieces)):
+            open_piece(i, [("piece", i - ahead, side) for side in (gate_side, vol_side)])
+            for side in (gate_side, vol_side):
+                for b in range(PASSES):
+                    product(i, side, b, 0, pieces[i][2], stop=(b == PASSES - 1))
             finish(i)

@@ -54,7 +54,8 @@ def tile_list_wind_bid_pages_kernel(tc, tab_words, tab_scales, offs, w1, w2_word
         tab_s = held("tab_s", [P, PASSES * T], U8)
         w2_s = [held("w2_s%d" % b, [P, PASSES * SPAN], U8) for b in range(PASSES)]
         w4_s = held("w4_s", [P, PASSES * N], U8)
-        for tile in (tab_s, w2_s[0], w2_s[1], w4_s):
+        wgs_rows = held("wgs_rows", [P, S], F32)
+        for tile in (tab_s, wgs_rows, w2_s[0], w2_s[1], w4_s):
             nc.vector.memset(tile[:].bitcast(I32), 0)
         ident = held("ident", [P, P], F32)
         nc.vector.memset(ident[:], 0.0)
@@ -66,9 +67,6 @@ def tile_list_wind_bid_pages_kernel(tc, tab_words, tab_scales, offs, w1, w2_word
         def add_page(slot):
             pages.append(held(slot, [P, T2], F32))
             nc.gpsimd.memset(pages[-1][:].bitcast(I32), 0)
-
-        warm = held("warm", [P, 16], F32)
-        nc.scalar.activation(out=warm[:, 0:1], in_=ident[:, 0:1], func=ACT.Abs_reciprocal_sqrt, bias=1.0)
 
         tab_w = [held("tab_w%d" % a, [P, T], U32) for a in range(PASSES)]
         w2_w = [held("w2_w%d" % b, [P, PASSES * 2 * SPAN], U8) for b in range(PASSES)]
@@ -116,6 +114,7 @@ def tile_list_wind_bid_pages_kernel(tc, tab_words, tab_scales, offs, w1, w2_word
         nc.sync.dma_start(list1[:], offs)
         load_tab(0)
         load_scales(tab_s, tab_scales)
+        nc.sync.dma_start(out=wgs_rows[0:P:GROUP], in_=wgs[0:P:GROUP])
         load_w2_words(0)
         load_tab(1)
         load_w2_scales(0)
@@ -143,7 +142,7 @@ def tile_list_wind_bid_pages_kernel(tc, tab_words, tab_scales, offs, w1, w2_word
         nc.vector.tensor_copy(out=v_w[1][:], in_=tab_w[1][:].indirect(list1[:]))
 
         w1_w, w1_s, w1_bf = {}, {}, {}
-        magnitudes, roots, turned, damp, expected, weighted = {}, {}, {}, {}, {}, {}
+        magnitudes, roots, turned, damp, expected, outside = {}, {}, {}, {}, {}, {}
 
         def round_w1(a, b, tile, copy):
             w1_bf[a, b] = tile
@@ -186,7 +185,7 @@ def tile_list_wind_bid_pages_kernel(tc, tab_words, tab_scales, offs, w1, w2_word
         def inverse_weights(after):
             acc = bank("wgs", after)
             for jb in range(BLOCKS):
-                nc.tensor.transpose(acc[:, jb * P:(jb + 1) * P], wgs_t[:, jb * P:(jb + 1) * P], ident[:])
+                nc.tensor.transpose(acc[:, jb * P:(jb + 1) * P], wgs_rows[:, jb * P:(jb + 1) * P], ident[:])
             inverse = held("inverse", [P, BLOCKS * LISTS], F32)
             picked = held("picked", [P, BLOCKS * LISTS], F32)
             nc.scalar.activation(out=picked[:], in_=acc[:, 0:BANK:GROUP], func=ACT.Abs_reciprocal_sqrt)
@@ -231,15 +230,15 @@ def tile_list_wind_bid_pages_kernel(tc, tab_words, tab_scales, offs, w1, w2_word
                                     start=(a == 0), stop=(a == PASSES - 1))
 
         def weigh(n, tile):
-            weighted[n] = tile
+            outside[n] = tile
             nc.vector.tensor_tensor(out=tile[:], in0=expected[n][:], in1=wgs_t[:], op=MULT)
 
         def copy_out(n, slot):
-            weighted[n] = held(slot, [P, S], F32)
-            nc.scalar.copy(out=weighted[n][:], in_=expected[n][:])
+            outside[n] = held(slot, [P, S], F32)
+            nc.scalar.copy(out=outside[n][:], in_=expected[n][:])
 
         def scatter(n):
-            nc.vector.tensor_tensor(out=pages[n % PAGES][:].indirect(list2[:]), in0=weighted[n][:],
+            nc.vector.tensor_tensor(out=pages[n % PAGES][:].indirect(list2[:]), in0=outside[n][:],
                                     in1=damp[n][:], op=MULT)
 
         sums, pairs, z_bf = {}, {}, {}
@@ -277,19 +276,43 @@ def tile_list_wind_bid_pages_kernel(tc, tab_words, tab_scales, offs, w1, w2_word
                            in_=back[:].rearrange("p (g u m) -> p g m u", g=2, u=2))
 
         def quantize_z(b, c):
-            h, side = divmod(c, 2)
-            cols = slice(side * CHUNK, (side + 1) * CHUNK)
+            h, odd = divmod(c, 2)
+            cols = slice(odd * CHUNK, (odd + 1) * CHUNK)
             nc.vector.quantize_mx(out=z_w[b, h][:, cols].bitcast(FP8X4), scales=z_s[b, h][:, cols],
                                   in_=z_bf[b, c][:])
 
         def part_pair(planes, c, after):
-            h, side = divmod(c, 2)
+            h, odd = divmod(c, 2)
             back = bank(("part", c), after)
             for g in range(2):
                 nc.tensor.transpose(back[:, g * P:(g + 1) * P], pairs[1, 0, c][:].bitcast(F32)[:, g * P:(g + 1) * P],
                                     ident[:])
-            nc.scalar.copy(out=planes[:, h, 0:2, side * CHUNK:(side + 1) * CHUNK],
+            nc.scalar.copy(out=planes[:, h, 0:2, odd * CHUNK:(odd + 1) * CHUNK],
                            in_=back[:, 0:CHUNK].bitcast(BF16).rearrange("p (m e) -> p e m", e=2))
+
+        def sum_single(n, h, after):
+            t = n % PACK
+            acc = bank("single", after)
+            for step, src in enumerate((clim_t[1, t // 2][:, t % 2, :], pages[n % PAGES])):
+                for block in range(4):
+                    m0 = h * HALF + block * P
+                    nc.tensor.matmul(out=acc[:, block * P:(block + 1) * P], lhsT=src[:, m0:m0 + P], rhs=ident[:],
+                                     is_transpose=True, start=(step == 0 and block == 0),
+                                     stop=(step == 1 and block == 3))
+            return acc
+
+        def round_single(acc):
+            words = held("pairs13", [P, BANK], BF16)
+            nc.scalar.copy(out=words[:].rearrange("m (g p e) -> m g p e", g=2, e=2),
+                           in_=acc[:].rearrange("m (g e p) -> m g p e", g=2, e=2))
+            return words
+
+        def part_single(planes, n, h, words, after):
+            back = bank("parted", after)
+            for g in range(2):
+                nc.tensor.transpose(back[:, g * P:(g + 1) * P], words[:].bitcast(F32)[:, g * P:(g + 1) * P], ident[:])
+            nc.scalar.copy(out=planes[:, h, n % PACK, :].rearrange("p (g e m) -> p g e m", g=2, e=2),
+                           in_=back[:, 0:CHUNK].bitcast(BF16).rearrange("p (g m e) -> p g e m", g=2, e=2))
 
         def add_plane(planes, n, m0, width):
             t = n % PACK
@@ -297,11 +320,12 @@ def tile_list_wind_bid_pages_kernel(tc, tab_words, tab_scales, offs, w1, w2_word
             nc.vector.tensor_tensor(out=planes[:, h, t, c0:c0 + width], in0=pages[n % PAGES][:, m0:m0 + width],
                                     in1=clim_t[1, t // 2][:, t % 2, m0:m0 + width], op=ADD)
 
-        def weave(planes, c, copy):
-            h, side = divmod(c, 2)
+        def weave(planes, c):
+            h, odd = divmod(c, 2)
             z_bf[1, c] = held("z_bf%d" % c, [P, PACK * CHUNK], BF16)
-            copy(out=z_bf[1, c][:].rearrange("p (m i t) -> p m t i", i=4, t=PACK),
-                 in_=planes[:, h, :, side * CHUNK:(side + 1) * CHUNK].rearrange("p t (m i) -> p m t i", i=4))
+            source = planes[:, h, :, odd * CHUNK:(odd + 1) * CHUNK]
+            nc.vector.tensor_copy(out=z_bf[1, c][:].rearrange("p (m i t) -> p m t i", i=4, t=PACK),
+                                  in_=source.rearrange("p t (m i) -> p m t i", i=4))
 
         w3_w = held("w3_w", [P, PASSES * N], U32)
         w3_s = held("w3_s", [P, PASSES * N], U8)
@@ -342,13 +366,14 @@ def tile_list_wind_bid_pages_kernel(tc, tab_words, tab_scales, offs, w1, w2_word
             nc.vector.tensor_tensor(out=result[:], in0=accs[i][vol_side][:, 0:width], in1=gate[:], op=MULT)
             nc.sync.dma_start(out=out[nt * P:(nt + 1) * P, m0:m0 + width], in_=result[:])
 
+        inverse = inverse_weights(("free", 0))
         spread = [bank(("early", jb), ("free", 4 + jb)) for jb in range(BLOCKS)]
         for a in range(PASSES):
             for jb in range(BLOCKS):
                 spread_pass(spread[jb], a, 0, jb)
         early_magnitudes(spread, 0, 1)
         early_root(0, held("root0", [P, BLOCKS, P], F32)[:])
-        turn_root(0, ("free", 0))
+        turn_root(0, "wgs")
         square(0)
         for a in range(PASSES):
             round_w1(a, 0, held("w1_bf%d" % a, [P, PACK * SPAN], BF16), nc.vector.tensor_copy)
@@ -368,7 +393,6 @@ def tile_list_wind_bid_pages_kernel(tc, tab_words, tab_scales, offs, w1, w2_word
             early_root(n, early_roots[:, n - 1])
         turn_root(1, ("root", 0))
         square(1)
-        inverse = inverse_weights(("root", 1))
         expect(1, ("free", 2))
         weigh(1, held("weighted1", [P, S], F32))
         scatter(1)
@@ -389,7 +413,7 @@ def tile_list_wind_bid_pages_kernel(tc, tab_words, tab_scales, offs, w1, w2_word
         scatter(3)
         add_page("damp3")
 
-        magnitude = late_magnitudes(["wgs", ("early", 1), ("early", 2), ("early", 3)], "w1_raw110")
+        magnitude = late_magnitudes([("root", 1), ("early", 1), ("early", 2), ("early", 3)], "w1_raw110")
         for c in (0, 1):
             sum_pair(0, 0, c, ("late", c))
         late_roots(magnitude, inverse, "w1_raw000")
@@ -407,7 +431,6 @@ def tile_list_wind_bid_pages_kernel(tc, tab_words, tab_scales, offs, w1, w2_word
         scatter(5)
         expect(6, ("root", 4))
         expect(7, ("root", 5))
-        nc.scalar.activation(out=warm[:, 8:9], in_=damp[5][:, 0:1], func=ACT.Sigmoid)
         round_pair(0, 0)
         for c in range(CHUNKS):
             sum_pair(0, 1, c, ("sum", 0, 0, c))
@@ -419,8 +442,7 @@ def tile_list_wind_bid_pages_kernel(tc, tab_words, tab_scales, offs, w1, w2_word
 
         prepare_w3("w1_raw000")
         planes = held("w1_raw000", [P, 2, PACK, HALF], BF16)
-        for h in range(2):
-            add_plane(planes, 6, h * HALF, HALF)
+        add_plane(planes, 6, 0, HALF)
         back_afters = [("a", 6), ("root", 6), ("root", 7), ("sum", 0, 1, 0)]
         for c in (0, 1):
             turn_back(c, back_afters[c])
@@ -431,30 +453,45 @@ def tile_list_wind_bid_pages_kernel(tc, tab_words, tab_scales, offs, w1, w2_word
         for c, after in enumerate([("sum", 0, 1, 1), ("sum", 0, 1, 2), ("sum", 0, 1, 3), ("back", 0)]):
             sum_pair(1, 0, c, after)
         round_pair(1, 0)
-        for c, after in enumerate([("back", 1), ("back", 2), ("back", 3), ("a", 7)]):
-            part_pair(planes, c, after)
+        single = sum_single(6, 1, ("sum", 1, 0, 0))
+        part_pair(planes, 0, ("back", 1))
+        part_pair(planes, 1, ("back", 2))
+        single_words = round_single(single)
+        part_pair(planes, 2, ("back", 3))
+        part_pair(planes, 3, ("a", 7))
+        part_single(planes, 6, 1, single_words, ("sum", 1, 0, 1))
         scatter(7)
 
+        freed = [("sum", 1, 0, 2), ("sum", 1, 0, 3), ("part", 0), ("part", 1), "single", ("part", 2), ("part", 3),
+                 "parted"]
+
+        def first_pass(h):
+            for i in (2 * h, 2 * h + 1):
+                open_piece(i, freed[2 * i:2 * i + 2])
+                for side in (gate_side, vol_side):
+                    product(i, side, 0, 0, HALF, stop=False)
+
+        def last_pass(h):
+            chunks = (2 * h, 2 * h + 1)
+            for c in chunks:
+                add_plane(planes, 7, c * CHUNK, CHUNK)
+            for c in chunks:
+                weave(planes, c)
+            for c in chunks:
+                quantize_z(1, c)
+            for i in (2 * h, 2 * h + 1):
+                for side in (gate_side, vol_side):
+                    for odd in range(2):
+                        product(i, side, 1, odd * CHUNK, CHUNK, stop=(odd == 1))
+                finish(i)
+
+        first_pass(0)
+        last_pass(0)
         z_w[0, 1] = held("damp7", [P, HALF], U32)
         for c in (2, 3):
             quantize_z(0, c)
-        freed = [("sum", 1, 0, c) for c in range(CHUNKS)] + [("part", c) for c in range(CHUNKS)]
-        for i in range(ahead):
-            open_piece(i, freed[2 * i:2 * i + 2])
-            for side in (gate_side, vol_side):
-                product(i, side, 0, 0, HALF, stop=False)
-
-        for c in range(CHUNKS):
-            add_plane(planes, 7, c * CHUNK, CHUNK)
-        for c in range(CHUNKS):
-            h, last = divmod(c, 2)
-            weave(planes, c, (nc.vector.tensor_copy, nc.scalar.copy)[h])
-            quantize_z(1, c)
-            for i in (2 * h, 2 * h + 1):
-                for side in (gate_side, vol_side):
-                    product(i, side, 1, last * CHUNK, CHUNK, stop=(last == 1))
-                if last == 1:
-                    finish(i)
+        first_pass(1)
+        last_pass(1)
         for i in range(ahead, len(pieces)):
             open_piece(i, [("piece", i - ahead, side) for side in (gate_side, vol_side)])
             for side in (gate_side, vol_side):

@@ -241,6 +241,18 @@ def tile_list_wind_bid_pages_kernel(tc, tab_words, tab_scales, offs, w1, w2_word
             nc.vector.tensor_tensor(out=pages[n % PAGES][:].indirect(list2[:]), in0=outside[n][:],
                                     in1=damp[n][:], op=MULT)
 
+        def scatter_copy(n):
+            nc.vector.tensor_copy(out=pages[n % PAGES][:].indirect(list2[:]), in_=outside[n][:])
+
+        def dampen_psum(n, slot):
+            outside[n] = held(slot, [P, S], F32)
+            nc.vector.tensor_tensor(out=outside[n][:], in0=expected[n][:], in1=damp[n][:], op=MULT)
+
+        def dampen_sbuf(n, slot):
+            plain = outside[n]
+            outside[n] = held(slot, [P, S], F32)
+            nc.gpsimd.tensor_tensor(out=outside[n][:], in0=plain[:], in1=damp[n][:], op=MULT)
+
         sums, pairs, z_bf = {}, {}, {}
         z_w = {(b, h): held("z_w%d%d" % (b, h), [P, HALF], U32) for b, h in ((0, 0), (1, 0), (1, 1))}
         z_s = {(b, h): held("z_s%d%d" % (b, h), [P, HALF], U8) for b in range(PASSES) for h in range(2)}
@@ -331,14 +343,14 @@ def tile_list_wind_bid_pages_kernel(tc, tab_words, tab_scales, offs, w1, w2_word
         w3_s = held("w3_s", [P, PASSES * N], U8)
 
         def prepare_w3(slot):
-            w3_bf = held(slot, [P, PASSES * PACK * N], BF16)
             for b in range(PASSES):
-                rounded = w3_bf[:, b * PACK * N:(b + 1) * PACK * N]
-                nc.scalar.copy(out=rounded.rearrange("p (c i j) -> p c j i", i=4, j=PACK),
-                               in_=w3_raw[b][:].rearrange("p j (c i) -> p c j i", i=4))
-            for c0, c1 in ((0, 512), (512, PASSES * N)):
-                nc.vector.quantize_mx(out=w3_w[:, c0:c1].bitcast(FP8X4), scales=w3_s[:, c0:c1],
-                                      in_=w3_bf[:, PACK * c0:PACK * c1])
+                rounded = held(slot[b], [P, PACK * N], BF16)[:]
+                nc.gpsimd.tensor_scalar(out=rounded.rearrange("p (c i j) -> p c j i", i=4, j=PACK),
+                                        in0=w3_raw[b][:].rearrange("p j (c i) -> p c j i", i=4),
+                                        scalar1=1.0, scalar2=0.0, op0=MULT, op1=ADD)
+                for c0, c1 in ((0, 256), (256, N)):
+                    nc.vector.quantize_mx(out=w3_w[:, b * N + c0:b * N + c1].bitcast(FP8X4),
+                                          scales=w3_s[:, b * N + c0:b * N + c1], in_=rounded[:, PACK * c0:PACK * c1])
 
         pieces = [(0, 0, HALF), (1, 0, HALF), (0, HALF, HALF), (1, HALF, HALF), (2, 0, HALF),
                   (2, HALF, CHUNK), (2, HALF + CHUNK, CHUNK)]
@@ -421,14 +433,15 @@ def tile_list_wind_bid_pages_kernel(tc, tab_words, tab_scales, offs, w1, w2_word
             turn_root(n, after)
         square(4)
         expect(4, ("late", 3))
-        copy_out(4, "weighted4")
-        scatter(4)
+        dampen_psum(4, "weighted4")
+        scatter_copy(4)
         expect(5, ("late", 2))
         copy_out(5, "weighted5")
         for c in (2, 3):
             sum_pair(0, 0, c, ("a", c + 2))
         square(5)
-        scatter(5)
+        dampen_sbuf(5, "product5")
+        scatter_copy(5)
         expect(6, ("root", 4))
         expect(7, ("root", 5))
         round_pair(0, 0)
@@ -436,18 +449,20 @@ def tile_list_wind_bid_pages_kernel(tc, tab_words, tab_scales, offs, w1, w2_word
             sum_pair(0, 1, c, ("sum", 0, 0, c))
         square(6)
         copy_out(6, "weighted6")
-        scatter(6)
+        dampen_sbuf(6, "product6")
+        scatter_copy(6)
+        copy_out(7, "weighted7")
         square(7)
         round_pair(0, 1)
 
-        prepare_w3("w1_raw000")
+        prepare_w3(("weighted5", "weighted6"))
         planes = held("w1_raw000", [P, 2, PACK, HALF], BF16)
         add_plane(planes, 6, 0, HALF)
         back_afters = [("a", 6), ("root", 6), ("root", 7), ("sum", 0, 1, 0)]
         for c in (0, 1):
             turn_back(c, back_afters[c])
             quantize_z(0, c)
-        copy_out(7, "pairs11")
+        dampen_sbuf(7, "pairs11")
         for c in (2, 3):
             turn_back(c, back_afters[c])
         for c, after in enumerate([("sum", 0, 1, 1), ("sum", 0, 1, 2), ("sum", 0, 1, 3), ("back", 0)]):
@@ -460,7 +475,7 @@ def tile_list_wind_bid_pages_kernel(tc, tab_words, tab_scales, offs, w1, w2_word
         part_pair(planes, 2, ("back", 3))
         part_pair(planes, 3, ("a", 7))
         part_single(planes, 6, 1, single_words, ("sum", 1, 0, 1))
-        scatter(7)
+        scatter_copy(7)
 
         freed = [("sum", 1, 0, 2), ("sum", 1, 0, 3), ("part", 0), ("part", 1), "single", ("part", 2), ("part", 3),
                  "parted"]

@@ -29,6 +29,7 @@ GROUP = P // LISTS
 PAGES = 6
 CHUNK = 256
 CHUNKS = T2 // CHUNK
+ROW = 12
 HALF = T2 // 2
 
 
@@ -87,12 +88,11 @@ def tile_list_wind_bid_pages_kernel(tc, tab_words, tab_scales, offs, w1, w2_word
                               in_=tab_words[a].rearrange("p t i -> p (t i)").bitcast(I32))
 
         def load_w1(a, b, parts=1):
-            width = SPAN // parts
-            w1_raw[a, b] = [held("w1_raw%d%d%d" % (a, b, part), [P, PACK, width], F32) for part in range(parts)]
+            depth = PACK // parts
+            w1_raw[a, b] = [held("w1_raw%d%d%d" % (a, b, part), [P, depth, SPAN], F32) for part in range(parts)]
+            rows = w1[SPAN * a:SPAN * (a + 1), SPAN * b:SPAN * (b + 1)].rearrange("(p j) c -> p j c", j=PACK)
             for part, raw in enumerate(w1_raw[a, b]):
-                c0 = SPAN * b + part * width
-                rows = w1[SPAN * a:SPAN * (a + 1), c0:c0 + width]
-                nc.sync.dma_start(out=raw[:], in_=rows.rearrange("(p j) c -> p j c", j=PACK))
+                nc.sync.dma_start(out=raw[:], in_=rows[:, part * depth:(part + 1) * depth])
 
         def load_w2_words(b):
             words = w2_words[:, :, 2 * SPAN * b:2 * SPAN * (b + 1)]
@@ -114,7 +114,7 @@ def tile_list_wind_bid_pages_kernel(tc, tab_words, tab_scales, offs, w1, w2_word
         nc.sync.dma_start(list1[:], offs)
         load_tab(0)
         load_scales(tab_s, tab_scales)
-        nc.sync.dma_start(out=wgs_rows[0:P:GROUP], in_=wgs[0:P:GROUP])
+        nc.sync.dma_start(out=wgs_rows[ROW:P:GROUP], in_=wgs[ROW:P:GROUP])
         load_w2_words(0)
         load_tab(1)
         load_w2_scales(0)
@@ -135,21 +135,43 @@ def tile_list_wind_bid_pages_kernel(tc, tab_words, tab_scales, offs, w1, w2_word
         load_clim(1)
 
         v_w = [held("v_w%d" % a, [P, S], U32) for a in range(PASSES)]
-        v_s = [held("v_s%d" % a, [P, S], U8) for a in range(PASSES)]
+        v_s = [held("v_s%d" % a, [P, S], U8)[:] for a in range(PASSES)]
         nc.vector.tensor_copy(out=v_w[0][:], in_=tab_w[0][:].indirect(list1[:]))
         for a in range(PASSES):
-            nc.vector.tensor_copy(out=v_s[a][:], in_=tab_s[:, a * T:(a + 1) * T].indirect(list1[:]))
+            nc.vector.tensor_copy(out=v_s[a], in_=tab_s[:, a * T:(a + 1) * T].indirect(list1[:]))
         nc.vector.tensor_copy(out=v_w[1][:], in_=tab_w[1][:].indirect(list1[:]))
+        for slot in ("tab_s", "tab_w0", "tab_w1"):
+            add_page(slot)
 
         w1_w, w1_s, w1_bf = {}, {}, {}
-        magnitudes, roots, turned, damp, expected, outside = {}, {}, {}, {}, {}, {}
+        roots, turned, damp, expected, outside, ready = {}, {}, {}, {}, {}, {}
+
+        def gpsimd_round(out, in_):
+            nc.gpsimd.tensor_scalar(out=out, in0=in_, scalar1=1.0, scalar2=0.0, op0=MULT, op1=ADD)
+
+        def round_late(a, t0, tile, copy, walk):
+            columns = w1_raw[a, 1][0][:].rearrange("p j (m t) -> p j m t", t=PACK)[:, :, :, t0:t0 + 2]
+            if walk == "rows":
+                copy(out=tile.rearrange("p (t m j) -> p t m j", t=2, j=PACK), in_=columns.rearrange("p j m t -> p t m j"))
+            else:
+                copy(out=tile.rearrange("p (t m u e) -> p m u t e", t=2, u=2, e=2),
+                     in_=columns.rearrange("p (u e) m t -> p m u t e", e=2))
+
+        def quantize_late(passes, t0, tile, slot):
+            words = held(slot, [P, len(passes) * 2 * P], U32)
+            scales = held("w1_s%d1%d" % (passes[0], t0), [P, len(passes) * 2 * P], U8)
+            nc.vector.quantize_mx(out=words[:].bitcast(FP8X4), scales=scales[:], in_=tile)
+            for i, a in enumerate(passes):
+                for t in range(2):
+                    cols = slice((2 * i + t) * P, (2 * i + t + 1) * P)
+                    w1_w[a, 1, t0 + t], w1_s[a, 1, t0 + t] = words[:, cols], scales[:, cols]
 
         def round_w1(a, b, tile, copy):
             w1_bf[a, b] = tile
             rounded = tile[:].rearrange("p (t m u e) -> p m u t e", t=PACK, u=2, e=2)
             parts = len(w1_raw[a, b])
             for part, raw in enumerate(w1_raw[a, b]):
-                copy(out=rounded[:, part * P // parts:(part + 1) * P // parts],
+                copy(out=rounded[:, :, part * 2 // parts:(part + 1) * 2 // parts],
                      in_=raw[:].rearrange("p (u e) (m t) -> p m u t e", t=PACK, e=2))
 
         def quantize_w1(a, b, t0, t1, slot=None):
@@ -173,14 +195,13 @@ def tile_list_wind_bid_pages_kernel(tc, tab_words, tab_scales, offs, w1, w2_word
 
         def early_magnitudes(accs, t0, t1):
             tile = held("magnitude", [P, BLOCKS, t1 - t0, P], F32)
-            for t in range(t0, t1):
-                magnitudes[t] = tile[:, :, t - t0, :]
             for jb in range(BLOCKS):
                 take_magnitude(tile[:, jb], accs[jb], t0, t1)
+            return tile[:]
 
-        def early_root(n, tile):
+        def plain_root(n, magnitude, tile):
             roots[n] = tile
-            nc.scalar.activation(out=tile, in_=magnitudes[n], func=ACT.Abs_reciprocal_sqrt, bias=1.0)
+            nc.scalar.activation(out=tile, in_=magnitude[:, :, 0, :], func=ACT.Abs_reciprocal_sqrt, bias=1.0)
 
         def inverse_weights(after):
             acc = bank("wgs", after)
@@ -188,7 +209,7 @@ def tile_list_wind_bid_pages_kernel(tc, tab_words, tab_scales, offs, w1, w2_word
                 nc.tensor.transpose(acc[:, jb * P:(jb + 1) * P], wgs_rows[:, jb * P:(jb + 1) * P], ident[:])
             inverse = held("inverse", [P, BLOCKS * LISTS], F32)
             picked = held("picked", [P, BLOCKS * LISTS], F32)
-            nc.scalar.activation(out=picked[:], in_=acc[:, 0:BANK:GROUP], func=ACT.Abs_reciprocal_sqrt)
+            nc.scalar.activation(out=picked[:], in_=acc[:, ROW:BANK:GROUP], func=ACT.Abs_reciprocal_sqrt)
             nc.scalar.activation(out=inverse[:], in_=picked[:], func=ACT.Square)
             return inverse
 
@@ -201,16 +222,15 @@ def tile_list_wind_bid_pages_kernel(tc, tab_words, tab_scales, offs, w1, w2_word
                 take_magnitude(tile[:, jb], acc, 0, PACK)
             return tile
 
-        def late_roots(magnitude, inverse, slot):
-            tile = held(slot, [P, BLOCKS, PACK, P], F32)
+        def weighted_roots(first, magnitude, tile, inverse):
             for jb in range(BLOCKS):
                 for g in range(LISTS):
                     factor = inverse[:, LISTS * jb + g:LISTS * jb + g + 1]
                     places = slice(g * GROUP, (g + 1) * GROUP)
                     nc.scalar.activation(out=tile[:, jb, :, places], in_=magnitude[:, jb, :, places],
                                          func=ACT.Abs_reciprocal_sqrt, bias=factor, scale=factor)
-            for t in range(PACK):
-                roots[PACK + t] = tile[:, :, t, :]
+            for t in range(tile.shape[2]):
+                roots[first + t] = tile[:, :, t, :]
 
         def turn_root(n, after):
             acc = turned[n] = bank(("root", n), after)
@@ -226,42 +246,38 @@ def tile_list_wind_bid_pages_kernel(tc, tab_words, tab_scales, offs, w1, w2_word
             acc = expected[n] = bank(("a", n), after)
             for a in range(PASSES):
                 nc.tensor.matmul_mx(out=acc[:], lhsT=w1_w[a, b, t].bitcast(FP8X4), lhsT_scale=w1_s[a, b, t],
-                                    rhs=v_w[a][:].bitcast(FP8X4), rhs_scale=v_s[a][:],
+                                    rhs=v_w[a][:].bitcast(FP8X4), rhs_scale=v_s[a],
                                     start=(a == 0), stop=(a == PASSES - 1))
 
         def weigh(n, tile):
             outside[n] = tile
             nc.vector.tensor_tensor(out=tile[:], in0=expected[n][:], in1=wgs_t[:], op=MULT)
 
-        def copy_out(n, slot):
-            outside[n] = held(slot, [P, S], F32)
+        def copy_out(n, slot=None):
+            outside[n] = held(slot or "outside%d" % n, [P, S], F32)
             nc.scalar.copy(out=outside[n][:], in_=expected[n][:])
 
+        def dampen(n, slot):
+            ready[n] = held(slot, [P, S], F32)
+            nc.gpsimd.tensor_tensor(out=ready[n][:], in0=outside[n][:], in1=damp[n][:], op=MULT)
+
+        def weigh_damping(n):
+            plain = damp[n]
+            damp[n] = held({2: "root1", 3: "picked_s"}[n], [P, S], F32)
+            nc.gpsimd.tensor_tensor(out=damp[n][:], in0=plain[:], in1=wgs_t[:], op=MULT)
+
         def scatter(n):
-            nc.vector.tensor_tensor(out=pages[n % PAGES][:].indirect(list2[:]), in0=outside[n][:],
-                                    in1=damp[n][:], op=MULT)
-
-        def scatter_copy(n):
-            nc.vector.tensor_copy(out=pages[n % PAGES][:].indirect(list2[:]), in_=outside[n][:])
-
-        def dampen_psum(n, slot):
-            outside[n] = held(slot, [P, S], F32)
-            nc.vector.tensor_tensor(out=outside[n][:], in0=expected[n][:], in1=damp[n][:], op=MULT)
-
-        def dampen_sbuf(n, slot):
-            plain = outside[n]
-            outside[n] = held(slot, [P, S], F32)
-            nc.gpsimd.tensor_tensor(out=outside[n][:], in0=plain[:], in1=damp[n][:], op=MULT)
+            nc.vector.tensor_copy(out=pages[n % PAGES][:].indirect(list2[:]), in_=ready[n][:])
 
         sums, pairs, z_bf = {}, {}, {}
-        z_w = {(b, h): held("z_w%d%d" % (b, h), [P, HALF], U32) for b, h in ((0, 0), (1, 0), (1, 1))}
+        z_w = {(b, h): held("z_w%d%d" % (b, h), [P, HALF], U32) for b, h in ((1, 0), (1, 1))}
         z_s = {(b, h): held("z_s%d%d" % (b, h), [P, HALF], U8) for b in range(PASSES) for h in range(2)}
 
         def sum_pair(b, u, c, after):
             first = PACK * b + 2 * u
             sources = [(0, clim_t[b, u][:, 0, :]), (1, clim_t[b, u][:, 1, :]),
                        (0, pages[first % PAGES]), (1, pages[(first + 1) % PAGES])]
-            acc = sums[c] = bank(("sum", b, u, c), after)
+            acc = sums[u, c] = bank(("sum", b, u, c), after)
             for step, (e, src) in enumerate(sources):
                 for g in range(2):
                     m0 = c * CHUNK + g * P
@@ -270,20 +286,20 @@ def tile_list_wind_bid_pages_kernel(tc, tab_words, tab_scales, offs, w1, w2_word
                                      is_transpose=True, start=(step == 0 and g == 0),
                                      stop=(step == len(sources) - 1 and g == 1))
 
-        def round_pair(b, u):
-            for c in range(CHUNKS):
+        def round_pair(b, u, chunks):
+            for c in chunks:
                 pairs[b, u, c] = held("pairs%d%d" % (u, c), [P, BANK], BF16)
                 nc.scalar.copy(out=pairs[b, u, c][:].rearrange("m (g p e) -> m g p e", g=2, e=2),
-                               in_=sums[c][:].rearrange("m (g e p) -> m g p e", g=2, e=2))
+                               in_=sums[u, c][:].rearrange("m (g e p) -> m g p e", g=2, e=2))
 
-        def turn_back(c, after):
+        def turn_back(c, after, tile):
             back = bank(("back", c), after)
             for u in (1, 0):
                 for g in range(2):
                     o0 = (2 * g + u) * P
                     nc.tensor.transpose(back[:, o0:o0 + P], pairs[0, u, c][:].bitcast(F32)[:, g * P:(g + 1) * P],
                                         ident[:])
-            z_bf[0, c] = held("z_bf%d" % c, [P, PACK * CHUNK], BF16)
+            z_bf[0, c] = tile
             nc.scalar.copy(out=z_bf[0, c][:].bitcast(F32).rearrange("p (g m u) -> p g m u", g=2, u=2),
                            in_=back[:].rearrange("p (g u m) -> p g m u", g=2, u=2))
 
@@ -293,64 +309,30 @@ def tile_list_wind_bid_pages_kernel(tc, tab_words, tab_scales, offs, w1, w2_word
             nc.vector.quantize_mx(out=z_w[b, h][:, cols].bitcast(FP8X4), scales=z_s[b, h][:, cols],
                                   in_=z_bf[b, c][:])
 
-        def part_pair(planes, c, after):
-            h, odd = divmod(c, 2)
-            back = bank(("part", c), after)
-            for g in range(2):
-                nc.tensor.transpose(back[:, g * P:(g + 1) * P], pairs[1, 0, c][:].bitcast(F32)[:, g * P:(g + 1) * P],
-                                    ident[:])
-            nc.scalar.copy(out=planes[:, h, 0:2, odd * CHUNK:(odd + 1) * CHUNK],
-                           in_=back[:, 0:CHUNK].bitcast(BF16).rearrange("p (m e) -> p e m", e=2))
-
-        def sum_single(n, h, after):
+        def add_plane(planes, n, m0, width, engine):
             t = n % PACK
-            acc = bank("single", after)
-            for step, src in enumerate((clim_t[1, t // 2][:, t % 2, :], pages[n % PAGES])):
-                for block in range(4):
-                    m0 = h * HALF + block * P
-                    nc.tensor.matmul(out=acc[:, block * P:(block + 1) * P], lhsT=src[:, m0:m0 + P], rhs=ident[:],
-                                     is_transpose=True, start=(step == 0 and block == 0),
-                                     stop=(step == 1 and block == 3))
-            return acc
+            engine.tensor_tensor(out=planes[:, t * T2 + m0:t * T2 + m0 + width], in0=pages[n % PAGES][:, m0:m0 + width],
+                                 in1=clim_t[1, t // 2][:, t % 2, m0:m0 + width], op=ADD)
 
-        def round_single(acc):
-            words = held("pairs13", [P, BANK], BF16)
-            nc.scalar.copy(out=words[:].rearrange("m (g p e) -> m g p e", g=2, e=2),
-                           in_=acc[:].rearrange("m (g e p) -> m g p e", g=2, e=2))
-            return words
+        def weave(planes, c, copy):
+            z_bf[1, c] = held(("z_bf0", "z_bf1", "pairs12", "pairs13")[c], [P, PACK * CHUNK], BF16)[:]
+            source = planes[:].rearrange("p (t m) -> p t m", t=PACK)[:, :, c * CHUNK:(c + 1) * CHUNK]
+            copy(out=z_bf[1, c].rearrange("p (m i t) -> p m t i", i=4, t=PACK),
+                 in_=source.rearrange("p t (m i) -> p m t i", i=4))
 
-        def part_single(planes, n, h, words, after):
-            back = bank("parted", after)
-            for g in range(2):
-                nc.tensor.transpose(back[:, g * P:(g + 1) * P], words[:].bitcast(F32)[:, g * P:(g + 1) * P], ident[:])
-            nc.scalar.copy(out=planes[:, h, n % PACK, :].rearrange("p (g e m) -> p g e m", g=2, e=2),
-                           in_=back[:, 0:CHUNK].bitcast(BF16).rearrange("p (g m e) -> p g e m", g=2, e=2))
-
-        def add_plane(planes, n, m0, width):
-            t = n % PACK
-            h, c0 = divmod(m0, HALF)
-            nc.vector.tensor_tensor(out=planes[:, h, t, c0:c0 + width], in0=pages[n % PAGES][:, m0:m0 + width],
-                                    in1=clim_t[1, t // 2][:, t % 2, m0:m0 + width], op=ADD)
-
-        def weave(planes, c):
-            h, odd = divmod(c, 2)
-            z_bf[1, c] = held("z_bf%d" % c, [P, PACK * CHUNK], BF16)
-            source = planes[:, h, :, odd * CHUNK:(odd + 1) * CHUNK]
-            nc.vector.tensor_copy(out=z_bf[1, c][:].rearrange("p (m i t) -> p m t i", i=4, t=PACK),
-                                  in_=source.rearrange("p t (m i) -> p m t i", i=4))
-
-        w3_w = held("w3_w", [P, PASSES * N], U32)
         w3_s = held("w3_s", [P, PASSES * N], U8)
 
-        def prepare_w3(slot):
-            for b in range(PASSES):
-                rounded = held(slot[b], [P, PACK * N], BF16)[:]
-                nc.gpsimd.tensor_scalar(out=rounded.rearrange("p (c i j) -> p c j i", i=4, j=PACK),
-                                        in0=w3_raw[b][:].rearrange("p j (c i) -> p c j i", i=4),
-                                        scalar1=1.0, scalar2=0.0, op0=MULT, op1=ADD)
-                for c0, c1 in ((0, 256), (256, N)):
-                    nc.vector.quantize_mx(out=w3_w[:, b * N + c0:b * N + c1].bitcast(FP8X4),
-                                          scales=w3_s[:, b * N + c0:b * N + c1], in_=rounded[:, PACK * c0:PACK * c1])
+        w3_bf, w3_w = {}, {}
+
+        def round_w3(b, slot, copy, run):
+            w3_bf[b] = held(slot, [P, PACK * N], BF16)
+            copy(out=w3_bf[b][:].rearrange("p (c i j) -> p c j i", i=run, j=PACK),
+                 in_=w3_raw[b][:].rearrange("p j (c i) -> p c j i", i=run))
+
+        def quantize_w3(b):
+            for c0, c1 in ((0, 256), (256, N)):
+                nc.vector.quantize_mx(out=w3_w[b][:, c0:c1].bitcast(FP8X4), scales=w3_s[:, b * N + c0:b * N + c1],
+                                      in_=w3_bf[b][:, PACK * c0:PACK * c1])
 
         pieces = [(0, 0, HALF), (1, 0, HALF), (0, HALF, HALF), (1, HALF, HALF), (2, 0, HALF),
                   (2, HALF, CHUNK), (2, HALF + CHUNK, CHUNK)]
@@ -363,10 +345,11 @@ def tile_list_wind_bid_pages_kernel(tc, tab_words, tab_scales, offs, w1, w2_word
 
         def product(i, side, b, o0, width, stop):
             nt, m0 = pieces[i][0:2]
-            words, scales = ((w4_w, w4_s), (w3_w, w3_s))[side]
+            words = (w4_w[:, b * N:(b + 1) * N], w3_w.get(b))[side][:, nt * P:(nt + 1) * P]
+            scales = (w4_s, w3_s)[side]
             cols = slice(b * N + nt * P, b * N + (nt + 1) * P)
             h, c0 = divmod(m0 + o0, HALF)
-            nc.tensor.matmul_mx(out=accs[i][side][:, o0:o0 + width], lhsT=words[:, cols].bitcast(FP8X4),
+            nc.tensor.matmul_mx(out=accs[i][side][:, o0:o0 + width], lhsT=words.bitcast(FP8X4),
                                 lhsT_scale=scales[:, cols], rhs=z_w[b, h][:, c0:c0 + width].bitcast(FP8X4),
                                 rhs_scale=z_s[b, h][:, c0:c0 + width], start=(b == 0), stop=stop)
 
@@ -379,106 +362,98 @@ def tile_list_wind_bid_pages_kernel(tc, tab_words, tab_scales, offs, w1, w2_word
             nc.sync.dma_start(out=out[nt * P:(nt + 1) * P, m0:m0 + width], in_=result[:])
 
         inverse = inverse_weights(("free", 0))
+        add_page("wgs_rows")
         spread = [bank(("early", jb), ("free", 4 + jb)) for jb in range(BLOCKS)]
         for a in range(PASSES):
             for jb in range(BLOCKS):
                 spread_pass(spread[jb], a, 0, jb)
-        early_magnitudes(spread, 0, 1)
-        early_root(0, held("root0", [P, BLOCKS, P], F32)[:])
+        first = early_magnitudes(spread, 0, 1)
+        plain_root(0, first, held("root0", [P, BLOCKS, P], F32)[:])
         turn_root(0, "wgs")
         square(0)
         for a in range(PASSES):
             round_w1(a, 0, held("w1_bf%d" % a, [P, PACK * SPAN], BF16), nc.vector.tensor_copy)
             quantize_w1(a, 0, 0, 1)
             quantize_w1(a, 0, 1, 2)
-        quantize_w1(0, 0, 2, PACK, slot="w1_raw101")
+        weighted = held("w1_raw101", [P, S], F32)
+        nc.vector.tensor_tensor(out=weighted[:], in0=damp[0][:], in1=wgs_t[:], op=MULT)
         quantize_w1(1, 0, 2, PACK)
+        quantize_w1(0, 0, 2, PACK, slot="damp0")
         expect(0, ("free", 1))
-        weigh(0, held("weighted0", [P, S], F32))
+        ready[0] = held("ready0", [P, S], F32)
+        nc.vector.tensor_tensor(out=ready[0][:], in0=expected[0][:], in1=weighted[:], op=MULT)
+        expect(1, ("free", 2))
+        weigh(1, held("outside1", [P, S], F32))
         scatter(0)
-        add_page("damp0")
-        add_page("weighted0")
 
-        early_magnitudes(spread, 1, PACK)
+        early = early_magnitudes(spread, 1, PACK)
         early_roots = held("w1_bf1", [P, PACK - 1, BLOCKS, P], F32)
         for n in range(1, PACK):
-            early_root(n, early_roots[:, n - 1])
+            plain_root(n, early[:, :, n - 1:], early_roots[:, n - 1])
+        late_bf = held("w1_raw101", [P, PASSES, PACK * SPAN], BF16)
+        round_late(0, 0, late_bf[:, 0, 0:2 * SPAN], gpsimd_round, "rows")
         turn_root(1, ("root", 0))
         square(1)
-        expect(1, ("free", 2))
-        weigh(1, held("weighted1", [P, S], F32))
+        dampen(1, "ready1")
         scatter(1)
         expect(2, ("free", 3))
         expect(3, ("early", 0))
-        late_bf = held("magnitude", [P, PASSES, PACK * SPAN], BF16)
-        for a in range(PASSES):
-            round_w1(a, 1, late_bf[:, a], nc.scalar.copy)
-        for a in range(PASSES):
-            quantize_w1(a, 1, 0, PACK)
-        held_back = held("magnitude", [P, 2, S], F32)
         for n in (2, 3):
             turn_root(n, ("a", n - 2))
             square(n)
-            weigh(n, held_back[:, n - 2])
+            weigh_damping(n)
+        round_late(0, 2, late_bf[:, 0, 2 * SPAN:], nc.scalar.copy, "words")
+        round_w1(1, 1, late_bf[:, 1], nc.scalar.copy)
+        late_w = held("late_w", [P, PASSES * SPAN], U32)
+        late_s = held("late_s", [P, PASSES * SPAN], U8)
+        for a in range(PASSES):
+            for t in range(PACK):
+                cols = slice(a * SPAN + t * P, a * SPAN + (t + 1) * P)
+                w1_w[a, 1, t], w1_s[a, 1, t] = late_w[:, cols], late_s[:, cols]
+        nc.vector.quantize_mx(out=late_w[:].bitcast(FP8X4), scales=late_s[:],
+                              in_=late_bf[:].rearrange("p a c -> p (a c)"))
+        held_back = held("w1_raw101", [P, 2, S], F32)
+        for n in (2, 3):
+            ready[n] = held_back[:, n - 2]
+            nc.vector.tensor_tensor(out=ready[n], in0=expected[n][:], in1=damp[n][:], op=MULT)
         scatter(2)
-        add_page("damp2")
         scatter(3)
-        add_page("damp3")
 
         magnitude = late_magnitudes([("root", 1), ("early", 1), ("early", 2), ("early", 3)], "w1_raw110")
         for c in (0, 1):
             sum_pair(0, 0, c, ("late", c))
-        late_roots(magnitude, inverse, "w1_raw000")
+        weighted_roots(PACK, magnitude[:], held("w1_raw000", [P, BLOCKS, PACK, P], F32)[:], inverse)
         for n, after in ((4, ("root", 2)), (5, ("root", 3)), (6, ("a", 2)), (7, ("a", 3))):
             turn_root(n, after)
-        square(4)
-        expect(4, ("late", 3))
-        dampen_psum(4, "weighted4")
-        scatter_copy(4)
-        expect(5, ("late", 2))
-        copy_out(5, "weighted5")
-        for c in (2, 3):
-            sum_pair(0, 0, c, ("a", c + 2))
-        square(5)
-        dampen_sbuf(5, "product5")
-        scatter_copy(5)
-        expect(6, ("root", 4))
-        expect(7, ("root", 5))
-        round_pair(0, 0)
+        round_w3(0, "outside1", gpsimd_round, 1)
+        for n, after, slot in ((4, ("late", 3), "w1_bf0"), (5, ("late", 2), "ready0"), (6, ("root", 4), "ready1"),
+                               (7, ("root", 5), "ready7")):
+            expect(n, after)
+            square(n)
+            copy_out(n)
+            dampen(n, slot)
+            scatter(n)
+            if n == 5:
+                for c in (2, 3):
+                    sum_pair(0, 0, c, ("a", c + 2))
+        round_pair(0, 0, range(CHUNKS))
         for c in range(CHUNKS):
             sum_pair(0, 1, c, ("sum", 0, 0, c))
-        square(6)
-        copy_out(6, "weighted6")
-        dampen_sbuf(6, "product6")
-        scatter_copy(6)
-        copy_out(7, "weighted7")
-        square(7)
-        round_pair(0, 1)
+        round_w3(1, "outside5", nc.scalar.copy, 4)
+        round_pair(0, 1, range(CHUNKS))
+        planes = held("outside7", [P, PACK * T2], BF16)
+        for n in (4, 5, 6):
+            add_plane(planes, n, 0, T2, nc.gpsimd)
+        for c, after in enumerate([("a", 6), ("root", 6), ("root", 7), ("sum", 0, 1, 0)]):
+            turn_back(c, after, planes[:, 3 * T2:] if c == 1 else held("z_bf%d" % c, [P, PACK * CHUNK], BF16)[:])
+        warm = held("warm", [P, 1], F32)
+        nc.scalar.activation(out=warm[:], in_=z_bf[0, CHUNKS - 1][:, 0:1], func=ACT.Sigmoid)
 
-        prepare_w3(("weighted5", "weighted6"))
-        planes = held("w1_raw000", [P, 2, PACK, HALF], BF16)
-        add_plane(planes, 6, 0, HALF)
-        back_afters = [("a", 6), ("root", 6), ("root", 7), ("sum", 0, 1, 0)]
-        for c in (0, 1):
-            turn_back(c, back_afters[c])
-            quantize_z(0, c)
-        dampen_sbuf(7, "pairs11")
-        for c in (2, 3):
-            turn_back(c, back_afters[c])
-        for c, after in enumerate([("sum", 0, 1, 1), ("sum", 0, 1, 2), ("sum", 0, 1, 3), ("back", 0)]):
-            sum_pair(1, 0, c, after)
-        round_pair(1, 0)
-        single = sum_single(6, 1, ("sum", 1, 0, 0))
-        part_pair(planes, 0, ("back", 1))
-        part_pair(planes, 1, ("back", 2))
-        single_words = round_single(single)
-        part_pair(planes, 2, ("back", 3))
-        part_pair(planes, 3, ("a", 7))
-        part_single(planes, 6, 1, single_words, ("sum", 1, 0, 1))
-        scatter_copy(7)
-
-        freed = [("sum", 1, 0, 2), ("sum", 1, 0, 3), ("part", 0), ("part", 1), "single", ("part", 2), ("part", 3),
-                 "parted"]
+        late_words = held("ready7", [P, N + T2], U32)
+        w3_w[0] = late_words[:, 0:N]
+        z_w[0, 0], z_w[0, 1] = late_words[:, N:N + HALF], late_words[:, N + HALF:]
+        freed = [("a", 7), ("sum", 0, 1, 1), ("sum", 0, 1, 2), ("sum", 0, 1, 3), ("back", 0), ("back", 1), ("back", 2),
+                 ("back", 3)]
 
         def first_pass(h):
             for i in (2 * h, 2 * h + 1):
@@ -487,25 +462,32 @@ def tile_list_wind_bid_pages_kernel(tc, tab_words, tab_scales, offs, w1, w2_word
                     product(i, side, 0, 0, HALF, stop=False)
 
         def last_pass(h):
-            chunks = (2 * h, 2 * h + 1)
-            for c in chunks:
-                add_plane(planes, 7, c * CHUNK, CHUNK)
-            for c in chunks:
-                weave(planes, c)
-            for c in chunks:
-                quantize_z(1, c)
             for i in (2 * h, 2 * h + 1):
                 for side in (gate_side, vol_side):
                     for odd in range(2):
                         product(i, side, 1, odd * CHUNK, CHUNK, stop=(odd == 1))
                 finish(i)
 
+        for c in (0, 1):
+            quantize_z(0, c)
+        quantize_w3(0)
         first_pass(0)
-        last_pass(0)
-        z_w[0, 1] = held("damp7", [P, HALF], U32)
+        for h in (1, 0):
+            add_plane(planes, 7, h * HALF, HALF, nc.vector)
         for c in (2, 3):
             quantize_z(0, c)
         first_pass(1)
+        for c in (0, 1):
+            weave(planes, c, nc.vector.tensor_copy)
+        for c in (2, 3):
+            weave(planes, c, nc.scalar.copy)
+        for c in (0, 1):
+            quantize_z(1, c)
+        w3_w[1] = held("z_bf1", [P, N], U32)[:]
+        quantize_w3(1)
+        for c in (2, 3):
+            quantize_z(1, c)
+        last_pass(0)
         last_pass(1)
         for i in range(ahead, len(pieces)):
             open_piece(i, [("piece", i - ahead, side) for side in (gate_side, vol_side)])

@@ -29,6 +29,7 @@ GROUP = P // LISTS
 PAGES = 6
 CHUNK = 256
 CHUNKS = T2 // CHUNK
+SPLIT = 0
 ROW = 12
 HALF = T2 // 2
 
@@ -114,10 +115,10 @@ def tile_list_wind_bid_pages_kernel(tc, tab_words, tab_scales, offs, w1, w2_word
         nc.sync.dma_start(list1[:], offs)
         load_tab(0)
         load_scales(tab_s, tab_scales)
+        load_w2_scales(0)
         nc.sync.dma_start(out=wgs_rows[ROW:P:GROUP], in_=wgs[ROW:P:GROUP])
         load_w2_words(0)
         load_tab(1)
-        load_w2_scales(0)
         load_w1(0, 0)
         load_w1(1, 0, parts=2)
         nc.sync.dma_start(out=wgs_t[:], in_=wgs)
@@ -140,7 +141,7 @@ def tile_list_wind_bid_pages_kernel(tc, tab_words, tab_scales, offs, w1, w2_word
         for a in range(PASSES):
             nc.vector.tensor_copy(out=v_s[a], in_=tab_s[:, a * T:(a + 1) * T].indirect(list1[:]))
         nc.vector.tensor_copy(out=v_w[1][:], in_=tab_w[1][:].indirect(list1[:]))
-        for slot in ("tab_s", "tab_w0", "tab_w1"):
+        for slot in ("tab_s", "tab_w0", "page5"):
             add_page(slot)
 
         w1_w, w1_s, w1_bf = {}, {}, {}
@@ -149,12 +150,12 @@ def tile_list_wind_bid_pages_kernel(tc, tab_words, tab_scales, offs, w1, w2_word
         def gpsimd_round(out, in_):
             nc.gpsimd.tensor_scalar(out=out, in0=in_, scalar1=1.0, scalar2=0.0, op0=MULT, op1=ADD)
 
-        def round_late(a, t0, tile, copy, walk):
-            columns = w1_raw[a, 1][0][:].rearrange("p j (m t) -> p j m t", t=PACK)[:, :, :, t0:t0 + 2]
+        def round_late(a, t0, t1, tile, copy, walk):
+            columns = w1_raw[a, 1][0][:].rearrange("p j (m t) -> p j m t", t=PACK)[:, :, :, t0:t1]
             if walk == "rows":
-                copy(out=tile.rearrange("p (t m j) -> p t m j", t=2, j=PACK), in_=columns.rearrange("p j m t -> p t m j"))
+                copy(out=tile.rearrange("p (t m j) -> p t m j", t=t1 - t0, j=PACK), in_=columns.rearrange("p j m t -> p t m j"))
             else:
-                copy(out=tile.rearrange("p (t m u e) -> p m u t e", t=2, u=2, e=2),
+                copy(out=tile.rearrange("p (t m u e) -> p m u t e", t=t1 - t0, u=2, e=2),
                      in_=columns.rearrange("p (u e) m t -> p m u t e", e=2))
 
         def quantize_late(passes, t0, tile, slot):
@@ -263,7 +264,7 @@ def tile_list_wind_bid_pages_kernel(tc, tab_words, tab_scales, offs, w1, w2_word
 
         def weigh_damping(n):
             plain = damp[n]
-            damp[n] = held({2: "root1", 3: "picked_s"}[n], [P, S], F32)
+            damp[n] = held({2: "w1_raw010", 3: "root1"}[n], [P, S], F32)
             nc.gpsimd.tensor_tensor(out=damp[n][:], in0=plain[:], in1=wgs_t[:], op=MULT)
 
         def scatter(n):
@@ -271,7 +272,7 @@ def tile_list_wind_bid_pages_kernel(tc, tab_words, tab_scales, offs, w1, w2_word
 
         sums, pairs, z_bf = {}, {}, {}
         z_w = {(b, h): held("z_w%d%d" % (b, h), [P, HALF], U32) for b, h in ((1, 0), (1, 1))}
-        z_s = {(b, h): held("z_s%d%d" % (b, h), [P, HALF], U8) for b in range(PASSES) for h in range(2)}
+        z_s = {(b, h): held("z_s%d%d" % (b, h), [P, HALF], U8) for b, h in ((1, 0), (1, 1))}
 
         def sum_pair(b, u, c, after):
             first = PACK * b + 2 * u
@@ -314,8 +315,28 @@ def tile_list_wind_bid_pages_kernel(tc, tab_words, tab_scales, offs, w1, w2_word
             engine.tensor_tensor(out=planes[:, t * T2 + m0:t * T2 + m0 + width], in0=pages[n % PAGES][:, m0:m0 + width],
                                  in1=clim_t[1, t // 2][:, t % 2, m0:m0 + width], op=ADD)
 
+        def sum_single(acc, src, h, first):
+            for block in range(4):
+                m0 = h * HALF + block * P
+                nc.tensor.matmul(out=acc[:, block * P:(block + 1) * P], lhsT=src[:, m0:m0 + P], rhs=ident[:],
+                                 is_transpose=True, start=(first and block == 0), stop=(not first and block == 3))
+
+        def round_single(acc, h):
+            words = held(("warm", "pairs01")[h], [P, BANK], BF16)
+            nc.scalar.copy(out=words[:].rearrange("m (g p e) -> m g p e", g=2, e=2),
+                           in_=acc[:].rearrange("m (g e p) -> m g p e", g=2, e=2))
+            return words
+
+        def part_single(planes, n, h, words, after):
+            back = bank(("parted", h), after)
+            for g in range(2):
+                nc.tensor.transpose(back[:, g * P:(g + 1) * P], words[:].bitcast(F32)[:, g * P:(g + 1) * P], ident[:])
+            m0 = n % PACK * T2 + h * HALF
+            nc.scalar.copy(out=planes[:, m0:m0 + HALF].rearrange("p (g e m) -> p g e m", g=2, e=2),
+                           in_=back[:, 0:CHUNK].bitcast(BF16).rearrange("p (g m e) -> p g e m", g=2, e=2))
+
         def weave(planes, c, copy):
-            z_bf[1, c] = held(("z_bf0", "z_bf1", "pairs12", "pairs13")[c], [P, PACK * CHUNK], BF16)[:]
+            z_bf[1, c] = held(("w1_raw000", "z_bf1", "pairs12", "pairs13")[c], [P, PACK * CHUNK], BF16)[:]
             source = planes[:].rearrange("p (t m) -> p t m", t=PACK)[:, :, c * CHUNK:(c + 1) * CHUNK]
             copy(out=z_bf[1, c].rearrange("p (m i t) -> p m t i", i=4, t=PACK),
                  in_=source.rearrange("p t (m i) -> p m t i", i=4))
@@ -391,19 +412,20 @@ def tile_list_wind_bid_pages_kernel(tc, tab_words, tab_scales, offs, w1, w2_word
         for n in range(1, PACK):
             plain_root(n, early[:, :, n - 1:], early_roots[:, n - 1])
         late_bf = held("w1_raw101", [P, PASSES, PACK * SPAN], BF16)
-        round_late(0, 0, late_bf[:, 0, 0:2 * SPAN], gpsimd_round, "rows")
         turn_root(1, ("root", 0))
         square(1)
-        dampen(1, "ready1")
+        dampen(1, "w1_raw100")
         scatter(1)
         expect(2, ("free", 3))
         expect(3, ("early", 0))
         for n in (2, 3):
             turn_root(n, ("a", n - 2))
             square(n)
+        for a, t0, copy in ((0, 0, nc.scalar.copy), (0, 2, nc.vector.tensor_copy), (1, 0, nc.scalar.copy),
+                            (1, 2, nc.scalar.copy)):
+            round_late(a, t0, t0 + 2, late_bf[:, a, t0 * SPAN:(t0 + 2) * SPAN], copy, "words")
+        for n in (2, 3):
             weigh_damping(n)
-        round_late(0, 2, late_bf[:, 0, 2 * SPAN:], nc.scalar.copy, "words")
-        round_w1(1, 1, late_bf[:, 1], nc.scalar.copy)
         late_w = held("late_w", [P, PASSES * SPAN], U32)
         late_s = held("late_s", [P, PASSES * SPAN], U8)
         for a in range(PASSES):
@@ -421,12 +443,12 @@ def tile_list_wind_bid_pages_kernel(tc, tab_words, tab_scales, offs, w1, w2_word
 
         magnitude = late_magnitudes([("root", 1), ("early", 1), ("early", 2), ("early", 3)], "w1_raw110")
         for c in (0, 1):
-            sum_pair(0, 0, c, ("late", c))
+            sum_pair(0, 0, c, ("root", c + 2))
         weighted_roots(PACK, magnitude[:], held("w1_raw000", [P, BLOCKS, PACK, P], F32)[:], inverse)
-        for n, after in ((4, ("root", 2)), (5, ("root", 3)), (6, ("a", 2)), (7, ("a", 3))):
+        for n, after in ((4, ("late", 0)), (5, ("late", 1)), (6, ("a", 2)), (7, ("a", 3))):
             turn_root(n, after)
         round_w3(0, "outside1", gpsimd_round, 1)
-        for n, after, slot in ((4, ("late", 3), "w1_bf0"), (5, ("late", 2), "ready0"), (6, ("root", 4), "ready1"),
+        for n, after, slot in ((4, ("late", 3), "w1_bf0"), (5, ("late", 2), "ready0"), (6, ("root", 4), "w1_raw100"),
                                (7, ("root", 5), "ready7")):
             expect(n, after)
             square(n)
@@ -441,19 +463,29 @@ def tile_list_wind_bid_pages_kernel(tc, tab_words, tab_scales, offs, w1, w2_word
             sum_pair(0, 1, c, ("sum", 0, 0, c))
         round_w3(1, "outside5", nc.scalar.copy, 4)
         round_pair(0, 1, range(CHUNKS))
-        planes = held("outside7", [P, PACK * T2], BF16)
-        for n in (4, 5, 6):
+        planes = held("outside7", [P, PACK * T2], F32)
+        for n in (4, 5):
             add_plane(planes, n, 0, T2, nc.gpsimd)
+
         for c, after in enumerate([("a", 6), ("root", 6), ("root", 7), ("sum", 0, 1, 0)]):
-            turn_back(c, after, planes[:, 3 * T2:] if c == 1 else held("z_bf%d" % c, [P, PACK * CHUNK], BF16)[:])
+            turn_back(c, after, planes[:, 3 * T2 + CHUNK:3 * T2 + 3 * CHUNK].bitcast(BF16) if c == 1 else held(("w1_raw000", None, "magnitude", "w1_bf1")[c], [P, PACK * CHUNK], BF16)[:])
+
         warm = held("warm", [P, 1], F32)
         nc.scalar.activation(out=warm[:], in_=z_bf[0, CHUNKS - 1][:, 0:1], func=ACT.Sigmoid)
+        singles = [bank(("single", h), ("back", h)) for h in range(2)]
+        for first, src in ((True, clim_t[1, 1][:, 0, :]), (False, pages[0])):
+            for h in range(2):
+                sum_single(singles[h], src, h, first)
+        for h in range(2):
+            part_single(planes, 6, h, round_single(singles[h], h), ("back", 2 + h))
+        early_s = held("pairs01", [P, T2], U8)
+        z_s[0, 0], z_s[0, 1] = early_s[:, 0:HALF], early_s[:, HALF:]
 
         late_words = held("ready7", [P, N + T2], U32)
         w3_w[0] = late_words[:, 0:N]
         z_w[0, 0], z_w[0, 1] = late_words[:, N:N + HALF], late_words[:, N + HALF:]
-        freed = [("a", 7), ("sum", 0, 1, 1), ("sum", 0, 1, 2), ("sum", 0, 1, 3), ("back", 0), ("back", 1), ("back", 2),
-                 ("back", 3)]
+        freed = [("single", 0), ("single", 1), ("parted", 0), ("parted", 1), ("a", 7), ("sum", 0, 1, 1),
+                 ("sum", 0, 1, 2), ("sum", 0, 1, 3)]
 
         def first_pass(h):
             for i in (2 * h, 2 * h + 1):

@@ -89,11 +89,12 @@ def tile_list_wind_bid_pages_kernel(tc, tab_words, tab_scales, offs, w1, w2_word
                               in_=tab_words[a].rearrange("p t i -> p (t i)").bitcast(I32))
 
         def load_w1(a, b, parts=1):
-            depth = PACK // parts
-            w1_raw[a, b] = [held("w1_raw%d%d%d" % (a, b, part), [P, depth, SPAN], F32) for part in range(parts)]
-            rows = w1[SPAN * a:SPAN * (a + 1), SPAN * b:SPAN * (b + 1)].rearrange("(p j) c -> p j c", j=PACK)
+            width = SPAN // parts
+            w1_raw[a, b] = [held("w1_raw%d%d%d" % (a, b, part), [P, PACK, width], F32) for part in range(parts)]
             for part, raw in enumerate(w1_raw[a, b]):
-                nc.sync.dma_start(out=raw[:], in_=rows[:, part * depth:(part + 1) * depth])
+                c0 = SPAN * b + part * width
+                rows = w1[SPAN * a:SPAN * (a + 1), c0:c0 + width]
+                nc.sync.dma_start(out=raw[:], in_=rows.rearrange("(p j) c -> p j c", j=PACK))
 
         def load_w2_words(b):
             words = w2_words[:, :, 2 * SPAN * b:2 * SPAN * (b + 1)]
@@ -115,10 +116,10 @@ def tile_list_wind_bid_pages_kernel(tc, tab_words, tab_scales, offs, w1, w2_word
         nc.sync.dma_start(list1[:], offs)
         load_tab(0)
         load_scales(tab_s, tab_scales)
-        load_w2_scales(0)
         nc.sync.dma_start(out=wgs_rows[ROW:P:GROUP], in_=wgs[ROW:P:GROUP])
         load_w2_words(0)
         load_tab(1)
+        load_w2_scales(0)
         load_w1(0, 0)
         load_w1(1, 0, parts=2)
         nc.sync.dma_start(out=wgs_t[:], in_=wgs)
@@ -172,7 +173,7 @@ def tile_list_wind_bid_pages_kernel(tc, tab_words, tab_scales, offs, w1, w2_word
             rounded = tile[:].rearrange("p (t m u e) -> p m u t e", t=PACK, u=2, e=2)
             parts = len(w1_raw[a, b])
             for part, raw in enumerate(w1_raw[a, b]):
-                copy(out=rounded[:, :, part * 2 // parts:(part + 1) * 2 // parts],
+                copy(out=rounded[:, part * P // parts:(part + 1) * P // parts],
                      in_=raw[:].rearrange("p (u e) (m t) -> p m u t e", t=PACK, e=2))
 
         def quantize_w1(a, b, t0, t1, slot=None):
@@ -264,7 +265,7 @@ def tile_list_wind_bid_pages_kernel(tc, tab_words, tab_scales, offs, w1, w2_word
 
         def weigh_damping(n):
             plain = damp[n]
-            damp[n] = held({2: "w1_raw010", 3: "root1"}[n], [P, S], F32)
+            damp[n] = held({2: "root1", 3: "root2"}[n], [P, S], F32)
             nc.gpsimd.tensor_tensor(out=damp[n][:], in0=plain[:], in1=wgs_t[:], op=MULT)
 
         def scatter(n):
@@ -272,7 +273,7 @@ def tile_list_wind_bid_pages_kernel(tc, tab_words, tab_scales, offs, w1, w2_word
 
         sums, pairs, z_bf = {}, {}, {}
         z_w = {(b, h): held("z_w%d%d" % (b, h), [P, HALF], U32) for b, h in ((1, 0), (1, 1))}
-        z_s = {(b, h): held("z_s%d%d" % (b, h), [P, HALF], U8) for b, h in ((1, 0), (1, 1))}
+        z_s = {(b, h): held("z_s%d%d" % (b, h), [P, HALF], U8) for b in range(PASSES) for h in range(2)}
 
         def sum_pair(b, u, c, after):
             first = PACK * b + 2 * u
@@ -321,8 +322,7 @@ def tile_list_wind_bid_pages_kernel(tc, tab_words, tab_scales, offs, w1, w2_word
                 nc.tensor.matmul(out=acc[:, block * P:(block + 1) * P], lhsT=src[:, m0:m0 + P], rhs=ident[:],
                                  is_transpose=True, start=(first and block == 0), stop=(not first and block == 3))
 
-        def round_single(acc, h):
-            words = held(("warm", "pairs01")[h], [P, BANK], BF16)
+        def round_single(acc, words):
             nc.scalar.copy(out=words[:].rearrange("m (g p e) -> m g p e", g=2, e=2),
                            in_=acc[:].rearrange("m (g e p) -> m g p e", g=2, e=2))
             return words
@@ -396,10 +396,10 @@ def tile_list_wind_bid_pages_kernel(tc, tab_words, tab_scales, offs, w1, w2_word
             round_w1(a, 0, held("w1_bf%d" % a, [P, PACK * SPAN], BF16), nc.vector.tensor_copy)
             quantize_w1(a, 0, 0, 1)
             quantize_w1(a, 0, 1, 2)
-        weighted = held("w1_raw101", [P, S], F32)
-        nc.vector.tensor_tensor(out=weighted[:], in0=damp[0][:], in1=wgs_t[:], op=MULT)
+        quantize_w1(0, 0, 2, PACK, slot="w1_raw101")
         quantize_w1(1, 0, 2, PACK)
-        quantize_w1(0, 0, 2, PACK, slot="damp0")
+        weighted = held("w1_bf0", [P, S], F32)
+        nc.vector.tensor_tensor(out=weighted[:], in0=damp[0][:], in1=wgs_t[:], op=MULT)
         expect(0, ("free", 1))
         ready[0] = held("ready0", [P, S], F32)
         nc.vector.tensor_tensor(out=ready[0][:], in0=expected[0][:], in1=weighted[:], op=MULT)
@@ -411,7 +411,7 @@ def tile_list_wind_bid_pages_kernel(tc, tab_words, tab_scales, offs, w1, w2_word
         early_roots = held("w1_bf1", [P, PACK - 1, BLOCKS, P], F32)
         for n in range(1, PACK):
             plain_root(n, early[:, :, n - 1:], early_roots[:, n - 1])
-        late_bf = held("w1_raw101", [P, PASSES, PACK * SPAN], BF16)
+        late_bf = held("magnitude", [P, PASSES, PACK * SPAN], BF16)
         turn_root(1, ("root", 0))
         square(1)
         dampen(1, "w1_raw100")
@@ -421,20 +421,20 @@ def tile_list_wind_bid_pages_kernel(tc, tab_words, tab_scales, offs, w1, w2_word
         for n in (2, 3):
             turn_root(n, ("a", n - 2))
             square(n)
-        for a, t0, copy in ((0, 0, nc.scalar.copy), (0, 2, nc.vector.tensor_copy), (1, 0, nc.scalar.copy),
-                            (1, 2, nc.scalar.copy)):
-            round_late(a, t0, t0 + 2, late_bf[:, a, t0 * SPAN:(t0 + 2) * SPAN], copy, "words")
-        for n in (2, 3):
             weigh_damping(n)
+        for t0 in (0, 2):
+            round_late(0, t0, t0 + 2, late_bf[:, 0, t0 * SPAN:(t0 + 2) * SPAN], nc.scalar.copy, "words")
+        round_w1(1, 1, late_bf[:, 1], nc.scalar.copy)
         late_w = held("late_w", [P, PASSES * SPAN], U32)
         late_s = held("late_s", [P, PASSES * SPAN], U8)
         for a in range(PASSES):
             for t in range(PACK):
                 cols = slice(a * SPAN + t * P, a * SPAN + (t + 1) * P)
                 w1_w[a, 1, t], w1_s[a, 1, t] = late_w[:, cols], late_s[:, cols]
-        nc.vector.quantize_mx(out=late_w[:].bitcast(FP8X4), scales=late_s[:],
-                              in_=late_bf[:].rearrange("p a c -> p (a c)"))
-        held_back = held("w1_raw101", [P, 2, S], F32)
+        for a in range(PASSES):
+            cols = slice(a * SPAN, (a + 1) * SPAN)
+            nc.vector.quantize_mx(out=late_w[:, cols].bitcast(FP8X4), scales=late_s[:, cols], in_=late_bf[:, a])
+        held_back = held("magnitude", [P, 2, S], F32)
         for n in (2, 3):
             ready[n] = held_back[:, n - 2]
             nc.vector.tensor_tensor(out=ready[n], in0=expected[n][:], in1=damp[n][:], op=MULT)
@@ -448,8 +448,7 @@ def tile_list_wind_bid_pages_kernel(tc, tab_words, tab_scales, offs, w1, w2_word
         for n, after in ((4, ("late", 0)), (5, ("late", 1)), (6, ("a", 2)), (7, ("a", 3))):
             turn_root(n, after)
         round_w3(0, "outside1", gpsimd_round, 1)
-        for n, after, slot in ((4, ("late", 3), "w1_bf0"), (5, ("late", 2), "ready0"), (6, ("root", 4), "w1_raw100"),
-                               (7, ("root", 5), "ready7")):
+        for n, after, slot in ((4, ("late", 3), "w1_bf0"), (5, ("late", 2), "ready0"), (6, ("root", 4), "w1_raw100")):
             expect(n, after)
             square(n)
             copy_out(n)
@@ -458,34 +457,40 @@ def tile_list_wind_bid_pages_kernel(tc, tab_words, tab_scales, offs, w1, w2_word
             if n == 5:
                 for c in (2, 3):
                     sum_pair(0, 0, c, ("a", c + 2))
+        square(7)
         round_pair(0, 0, range(CHUNKS))
         for c in range(CHUNKS):
             sum_pair(0, 1, c, ("sum", 0, 0, c))
         round_w3(1, "outside5", nc.scalar.copy, 4)
         round_pair(0, 1, range(CHUNKS))
-        planes = held("outside7", [P, PACK * T2], F32)
+        planes = held("outside6", [P, PACK * T2], F32)
         for n in (4, 5):
             add_plane(planes, n, 0, T2, nc.gpsimd)
-
+        late_words = held("wgs_rows", [P, PASSES * N + T2], U32)
+        for h in range(2):
+            z_w[0, h] = late_words[:, PASSES * N + h * HALF:PASSES * N + (h + 1) * HALF]
         for c, after in enumerate([("a", 6), ("root", 6), ("root", 7), ("sum", 0, 1, 0)]):
-            turn_back(c, after, planes[:, 3 * T2 + CHUNK:3 * T2 + 3 * CHUNK].bitcast(BF16) if c == 1 else held(("w1_raw000", None, "magnitude", "w1_bf1")[c], [P, PACK * CHUNK], BF16)[:])
-
+            turn_back(c, after, held(("w1_raw000", "z_bf1", "magnitude", "w1_bf1")[c], [P, PACK * CHUNK], BF16)[:])
+            quantize_z(0, c)
+        for b in range(PASSES):
+            w3_w[b] = late_words[:, b * N:(b + 1) * N]
+            quantize_w3(b)
+        expect(7, ("back", 1))
+        copy_out(7, "wgs_t")
+        nc.vector.tensor_tensor(out=pages[1][:].indirect(list2[:]), in0=outside[7][:], in1=damp[7][:], op=MULT)
         warm = held("warm", [P, 1], F32)
         nc.scalar.activation(out=warm[:], in_=z_bf[0, CHUNKS - 1][:, 0:1], func=ACT.Sigmoid)
-        singles = [bank(("single", h), ("back", h)) for h in range(2)]
+        singles = [bank(("single", h), ("back", 2 + h)) for h in range(2)]
         for first, src in ((True, clim_t[1, 1][:, 0, :]), (False, pages[0])):
             for h in range(2):
                 sum_single(singles[h], src, h, first)
+        single_words = held("warm", [P, 2 * BANK], BF16)
         for h in range(2):
-            part_single(planes, 6, h, round_single(singles[h], h), ("back", 2 + h))
-        early_s = held("pairs01", [P, T2], U8)
-        z_s[0, 0], z_s[0, 1] = early_s[:, 0:HALF], early_s[:, HALF:]
+            part_single(planes, 6, h, round_single(singles[h], single_words[:, h * BANK:(h + 1) * BANK]),
+                        (("back", 0), ("a", 7))[h])
 
-        late_words = held("ready7", [P, N + T2], U32)
-        w3_w[0] = late_words[:, 0:N]
-        z_w[0, 0], z_w[0, 1] = late_words[:, N:N + HALF], late_words[:, N + HALF:]
-        freed = [("single", 0), ("single", 1), ("parted", 0), ("parted", 1), ("a", 7), ("sum", 0, 1, 1),
-                 ("sum", 0, 1, 2), ("sum", 0, 1, 3)]
+        freed = [("single", 0), ("single", 1), ("parted", 0), ("parted", 1), ("sum", 0, 1, 1),
+                 ("sum", 0, 1, 2), ("sum", 0, 1, 3), ("root", 5)]
 
         def first_pass(h):
             for i in (2 * h, 2 * h + 1):
@@ -500,24 +505,13 @@ def tile_list_wind_bid_pages_kernel(tc, tab_words, tab_scales, offs, w1, w2_word
                         product(i, side, 1, odd * CHUNK, CHUNK, stop=(odd == 1))
                 finish(i)
 
-        for c in (0, 1):
-            quantize_z(0, c)
-        quantize_w3(0)
-        first_pass(0)
-        for h in (1, 0):
-            add_plane(planes, 7, h * HALF, HALF, nc.vector)
-        for c in (2, 3):
-            quantize_z(0, c)
         first_pass(1)
-        for c in (0, 1):
-            weave(planes, c, nc.vector.tensor_copy)
-        for c in (2, 3):
-            weave(planes, c, nc.scalar.copy)
-        for c in (0, 1):
-            quantize_z(1, c)
-        w3_w[1] = held("z_bf1", [P, N], U32)[:]
-        quantize_w3(1)
-        for c in (2, 3):
+        first_pass(0)
+        for h in range(2):
+            add_plane(planes, 7, h * HALF, HALF, nc.vector)
+        for c in range(CHUNKS):
+            weave(planes, c, nc.scalar.copy if c % 2 else nc.vector.tensor_copy)
+        for c in range(CHUNKS):
             quantize_z(1, c)
         last_pass(0)
         last_pass(1)

@@ -273,7 +273,7 @@ def tile_list_wind_bid_pages_kernel(tc, tab_words, tab_scales, offs, w1, w2_word
 
         sums, pairs, z_bf = {}, {}, {}
         z_w = {(b, h): held("z_w%d%d" % (b, h), [P, HALF], U32) for b, h in ((1, 0), (1, 1))}
-        z_s = {(b, h): held("z_s%d%d" % (b, h), [P, HALF], U8) for b in range(PASSES) for h in range(2)}
+        z_s = {(b, h): held("z_s%d%d" % (b, h), [P, HALF], U8) for b, h in ((0, 0), (1, 0), (1, 1))}
 
         def sum_pair(b, u, c, after):
             first = PACK * b + 2 * u
@@ -389,7 +389,9 @@ def tile_list_wind_bid_pages_kernel(tc, tab_words, tab_scales, offs, w1, w2_word
             for jb in range(BLOCKS):
                 spread_pass(spread[jb], a, 0, jb)
         first = early_magnitudes(spread, 0, 1)
-        plain_root(0, first, held("root0", [P, BLOCKS, P], F32)[:])
+        roots[0] = held("root0", [P, BLOCKS, P], F32)[:]
+        for jb in range(BLOCKS):
+            nc.scalar.activation(out=roots[0][:, jb], in_=first[:, jb, 0, :], func=ACT.Abs_reciprocal_sqrt, bias=1.0)
         turn_root(0, "wgs")
         square(0)
         for a in range(PASSES):
@@ -466,15 +468,14 @@ def tile_list_wind_bid_pages_kernel(tc, tab_words, tab_scales, offs, w1, w2_word
         planes = held("outside6", [P, PACK * T2], F32)
         for n in (4, 5):
             add_plane(planes, n, 0, T2, nc.gpsimd)
-        late_words = held("wgs_rows", [P, PASSES * N + T2], U32)
-        for h in range(2):
-            z_w[0, h] = late_words[:, PASSES * N + h * HALF:PASSES * N + (h + 1) * HALF]
+        late_words = held("wgs_rows", [P, N + HALF], U32)
+        z_w[0, 0] = late_words[:, N:]
         for c, after in enumerate([("a", 6), ("root", 6), ("root", 7), ("sum", 0, 1, 0)]):
             turn_back(c, after, held(("w1_raw000", "z_bf1", "magnitude", "w1_bf1")[c], [P, PACK * CHUNK], BF16)[:])
-            quantize_z(0, c)
-        for b in range(PASSES):
-            w3_w[b] = late_words[:, b * N:(b + 1) * N]
-            quantize_w3(b)
+            if c < 2:
+                quantize_z(0, c)
+        w3_w[0] = late_words[:, 0:N]
+        quantize_w3(0)
         expect(7, ("back", 1))
         copy_out(7, "wgs_t")
         nc.vector.tensor_tensor(out=pages[1][:].indirect(list2[:]), in0=outside[7][:], in1=damp[7][:], op=MULT)
@@ -505,13 +506,20 @@ def tile_list_wind_bid_pages_kernel(tc, tab_words, tab_scales, offs, w1, w2_word
                         product(i, side, 1, odd * CHUNK, CHUNK, stop=(odd == 1))
                 finish(i)
 
-        first_pass(1)
         first_pass(0)
+        z_w[0, 1], z_s[0, 1] = held("damp7", [P, HALF], U32), held("warm", [P, HALF], U8)
+        for c in (2, 3):
+            quantize_z(0, c)
+        first_pass(1)
         for h in range(2):
             add_plane(planes, 7, h * HALF, HALF, nc.vector)
         for c in range(CHUNKS):
             weave(planes, c, nc.scalar.copy if c % 2 else nc.vector.tensor_copy)
-        for c in range(CHUNKS):
+        for c in (0, 1):
+            quantize_z(1, c)
+        w3_w[1] = held("z_bf1", [P, N], U32)[:]
+        quantize_w3(1)
+        for c in (2, 3):
             quantize_z(1, c)
         last_pass(0)
         last_pass(1)

@@ -479,8 +479,6 @@ def tile_list_wind_bid_pages_kernel(tc, tab_words, tab_scales, offs, w1, w2_word
         expect(7, ("back", 1))
         copy_out(7, "wgs_t")
         nc.vector.tensor_tensor(out=pages[1][:].indirect(list2[:]), in0=outside[7][:], in1=damp[7][:], op=MULT)
-        warm = held("warm", [P, 1], F32)
-        nc.scalar.activation(out=warm[:], in_=z_bf[0, CHUNKS - 1][:, 0:1], func=ACT.Sigmoid)
         singles = [bank(("single", h), ("back", 2 + h)) for h in range(2)]
         for first, src in ((True, clim_t[1, 1][:, 0, :]), (False, pages[0])):
             for h in range(2):

@@ -29,7 +29,6 @@ GROUP = P // LISTS
 PAGES = 6
 CHUNK = 256
 CHUNKS = T2 // CHUNK
-SPLIT = 0
 ROW = 12
 HALF = T2 // 2
 
@@ -158,15 +157,6 @@ def tile_list_wind_bid_pages_kernel(tc, tab_words, tab_scales, offs, w1, w2_word
             else:
                 copy(out=tile.rearrange("p (t m u e) -> p m u t e", t=t1 - t0, u=2, e=2),
                      in_=columns.rearrange("p (u e) m t -> p m u t e", e=2))
-
-        def quantize_late(passes, t0, tile, slot):
-            words = held(slot, [P, len(passes) * 2 * P], U32)
-            scales = held("w1_s%d1%d" % (passes[0], t0), [P, len(passes) * 2 * P], U8)
-            nc.vector.quantize_mx(out=words[:].bitcast(FP8X4), scales=scales[:], in_=tile)
-            for i, a in enumerate(passes):
-                for t in range(2):
-                    cols = slice((2 * i + t) * P, (2 * i + t + 1) * P)
-                    w1_w[a, 1, t0 + t], w1_s[a, 1, t0 + t] = words[:, cols], scales[:, cols]
 
         def round_w1(a, b, tile, copy):
             w1_bf[a, b] = tile
@@ -384,22 +374,29 @@ def tile_list_wind_bid_pages_kernel(tc, tab_words, tab_scales, offs, w1, w2_word
 
         inverse = inverse_weights(("free", 0))
         add_page("wgs_rows")
+        own_w = held("picked", [P, PASSES, P], U16)
+        own_s = held("own_s", [P, PASSES, P], U8)
+        nc.scalar.copy(out=own_w[:], in_=w2_w[0][:].bitcast(U16).rearrange("p (a m t) -> p a m t", a=PASSES, t=PACK)[:, :, :, 0])
+        nc.vector.tensor_copy(out=own_s[:], in_=w2_s[0][:].rearrange("p (a m t) -> p a m t", a=PASSES, t=PACK)[:, :, :, 0])
+        acc = bank(("root", 0), "wgs")
+        for a in range(PASSES):
+            nc.tensor.matmul_mx(out=acc[:], lhsT=own_w[:, a].bitcast(FP4X4), lhsT_scale=own_s[:, a],
+                                rhs=v_w[a][:].bitcast(FP8X4), rhs_scale=v_s[a], start=(a == 0), stop=(a == PASSES - 1))
+        first = held("first", [P, S], F32)
+        nc.scalar.activation(out=first[:], in_=acc[:], func=ACT.Abs)
+        root = held("root0", [P, S], F32)
+        nc.scalar.activation(out=root[:], in_=first[:], func=ACT.Abs_reciprocal_sqrt, bias=1.0)
+        damp[0] = held("damp0", [P, S], F32)
+        nc.scalar.activation(out=damp[0][:], in_=root[:], func=ACT.Square)
         spread = [bank(("early", jb), ("free", 4 + jb)) for jb in range(BLOCKS)]
         for a in range(PASSES):
             for jb in range(BLOCKS):
                 spread_pass(spread[jb], a, 0, jb)
-        first = early_magnitudes(spread, 0, 1)
-        roots[0] = held("root0", [P, BLOCKS, P], F32)[:]
-        for jb in range(BLOCKS):
-            nc.scalar.activation(out=roots[0][:, jb], in_=first[:, jb, 0, :], func=ACT.Abs_reciprocal_sqrt, bias=1.0)
-        turn_root(0, "wgs")
-        square(0)
         for a in range(PASSES):
             round_w1(a, 0, held("w1_bf%d" % a, [P, PACK * SPAN], BF16), nc.vector.tensor_copy)
             quantize_w1(a, 0, 0, 1)
             quantize_w1(a, 0, 1, 2)
-        quantize_w1(0, 0, 2, PACK, slot="w1_raw101")
-        quantize_w1(1, 0, 2, PACK)
+            quantize_w1(a, 0, 2, PACK)
         weighted = held("w1_bf0", [P, S], F32)
         nc.vector.tensor_tensor(out=weighted[:], in0=damp[0][:], in1=wgs_t[:], op=MULT)
         expect(0, ("free", 1))
@@ -410,18 +407,18 @@ def tile_list_wind_bid_pages_kernel(tc, tab_words, tab_scales, offs, w1, w2_word
         scatter(0)
 
         early = early_magnitudes(spread, 1, PACK)
-        early_roots = held("w1_bf1", [P, PACK - 1, BLOCKS, P], F32)
+        early_roots = held("early_roots", [P, PACK - 1, BLOCKS, P], F32)
         for n in range(1, PACK):
             plain_root(n, early[:, :, n - 1:], early_roots[:, n - 1])
         late_bf = held("magnitude", [P, PASSES, PACK * SPAN], BF16)
-        turn_root(1, ("root", 0))
+        turn_root(1, ("a", 0))
         square(1)
         dampen(1, "w1_raw100")
         scatter(1)
         expect(2, ("free", 3))
         expect(3, ("early", 0))
         for n in (2, 3):
-            turn_root(n, ("a", n - 2))
+            turn_root(n, (("a", 1), ("root", 1))[n - 2])
             square(n)
             weigh_damping(n)
         for t0 in (0, 2):
@@ -443,7 +440,7 @@ def tile_list_wind_bid_pages_kernel(tc, tab_words, tab_scales, offs, w1, w2_word
         scatter(2)
         scatter(3)
 
-        magnitude = late_magnitudes([("root", 1), ("early", 1), ("early", 2), ("early", 3)], "w1_raw110")
+        magnitude = late_magnitudes([("root", 0), ("early", 1), ("early", 2), ("early", 3)], "w1_raw110")
         for c in (0, 1):
             sum_pair(0, 0, c, ("root", c + 2))
         weighted_roots(PACK, magnitude[:], held("w1_raw000", [P, BLOCKS, PACK, P], F32)[:], inverse)
@@ -479,6 +476,8 @@ def tile_list_wind_bid_pages_kernel(tc, tab_words, tab_scales, offs, w1, w2_word
         expect(7, ("back", 1))
         copy_out(7, "wgs_t")
         nc.vector.tensor_tensor(out=pages[1][:].indirect(list2[:]), in0=outside[7][:], in1=damp[7][:], op=MULT)
+        warm = held("warm", [P, 1], F32)
+        nc.scalar.activation(out=warm[:], in_=outside[7][:, 0:1], func=ACT.Sigmoid)
         singles = [bank(("single", h), ("back", 2 + h)) for h in range(2)]
         for first, src in ((True, clim_t[1, 1][:, 0, :]), (False, pages[0])):
             for h in range(2):
@@ -512,7 +511,7 @@ def tile_list_wind_bid_pages_kernel(tc, tab_words, tab_scales, offs, w1, w2_word
         for h in range(2):
             add_plane(planes, 7, h * HALF, HALF, nc.vector)
         for c in range(CHUNKS):
-            weave(planes, c, nc.scalar.copy if c % 2 else nc.vector.tensor_copy)
+            weave(planes, c, nc.scalar.copy if c else nc.vector.tensor_copy)
         for c in (0, 1):
             quantize_z(1, c)
         w3_w[1] = held("z_bf1", [P, N], U32)[:]

from contextlib import ExitStack

import concourse.mybir as mybir
from concourse.masks import make_identity

K, T, S, H, T2, N = 1024, 2048, 512, 1024, 1024, 384
FLOPS = 2 * (2 * K * H * S + 2 * H * N * T2)

F32 = mybir.dt.float32
BF16 = mybir.dt.bfloat16
I32 = mybir.dt.int32
U32 = mybir.dt.uint32
U16 = mybir.dt.uint16
U8 = mybir.dt.uint8
FP8X4 = mybir.dt.float8_e4m3fn_x4
FP4X4 = mybir.dt.float4_e2m1fn_x4
ACT = mybir.ActivationFunctionType
MULT = mybir.AluOpType.mult
ADD = mybir.AluOpType.add

P = 128
PACK = 4
SPAN = P * PACK
PASSES = 2
BANK = 512
BLOCKS = S // P
LISTS = 8
GROUP = P // LISTS
PAGES = 6
CHUNK = 256
CHUNKS = T2 // CHUNK
ROW = 12
HALF = T2 // 2


def tile_list_wind_bid_pages_kernel(tc, tab_words, tab_scales, offs, w1, w2_words, w2_scales, offs2, wgs,
                                                 clim, w3, w4_words, w4_scales, out):
    nc = tc.nc
    with ExitStack() as ctx:
        keep = ctx.enter_context(tc.tile_pool(name="keep", bufs=1))
        psum = ctx.enter_context(tc.psum_pool(name="psum", bufs=1))

        def held(slot, shape, dtype):
            return keep.tile(shape, dtype, name=slot, align_bytes=64)

        banks = {("free", i): i for i in range(8)}

        def bank(step, after):
            banks[step] = banks[after]
            name = "bank%d" % banks[step]
            return psum.tile([P, BANK], F32, name=name, tag=name)

        list1 = keep.tile([P, S // GROUP], U16, name="list1")
        list2 = keep.tile([P, S // GROUP], U16, name="list2")
        tab_s = held("tab_s", [P, PASSES * T], U8)
        w2_s = [held("w2_s%d" % b, [P, PASSES * SPAN], U8) for b in range(PASSES)]
        w4_s = held("w4_s", [P, PASSES * N], U8)
        wgs_rows = held("wgs_rows", [P, S], F32)
        for tile in (tab_s, wgs_rows, w2_s[0], w2_s[1], w4_s):
            nc.vector.memset(tile[:].bitcast(I32), 0)
        ident = held("ident", [P, P], F32)
        nc.vector.memset(ident[:], 0.0)
        make_identity(nc, ident[:], nomemset=True)
        pages = [held("page%d" % n, [P, T2], F32) for n in range(2)]
        for tile in pages:
            nc.vector.memset(tile[:].bitcast(I32), 0)

        def add_page(slot):
            pages.append(held(slot, [P, T2], F32))
            nc.gpsimd.memset(pages[-1][:].bitcast(I32), 0)

        tab_w = [held("tab_w%d" % a, [P, T], U32) for a in range(PASSES)]
        w2_w = [held("w2_w%d" % b, [P, PASSES * 2 * SPAN], U8) for b in range(PASSES)]
        w1_raw = {}
        wgs_t = held("wgs_t", [P, S], F32)
        clim_t = {(b, u): held("clim%d%d" % (b, u), [P, 2, T2], F32) for b in range(PASSES) for u in range(2)}
        w3_raw = [held("w3_raw%d" % b, [P, PACK, N], F32) for b in range(PASSES)]
        w4_w = held("w4_w", [P, PASSES * N], U32)

        def load_scales(tile, src):
            view = tile[:].bitcast(I32).rearrange("p (a c) -> p a c", a=PASSES)
            rows = src.bitcast(I32).rearrange("a (q r) c -> r q a c", r=4)
            for r in range(4):
                nc.sync.dma_start(out=view[r:P:32], in_=rows[r])

        def load_tab(a):
            nc.sync.dma_start(out=tab_w[a][:].bitcast(I32),
                              in_=tab_words[a].rearrange("p t i -> p (t i)").bitcast(I32))

        def load_w1(a, b, parts=1):
            width = SPAN // parts
            w1_raw[a, b] = [held("w1_raw%d%d%d" % (a, b, part), [P, PACK, width], F32) for part in range(parts)]
            for part, raw in enumerate(w1_raw[a, b]):
                c0 = SPAN * b + part * width
                rows = w1[SPAN * a:SPAN * (a + 1), c0:c0 + width]
                nc.sync.dma_start(out=raw[:], in_=rows.rearrange("(p j) c -> p j c", j=PACK))

        def load_w2_words(b):
            words = w2_words[:, :, 2 * SPAN * b:2 * SPAN * (b + 1)]
            nc.sync.dma_start(out=w2_w[b][:].bitcast(I32).rearrange("p (a c) -> p a c", a=PASSES),
                              in_=words.bitcast(I32).rearrange("a p c -> p a c"))

        def load_w2_scales(b):
            load_scales(w2_s[b], w2_scales[:, :, SPAN * b:SPAN * (b + 1)])

        def load_clim(b):
            rows = clim[SPAN * b:SPAN * (b + 1), :].rearrange("(p j) c -> p j c", j=PACK)
            for u in range(2):
                nc.sync.dma_start(out=clim_t[b, u][:], in_=rows[:, 2 * u:2 * u + 2, :])

        def load_w3(b):
            rows = w3[SPAN * b:SPAN * (b + 1), :]
            nc.sync.dma_start(out=w3_raw[b][:], in_=rows.rearrange("(p j) c -> p j c", j=PACK))

        nc.sync.dma_start(list1[:], offs)
        load_tab(0)
        load_scales(tab_s, tab_scales)
        nc.sync.dma_start(out=wgs_rows[ROW:P:GROUP], in_=wgs[ROW:P:GROUP])
        load_w2_words(0)
        load_tab(1)
        load_w2_scales(0)
        load_w1(0, 0)
        load_w1(1, 0, parts=2)
        nc.sync.dma_start(out=wgs_t[:], in_=wgs)
        nc.sync.dma_start(list2[:], offs2)
        load_w1(0, 1)
        load_w2_words(1)
        load_w2_scales(1)
        load_w1(1, 1)
        load_clim(0)
        load_w3(0)
        load_w3(1)
        nc.sync.dma_start(out=w4_w[:].bitcast(I32).rearrange("p (a c) -> p a c", a=PASSES),
                          in_=w4_words.rearrange("a p c i -> p a (c i)").bitcast(I32))
        load_scales(w4_s, w4_scales)
        load_clim(1)

        v_w = [held("v_w%d" % a, [P, S], U32) for a in range(PASSES)]
        v_s = [held("v_s%d" % a, [P, S], U8)[:] for a in range(PASSES)]
        nc.vector.tensor_copy(out=v_w[0][:], in_=tab_w[0][:].indirect(list1[:]))
        for a in range(PASSES):
            nc.vector.tensor_copy(out=v_s[a], in_=tab_s[:, a * T:(a + 1) * T].indirect(list1[:]))
        nc.vector.tensor_copy(out=v_w[1][:], in_=tab_w[1][:].indirect(list1[:]))
        for slot in ("tab_s", "tab_w0", "page5"):
            add_page(slot)

        w1_w, w1_s, w1_bf = {}, {}, {}
        roots, turned, damp, expected, outside, ready = {}, {}, {}, {}, {}, {}

        def gpsimd_round(out, in_):
            nc.gpsimd.tensor_scalar(out=out, in0=in_, scalar1=1.0, scalar2=0.0, op0=MULT, op1=ADD)

        def round_late(a, t0, t1, tile, copy, walk):
            columns = w1_raw[a, 1][0][:].rearrange("p j (m t) -> p j m t", t=PACK)[:, :, :, t0:t1]
            if walk == "rows":
                copy(out=tile.rearrange("p (t m j) -> p t m j", t=t1 - t0, j=PACK), in_=columns.rearrange("p j m t -> p t m j"))
            else:
                copy(out=tile.rearrange("p (t m u e) -> p m u t e", t=t1 - t0, u=2, e=2),
                     in_=columns.rearrange("p (u e) m t -> p m u t e", e=2))

        def round_w1(a, b, tile, copy):
            w1_bf[a, b] = tile
            rounded = tile[:].rearrange("p (t m u e) -> p m u t e", t=PACK, u=2, e=2)
            parts = len(w1_raw[a, b])
            for part, raw in enumerate(w1_raw[a, b]):
                copy(out=rounded[:, part * P // parts:(part + 1) * P // parts],
                     in_=raw[:].rearrange("p (u e) (m t) -> p m u t e", t=PACK, e=2))

        def quantize_w1(a, b, t0, t1, slot=None):
            name = "%d%d%d" % (a, b, t0)
            words = held(slot or "w1_w" + name, [P, (t1 - t0) * P], U32)
            scales = held("w1_s" + name, [P, (t1 - t0) * P], U8)
            nc.vector.quantize_mx(out=words[:].bitcast(FP8X4), scales=scales[:],
                                  in_=w1_bf[a, b][:, SPAN * t0:SPAN * t1])
            for t in range(t0, t1):
                cols = slice((t - t0) * P, (t - t0 + 1) * P)
                w1_w[a, b, t], w1_s[a, b, t] = words[:, cols], scales[:, cols]

        def spread_pass(acc, a, b, jb):
            cols = slice(jb * P, (jb + 1) * P)
            nc.tensor.matmul_mx(out=acc[:], lhsT=v_w[a][:, cols].bitcast(FP8X4), lhsT_scale=v_s[a][:, cols],
                                rhs=w2_w[b][:, 2 * SPAN * a:2 * SPAN * (a + 1)].bitcast(FP4X4),
                                rhs_scale=w2_s[b][:, a * SPAN:(a + 1) * SPAN], start=(a == 0), stop=(a == PASSES - 1))

        def take_magnitude(tile, acc, t0, t1):
            nc.scalar.activation(out=tile, in_=acc[:].rearrange("j (p t) -> j t p", t=PACK)[:, t0:t1], func=ACT.Abs)

        def early_magnitudes(accs, t0, t1):
            tile = held("magnitude", [P, BLOCKS, t1 - t0, P], F32)
            for jb in range(BLOCKS):
                take_magnitude(tile[:, jb], accs[jb], t0, t1)
            return tile[:]

        def plain_root(n, magnitude, tile):
            roots[n] = tile
            nc.scalar.activation(out=tile, in_=magnitude[:, :, 0, :], func=ACT.Abs_reciprocal_sqrt, bias=1.0)

        def inverse_weights(after):
            acc = bank("wgs", after)
            for jb in range(BLOCKS):
                nc.tensor.transpose(acc[:, jb * P:(jb + 1) * P], wgs_rows[:, jb * P:(jb + 1) * P], ident[:])
            inverse = held("inverse", [P, BLOCKS * LISTS], F32)
            picked = held("picked", [P, BLOCKS * LISTS], F32)
            nc.scalar.activation(out=picked[:], in_=acc[:, ROW:BANK:GROUP], func=ACT.Abs_reciprocal_sqrt)
            nc.scalar.activation(out=inverse[:], in_=picked[:], func=ACT.Square)
            return inverse

        def late_magnitudes(afters, slot):
            tile = held(slot, [P, BLOCKS, PACK, P], F32)
            for jb in range(BLOCKS):
                acc = bank(("late", jb), afters[jb])
                for a in range(PASSES):
                    spread_pass(acc, a, 1, jb)
                take_magnitude(tile[:, jb], acc, 0, PACK)
            return tile

        def weighted_roots(first, magnitude, tile, inverse):
            for jb in range(BLOCKS):
                for g in range(LISTS):
                    factor = inverse[:, LISTS * jb + g:LISTS * jb + g + 1]
                    places = slice(g * GROUP, (g + 1) * GROUP)
                    nc.scalar.activation(out=tile[:, jb, :, places], in_=magnitude[:, jb, :, places],
                                         func=ACT.Abs_reciprocal_sqrt, bias=factor, scale=factor)
            for t in range(tile.shape[2]):
                roots[first + t] = tile[:, :, t, :]

        def turn_root(n, after):
            acc = turned[n] = bank(("root", n), after)
            for jb in range(BLOCKS):
                nc.tensor.transpose(acc[:, jb * P:(jb + 1) * P], roots[n][:, jb, :], ident[:])

        def square(n):
            damp[n] = held("damp%d" % n, [P, S], F32)
            nc.scalar.activation(out=damp[n][:], in_=turned[n][:], func=ACT.Square)

        def expect(n, after):
            b, t = divmod(n, PACK)
            acc = expected[n] = bank(("a", n), after)
            for a in range(PASSES):
                nc.tensor.matmul_mx(out=acc[:], lhsT=w1_w[a, b, t].bitcast(FP8X4), lhsT_scale=w1_s[a, b, t],
                                    rhs=v_w[a][:].bitcast(FP8X4), rhs_scale=v_s[a],
                                    start=(a == 0), stop=(a == PASSES - 1))

        def weigh(n, tile):
            outside[n] = tile
            nc.vector.tensor_tensor(out=tile[:], in0=expected[n][:], in1=wgs_t[:], op=MULT)

        def copy_out(n, slot=None):
            outside[n] = held(slot or "outside%d" % n, [P, S], F32)
            nc.scalar.copy(out=outside[n][:], in_=expected[n][:])

        def dampen(n, slot):
            ready[n] = held(slot, [P, S], F32)
            nc.gpsimd.tensor_tensor(out=ready[n][:], in0=outside[n][:], in1=damp[n][:], op=MULT)

        def weigh_damping(n):
            plain = damp[n]
            damp[n] = held({2: "root1", 3: "root2"}[n], [P, S], F32)
            nc.gpsimd.tensor_tensor(out=damp[n][:], in0=plain[:], in1=wgs_t[:], op=MULT)

        def scatter(n):
            nc.vector.tensor_copy(out=pages[n % PAGES][:].indirect(list2[:]), in_=ready[n][:])

        sums, pairs, z_bf = {}, {}, {}
        z_w = {(b, h): held("z_w%d%d" % (b, h), [P, HALF], U32) for b, h in ((1, 0), (1, 1))}
        z_s = {(b, h): held("z_s%d%d" % (b, h), [P, HALF], U8) for b, h in ((0, 0), (1, 0), (1, 1))}

        def sum_pair(b, u, c, after):
            first = PACK * b + 2 * u
            sources = [(0, clim_t[b, u][:, 0, :]), (1, clim_t[b, u][:, 1, :]),
                       (0, pages[first % PAGES]), (1, pages[(first + 1) % PAGES])]
            acc = sums[u, c] = bank(("sum", b, u, c), after)
            for step, (e, src) in enumerate(sources):
                for g in range(2):
                    m0 = c * CHUNK + g * P
                    o0 = (2 * g + e) * P
                    nc.tensor.matmul(out=acc[:, o0:o0 + P], lhsT=src[:, m0:m0 + P], rhs=ident[:],
                                     is_transpose=True, start=(step == 0 and g == 0),
                                     stop=(step == len(sources) - 1 and g == 1))

        def round_pair(b, u, chunks):
            for c in chunks:
                pairs[b, u, c] = held("pairs%d%d" % (u, c), [P, BANK], BF16)
                nc.scalar.copy(out=pairs[b, u, c][:].rearrange("m (g p e) -> m g p e", g=2, e=2),
                               in_=sums[u, c][:].rearrange("m (g e p) -> m g p e", g=2, e=2))

        def turn_back(c, after, tile):
            back = bank(("back", c), after)
            for u in (1, 0):
                for g in range(2):
                    o0 = (2 * g + u) * P
                    nc.tensor.transpose(back[:, o0:o0 + P], pairs[0, u, c][:].bitcast(F32)[:, g * P:(g + 1) * P],
                                        ident[:])
            z_bf[0, c] = tile
            nc.scalar.copy(out=z_bf[0, c][:].bitcast(F32).rearrange("p (g m u) -> p g m u", g=2, u=2),
                           in_=back[:].rearrange("p (g u m) -> p g m u", g=2, u=2))

        def quantize_z(b, c):
            h, odd = divmod(c, 2)
            cols = slice(odd * CHUNK, (odd + 1) * CHUNK)
            nc.vector.quantize_mx(out=z_w[b, h][:, cols].bitcast(FP8X4), scales=z_s[b, h][:, cols],
                                  in_=z_bf[b, c][:])

        def add_plane(planes, n, m0, width, engine):
            t = n % PACK
            engine.tensor_tensor(out=planes[:, t * T2 + m0:t * T2 + m0 + width], in0=pages[n % PAGES][:, m0:m0 + width],
                                 in1=clim_t[1, t // 2][:, t % 2, m0:m0 + width], op=ADD)

        def sum_single(acc, src, h, first):
            for block in range(4):
                m0 = h * HALF + block * P
                nc.tensor.matmul(out=acc[:, block * P:(block + 1) * P], lhsT=src[:, m0:m0 + P], rhs=ident[:],
                                 is_transpose=True, start=(first and block == 0), stop=(not first and block == 3))

        def round_single(acc, words):
            nc.scalar.copy(out=words[:].rearrange("m (g p e) -> m g p e", g=2, e=2),
                           in_=acc[:].rearrange("m (g e p) -> m g p e", g=2, e=2))
            return words

        def part_single(planes, n, h, words, after):
            back = bank(("parted", h), after)
            for g in range(2):
                nc.tensor.transpose(back[:, g * P:(g + 1) * P], words[:].bitcast(F32)[:, g * P:(g + 1) * P], ident[:])
            m0 = n % PACK * T2 + h * HALF
            nc.scalar.copy(out=planes[:, m0:m0 + HALF].rearrange("p (g e m) -> p g e m", g=2, e=2),
                           in_=back[:, 0:CHUNK].bitcast(BF16).rearrange("p (g m e) -> p g e m", g=2, e=2))

        def weave(planes, c, copy):
            z_bf[1, c] = held(("w1_raw000", "z_bf1", "pairs12", "pairs13")[c], [P, PACK * CHUNK], BF16)[:]
            source = planes[:].rearrange("p (t m) -> p t m", t=PACK)[:, :, c * CHUNK:(c + 1) * CHUNK]
            copy(out=z_bf[1, c].rearrange("p (m i t) -> p m t i", i=4, t=PACK),
                 in_=source.rearrange("p t (m i) -> p m t i", i=4))

        w3_s = held("w3_s", [P, PASSES * N], U8)

        w3_bf, w3_w = {}, {}

        def round_w3(b, slot, copy, run):
            w3_bf[b] = held(slot, [P, PACK * N], BF16)
            copy(out=w3_bf[b][:].rearrange("p (c i j) -> p c j i", i=run, j=PACK),
                 in_=w3_raw[b][:].rearrange("p j (c i) -> p c j i", i=run))

        def quantize_w3(b):
            for c0, c1 in ((0, 256), (256, N)):
                nc.vector.quantize_mx(out=w3_w[b][:, c0:c1].bitcast(FP8X4), scales=w3_s[:, b * N + c0:b * N + c1],
                                      in_=w3_bf[b][:, PACK * c0:PACK * c1])

        pieces = [(0, 0, HALF), (1, 0, HALF), (0, HALF, HALF), (1, HALF, HALF), (2, 0, HALF),
                  (2, HALF, CHUNK), (2, HALF + CHUNK, CHUNK)]
        ahead = 4
        gate_side, vol_side = 0, 1
        accs = {}

        def open_piece(i, afters):
            accs[i] = [bank(("piece", i, side), afters[side]) for side in (gate_side, vol_side)]

        def product(i, side, b, o0, width, stop):
            nt, m0 = pieces[i][0:2]
            words = (w4_w[:, b * N:(b + 1) * N], w3_w.get(b))[side][:, nt * P:(nt + 1) * P]
            scales = (w4_s, w3_s)[side]
            cols = slice(b * N + nt * P, b * N + (nt + 1) * P)
            h, c0 = divmod(m0 + o0, HALF)
            nc.tensor.matmul_mx(out=accs[i][side][:, o0:o0 + width], lhsT=words.bitcast(FP8X4),
                                lhsT_scale=scales[:, cols], rhs=z_w[b, h][:, c0:c0 + width].bitcast(FP8X4),
                                rhs_scale=z_s[b, h][:, c0:c0 + width], start=(b == 0), stop=stop)

        def finish(i):
            nt, m0, width = pieces[i]
            gate = held("root%d" % (i % 3), [P, width], F32)
            nc.scalar.activation(out=gate[:], in_=accs[i][gate_side][:, 0:width], func=ACT.Sigmoid)
            result = held("damp%d" % i, [P, width], F32)
            nc.vector.tensor_tensor(out=result[:], in0=accs[i][vol_side][:, 0:width], in1=gate[:], op=MULT)
            nc.sync.dma_start(out=out[nt * P:(nt + 1) * P, m0:m0 + width], in_=result[:])

        inverse = inverse_weights(("free", 0))
        add_page("wgs_rows")
        own_w = held("picked", [P, PASSES, P], U16)
        own_s = held("own_s", [P, PASSES, P], U8)
        nc.scalar.copy(out=own_w[:], in_=w2_w[0][:].bitcast(U16).rearrange("p (a m t) -> p a m t", a=PASSES, t=PACK)[:, :, :, 0])
        nc.vector.tensor_copy(out=own_s[:], in_=w2_s[0][:].rearrange("p (a m t) -> p a m t", a=PASSES, t=PACK)[:, :, :, 0])
        acc = bank(("root", 0), "wgs")
        for a in range(PASSES):
            nc.tensor.matmul_mx(out=acc[:], lhsT=own_w[:, a].bitcast(FP4X4), lhsT_scale=own_s[:, a],
                                rhs=v_w[a][:].bitcast(FP8X4), rhs_scale=v_s[a], start=(a == 0), stop=(a == PASSES - 1))
        first = held("first", [P, S], F32)
        nc.scalar.activation(out=first[:], in_=acc[:], func=ACT.Abs)
        root = held("root0", [P, S], F32)
        nc.scalar.activation(out=root[:], in_=first[:], func=ACT.Abs_reciprocal_sqrt, bias=1.0)
        damp[0] = held("damp0", [P, S], F32)
        nc.scalar.activation(out=damp[0][:], in_=root[:], func=ACT.Square)
        spread = [bank(("early", jb), ("free", 4 + jb)) for jb in range(BLOCKS)]
        for a in range(PASSES):
            for jb in range(BLOCKS):
                spread_pass(spread[jb], a, 0, jb)
        for a in range(PASSES):
            round_w1(a, 0, held("w1_bf%d" % a, [P, PACK * SPAN], BF16), nc.vector.tensor_copy)
            quantize_w1(a, 0, 0, 1)
            quantize_w1(a, 0, 1, 2)
            quantize_w1(a, 0, 2, PACK)
        weighted = held("w1_bf0", [P, S], F32)
        nc.vector.tensor_tensor(out=weighted[:], in0=damp[0][:], in1=wgs_t[:], op=MULT)
        expect(0, ("free", 1))
        ready[0] = held("ready0", [P, S], F32)
        nc.vector.tensor_tensor(out=ready[0][:], in0=expected[0][:], in1=weighted[:], op=MULT)
        expect(1, ("free", 2))
        weigh(1, held("outside1", [P, S], F32))
        scatter(0)

        early = early_magnitudes(spread, 1, PACK)
        early_roots = held("early_roots", [P, PACK - 1, BLOCKS, P], F32)
        for n in range(1, PACK):
            plain_root(n, early[:, :, n - 1:], early_roots[:, n - 1])
        late_bf = held("magnitude", [P, PASSES, PACK * SPAN], BF16)
        turn_root(1, ("a", 0))
        square(1)
        dampen(1, "w1_raw100")
        scatter(1)
        expect(2, ("free", 3))
        expect(3, ("early", 0))
        for n in (2, 3):
            turn_root(n, (("a", 1), ("root", 1))[n - 2])
            square(n)
            weigh_damping(n)
        for t0 in (0, 2):
            round_late(0, t0, t0 + 2, late_bf[:, 0, t0 * SPAN:(t0 + 2) * SPAN], nc.scalar.copy, "words")
        round_w1(1, 1, late_bf[:, 1], nc.scalar.copy)
        late_w = held("late_w", [P, PASSES * SPAN], U32)
        late_s = held("late_s", [P, PASSES * SPAN], U8)
        for a in range(PASSES):
            for t in range(PACK):
                cols = slice(a * SPAN + t * P, a * SPAN + (t + 1) * P)
                w1_w[a, 1, t], w1_s[a, 1, t] = late_w[:, cols], late_s[:, cols]
        for a in range(PASSES):
            cols = slice(a * SPAN, (a + 1) * SPAN)
            nc.vector.quantize_mx(out=late_w[:, cols].bitcast(FP8X4), scales=late_s[:, cols], in_=late_bf[:, a])
        held_back = held("magnitude", [P, 2, S], F32)
        for n in (2, 3):
            ready[n] = held_back[:, n - 2]
            nc.vector.tensor_tensor(out=ready[n], in0=expected[n][:], in1=damp[n][:], op=MULT)
        scatter(2)
        scatter(3)

        magnitude = late_magnitudes([("root", 0), ("early", 1), ("early", 2), ("early", 3)], "w1_raw110")
        for c in (0, 1):
            sum_pair(0, 0, c, ("root", c + 2))
        weighted_roots(PACK, magnitude[:], held("w1_raw000", [P, BLOCKS, PACK, P], F32)[:], inverse)
        for n, after in ((4, ("late", 0)), (5, ("late", 1)), (6, ("a", 2)), (7, ("a", 3))):
            turn_root(n, after)
        round_w3(0, "outside1", gpsimd_round, 1)
        for n, after, slot in ((4, ("late", 3), "w1_bf0"), (5, ("late", 2), "ready0"), (6, ("root", 4), "w1_raw100")):
            expect(n, after)
            square(n)
            copy_out(n)
            dampen(n, slot)
            scatter(n)
            if n == 5:
                for c in (2, 3):
                    sum_pair(0, 0, c, ("a", c + 2))
        square(7)
        round_pair(0, 0, range(CHUNKS))
        for c in range(CHUNKS):
            sum_pair(0, 1, c, ("sum", 0, 0, c))
        round_w3(1, "outside5", nc.scalar.copy, 4)
        round_pair(0, 1, range(CHUNKS))
        planes = held("outside6", [P, PACK * T2], F32)
        for n in (4, 5):
            add_plane(planes, n, 0, T2, nc.gpsimd)
        late_words = held("wgs_rows", [P, N + HALF], U32)
        z_w[0, 0] = late_words[:, N:]
        for c, after in enumerate([("a", 6), ("root", 6), ("root", 7), ("sum", 0, 1, 0)]):
            turn_back(c, after, held(("w1_raw000", "z_bf1", "magnitude", "w1_bf1")[c], [P, PACK * CHUNK], BF16)[:])
            if c < 2:
                quantize_z(0, c)
        w3_w[0] = late_words[:, 0:N]
        quantize_w3(0)
        expect(7, ("back", 1))
        copy_out(7, "wgs_t")
        nc.vector.tensor_tensor(out=pages[1][:].indirect(list2[:]), in0=outside[7][:], in1=damp[7][:], op=MULT)
        warm = held("warm", [P, 1], F32)
        nc.scalar.activation(out=warm[:], in_=outside[7][:, 0:1], func=ACT.Sigmoid)
        singles = [bank(("single", h), ("back", 2 + h)) for h in range(2)]
        for first, src in ((True, clim_t[1, 1][:, 0, :]), (False, pages[0])):
            for h in range(2):
                sum_single(singles[h], src, h, first)
        single_words = held("warm", [P, 2 * BANK], BF16)
        for h in range(2):
            part_single(planes, 6, h, round_single(singles[h], single_words[:, h * BANK:(h + 1) * BANK]),
                        (("back", 0), ("a", 7))[h])

        freed = [("single", 0), ("single", 1), ("parted", 0), ("parted", 1), ("sum", 0, 1, 1),
                 ("sum", 0, 1, 2), ("sum", 0, 1, 3), ("root", 5)]

        def first_pass(h):
            for i in (2 * h, 2 * h + 1):
                open_piece(i, freed[2 * i:2 * i + 2])
                for side in (gate_side, vol_side):
                    product(i, side, 0, 0, HALF, stop=False)

        def last_pass(h):
            for i in (2 * h, 2 * h + 1):
                for side in (gate_side, vol_side):
                    for odd in range(2):
                        product(i, side, 1, odd * CHUNK, CHUNK, stop=(odd == 1))
                finish(i)

        first_pass(0)
        z_w[0, 1], z_s[0, 1] = held("damp7", [P, HALF], U32), held("warm", [P, HALF], U8)
        for c in (2, 3):
            quantize_z(0, c)
        first_pass(1)
        for h in range(2):
            add_plane(planes, 7, h * HALF, HALF, nc.vector)
        for c in range(CHUNKS):
            weave(planes, c, nc.scalar.copy if c else nc.vector.tensor_copy)
        for c in (0, 1):
            quantize_z(1, c)
        w3_w[1] = held("z_bf1", [P, N], U32)[:]
        quantize_w3(1)
        for c in (2, 3):
            quantize_z(1, c)
        last_pass(0)
        last_pass(1)
        for i in range(ahead, len(pieces)):
            open_piece(i, [("piece", i - ahead, side) for side in (gate_side, vol_side)])
            for side in (gate_side, vol_side):
                for b in range(PASSES):
                    product(i, side, b, 0, pieces[i][2], stop=(b == PASSES - 1))
            finish(i)
